import numpy as np
import ml_dtypes


def mxq(x, axis, fmt="e4m3"):
    dtype, down = {"e4m3": (ml_dtypes.float8_e4m3fn, 7), "e5m2": (ml_dtypes.float8_e5m2, 14)}[fmt]
    v = np.moveaxis(np.asarray(x, np.float32).astype(ml_dtypes.bfloat16).astype(np.float64), axis, -1)
    blocks = v.reshape(v.shape[:-1] + (-1, 32))
    amax = np.abs(blocks).max(-1, keepdims=True)
    byte = np.maximum(np.where(amax > 0, np.frexp(amax)[1] - 1 + 127, 0) - down, 1)
    scale = np.exp2(byte - 127.0)
    codes = (blocks / scale).astype(np.float32).astype(dtype).astype(np.float64)
    return np.moveaxis((codes * scale).reshape(v.shape), -1, axis)


WIDE = False


def mx_kscale(k):
    if not WIDE:
        return np.ones(k)
    levels = np.array([10, -10, 5, -5, 0])
    if k % 512:
        return np.exp2(np.random.permutation(np.resize(levels, k // 32))).repeat(32)
    a = np.empty((k // 512, 16))
    for p in range(k // 512):
        a[p, :8] = np.random.permutation(np.resize(levels, 8))
        for g in range(8):
            far = levels[np.abs(levels - a[p, g]) >= 10]
            a[p, g + 8] = far[np.random.randint(len(far))]
    return np.exp2(a.ravel()).repeat(32)


def f64(x):
    return np.asarray(x).astype(np.float64)


def striped(idx):
    return np.tile(idx.reshape(-1, 16).T, (8, 1)).astype(np.uint16)


def unstriped(offs):
    return offs[:16].T.reshape(-1).astype(np.int64)


E2M1 = np.array([0.0, 0.5, 1.0, 1.5, 2.0, 3.0, 4.0, 6.0, -0.0, -0.5, -1.0, -1.5, -2.0, -3.0, -4.0, -6.0])


def pack_weight(w, fmt):
    k, n = w.shape
    w = f64(np.asarray(w, np.float32).astype(ml_dtypes.bfloat16)).reshape(k // 32, 32, n)
    amax = np.abs(w).max(1)
    if fmt == "e4m3":
        byte = np.frexp(amax)[1] - 1 + 127 - 7
    else:
        mant, ex = np.frexp(amax / 6.0)
        byte = np.where(mant > 0.5, ex, ex - 1) + 127
    byte = np.clip(np.where(amax > 0, byte, 1), 1, 254)
    scaled = (w * np.exp2(127.0 - byte)[:, None, :]).reshape(k, n).astype(np.float32)
    by_word = np.ascontiguousarray(scaled.reshape(k // 512, 128, 4, n).transpose(0, 1, 3, 2))
    if fmt == "e4m3":
        words = by_word.astype(ml_dtypes.float8_e4m3fn).view(np.uint8)
    else:
        c = by_word.astype(ml_dtypes.float4_e2m1fn).view(np.uint8) & 0xF
        words = (c[..., 0::2] | (c[..., 1::2] << 4)).reshape(k // 512, 128, 2 * n)
    return np.ascontiguousarray(words), np.ascontiguousarray(byte.astype(np.uint8).reshape(k // 512, 16, n))


def unpack_weight(words, scales, fmt):
    g, _, n = scales.shape
    words = np.ascontiguousarray(words).reshape(g, 128, n, -1)
    if fmt == "e4m3":
        vals = words.view(ml_dtypes.float8_e4m3fn).astype(np.float64)
    else:
        nib = np.empty((g, 128, n, 4), np.uint8)
        nib[..., 0::2] = words & 0xF
        nib[..., 1::2] = words >> 4
        vals = E2M1[nib]
    vals = vals * np.repeat(np.exp2(scales.astype(np.float64) - 127.0), 8, axis=1)[..., None]
    return vals.transpose(0, 1, 3, 2).reshape(g * 512, n)


def gelu(v):
    return 0.5 * v * (1.0 + np.tanh(np.sqrt(2.0 / np.pi) * (v + 0.044715 * v**3)))


K, H, N, T, S = 1024, 1024, 512, 2048, 1024

def setup_inputs():
    n = np.random.standard_normal
    s = mx_kscale(K)[:, None]
    u = mx_kscale(H)[:, None]
    tab_words, tab_scales = pack_weight(n((K, T)) * s, "e4m3")
    w4_words, w4_scales = pack_weight(n((H, N)) / np.sqrt(H) / u, "e2m1")
    return {
        "tab_words": tab_words, "tab_scales": tab_scales,
        "offs": striped(np.random.permutation(T)[:S]),
        "gT": n((N, T)).astype(np.float32),
        "w1": (0.32 * n((K, H)) / np.sqrt(K) / s).astype(np.float32),
        "bias": np.random.uniform(-1.0, 1.0, H).astype(np.float32),
        "w4_words": w4_words, "w4_scales": w4_scales,
        "w5": (n((H, N)) / np.sqrt(H) / u).astype(np.float32),
        "amps": (np.exp(0.3 * n(H)) * u[:, 0]).astype(np.float32),
        "ampc": (np.exp(0.3 * n(H)) * u[:, 0]).astype(np.float32),
    }

def reference(tab_words, tab_scales, offs, gT, w1, bias, w4_words, w4_scales, w5, amps, ampc):
    v = unpack_weight(tab_words, tab_scales, "e4m3")[:, unstriped(offs)]
    h = (mxq(f64(w1), 0, "e4m3").T @ v) + f64(bias)[:, None]
    hs = mxq(np.sin(h) * f64(amps)[:, None], 0, "e4m3")
    hc = mxq(np.cos(h) * f64(ampc)[:, None], 0, "e4m3")
    w4 = unpack_weight(w4_words, w4_scales, "e2m1")
    y = w4.T @ hs + mxq(f64(w5), 0, "e4m3").T @ hc
    g = f64(gT)[:, unstriped(offs)]
    out = f64(gT).copy()
    out[:, unstriped(offs)] = g + y
    return out

@@ -1,0 +1,277 @@
+import math
+from contextlib import ExitStack
+
+import concourse.mybir as mybir
+
+K, H, N, T, S = 1024, 1024, 512, 2048, 1024
+FLOPS = 2 * K * H * S + 2 * 2 * H * N * S
+
+F32 = mybir.dt.float32
+BF16 = mybir.dt.bfloat16
+I32 = mybir.dt.int32
+U32 = mybir.dt.uint32
+U16 = mybir.dt.uint16
+U8 = mybir.dt.uint8
+FP8X4 = mybir.dt.float8_e4m3fn_x4
+FP4X4 = mybir.dt.float4_e2m1fn_x4
+ACT = mybir.ActivationFunctionType
+ALU = mybir.AluOpType
+
+P = 128
+SLICES = [256,512,256]
+CAST = {"w1_00":"S","w1_01":"SV","w1_10":"V","w1_11":"V","w5_0":"VV","w5_1":"VV"}
+SI = {"00s":"V","00c":"V","01s":"V","01c":"V","10s":"SS","10c":"V","11s":"SS","11c":"V","20s":"V","20c":"V","21s":"SS","21c":"V"}
+Y_ORDER = []
+
+
+def tile_list_choir_phase_retune_kernel(
+    tc, tab_words, tab_scales, offs, gT, w1, bias, w4_words, w4_scales, w5, amps, ampc, out
+):
+    nc = tc.nc
+    with ExitStack() as ctx:
+        keep = ctx.enter_context(tc.tile_pool(name="keep", bufs=1))
+        trig = ctx.enter_context(tc.tile_pool(name="trig", bufs=10))
+        hq = ctx.enter_context(tc.tile_pool(name="hq", bufs=4))
+        rowp = ctx.enter_context(tc.tile_pool(name="rowp", bufs=2))
+        ysb = ctx.enter_context(tc.tile_pool(name="ysb", bufs=6))
+        hps = ctx.enter_context(tc.psum_pool(name="hps", bufs=5))
+        yps = ctx.enter_context(tc.psum_pool(name="yps", bufs=3))
+
+        offsets = keep.tile([P, S // 16], U16, name="offsets")
+        nc.sync.dma_start(offsets[:], offs)
+
+        tab_sc = keep.tile([P, T], U8, name="tab_sc", align_bytes=64)
+        nc.vector.memset(tab_sc[:].bitcast(I32), 0)
+        w4_sc = keep.tile([P, 2, N], U8, name="w4_sc", align_bytes=64)
+        nc.gpsimd.memset(w4_sc[:].rearrange("p a c -> p (a c)").bitcast(I32), 0)
+        vecs = {}
+        tab_w = [keep.tile([P, T], I32, name="tab_w%d" % ka, align_bytes=64) for ka in range(2)]
+        w1_raw = {}
+        w5_raw = {}
+        win = [keep.tile([P, T], F32, name="win%d" % n, align_bytes=64) for n in range(4)]
+        w4_w = keep.tile([P, 2, 2 * N], U8, name="w4_w", align_bytes=64)
+
+        def load(what):
+            if what[0] == "tab":
+                ka = what[1]
+                nc.sync.dma_start(tab_w[ka][:], tab_words[ka].rearrange("p t i -> p (t i)").bitcast(I32))
+            elif what[0] == "w1":
+                a, ka = what[1], what[2]
+                w1_raw[a, ka] = trig.tile([P, 4, 512], F32, name="w1_raw%d%d" % (a, ka), tag="f32")
+                nc.sync.dma_start(
+                    w1_raw[a, ka][:],
+                    w1[512 * ka : 512 * ka + 512, 512 * a : 512 * a + 512].rearrange("(p j) c -> p j c", j=4),
+                )
+            elif what[0] == "vec":
+                src = {"bias": bias, "amps": amps, "ampc": ampc}[what[1]]
+                vecs[what[1]] = keep.tile([P, 2, 4], F32, name="vec_" + what[1])
+                nc.sync.dma_start(vecs[what[1]][:], src.rearrange("(a p t) -> p a t", a=2, t=4))
+            elif what[0] == "tsc":
+                for q in range(4):
+                    nc.sync.dma_start(
+                        tab_sc[32 * q : 32 * q + 8, :].bitcast(I32),
+                        tab_scales[:, 4 * q : 4 * q + 4, :].bitcast(I32),
+                    )
+            elif what[0] == "w4s":
+                for q in range(4):
+                    nc.sync.dma_start(
+                        w4_sc[32 * q : 32 * q + 4, :, :].bitcast(I32),
+                        w4_scales[:, 4 * q : 4 * q + 4, :].rearrange("a r c -> r a c").bitcast(I32),
+                    )
+            elif what[0] == "w4":
+                nc.sync.dma_start(w4_w[:].bitcast(I32), w4_words.rearrange("a p c -> p a c").bitcast(I32))
+            elif what[0] == "w5":
+                half = what[1]
+                w5_raw[half] = trig.tile([P, 2, 4, 256], F32, name="w5_raw%d" % half, tag="f32")
+                for a in range(2):
+                    nc.sync.dma_start(
+                        w5_raw[half][:, a, :, :],
+                        w5[512 * a : 512 * a + 512, 256 * half : 256 * half + 256].rearrange("(p j) c -> p j c", j=4),
+                    )
+            else:
+                n = what[1]
+                nc.sync.dma_start(win[n][:], gT[P * n : P * n + P, :])
+
+        for what in [["tab",0],["tsc"],["tab",1],["w1",0,0],["w1",0,1],["vec","bias"],["w1",1,0],["vec","amps"],["vec","ampc"],["w1",1,1],["w4s"],["w4"],["w5",0],["w5",1],["g",0],["g",1],["g",2],["g",3]]:
+            load(what)
+
+        def copy_on(eng, out, in_):
+            if eng == "S":
+                nc.scalar.copy(out, in_)
+            elif eng == "V":
+                nc.vector.tensor_copy(out, in_)
+            else:
+                nc.gpsimd.tensor_scalar(out, in_, 1.0, 0.0, ALU.mult, ALU.add)
+
+        starts = [sum(SLICES[:s]) for s in range(len(SLICES))]
+
+        def lst(s):
+            return offsets[:, starts[s] // 16 : (starts[s] + SLICES[s]) // 16]
+
+        v_w, v_sc = {}, {}
+
+        def gather_words(s, ka):
+            v_w[s, ka] = keep.tile([P, SLICES[s]], U32, name="v_w%d%d" % (s, ka), align_bytes=64)
+            nc.vector.tensor_copy(v_w[s, ka][:], tab_w[ka][:].bitcast(U32).indirect(lst(s)))
+
+        def gather_scales(s):
+            v_sc[s] = keep.tile([P, SLICES[s]], U8, name="v_sc%d" % s, align_bytes=64)
+            nc.vector.tensor_copy(v_sc[s][:], tab_sc[:].indirect(lst(s)))
+
+        w1_c, w1_s = {}, {}
+
+        def prep_w1(a, ka):
+            grouped = hq.tile([P, 4, 128, 4], BF16, name="w1_g%d%d" % (a, ka), tag="grp", align_bytes=64)
+            engs = CAST["w1_%d%d" % (a, ka)]
+            w = 128 // len(engs)
+            for i, eng in enumerate(engs):
+                copy_on(
+                    eng,
+                    grouped[:, :, i * w : (i + 1) * w, :].rearrange("p t m j -> p m j t"),
+                    w1_raw[a, ka][:, :, 4 * i * w : 4 * (i + 1) * w].rearrange("p j (m t) -> p m j t", t=4),
+                )
+            w1_c[a, ka] = keep.tile([P, 512], U32, name="w1_c%d%d" % (a, ka), align_bytes=64)
+            w1_s[a, ka] = keep.tile([P, 512], U8, name="w1_s%d%d" % (a, ka), align_bytes=64)
+            nc.vector.quantize_mx(
+                out=w1_c[a, ka][:].bitcast(FP8X4), scales=w1_s[a, ka][:], in_=grouped[:].rearrange("p t m j -> p (t m j)")
+            )
+
+        w5_c, w5_s = {}, {}
+
+        def prep_w5(half):
+            grouped = hq.tile([P, 2, 256, 4], BF16, name="w5_g%d" % half, tag="grp", align_bytes=64)
+            for a in range(2):
+                copy_on(
+                    CAST["w5_%d" % half][a],
+                    grouped[:, a, :, :].rearrange("p (c i) j -> p c j i", i=4),
+                    w5_raw[half][:, a, :, :].rearrange("p j (c i) -> p c j i", i=4),
+                )
+            w5_c[half] = keep.tile([P, 2, 256], U32, name="w5_c%d" % half, align_bytes=64)
+            w5_s[half] = keep.tile([P, 2, 256], U8, name="w5_s%d" % half, align_bytes=64)
+            nc.vector.quantize_mx(
+                out=w5_c[half][:].rearrange("p a c -> p (a c)").bitcast(FP8X4),
+                scales=w5_s[half][:].rearrange("p a c -> p (a c)"),
+                in_=grouped[:].rearrange("p a c j -> p (a c j)"),
+            )
+
+        g_sb = {}
+
+        def gather_g(n, s):
+            g_sb[n, s] = keep.tile([P, SLICES[s]], F32, name="g_sb%d%d" % (n, s))
+            nc.vector.tensor_copy(g_sb[n, s][:], win[n][:].indirect(lst(s)))
+
+        trig_sb = {}
+
+        def angles(s, a):
+            w = SLICES[s]
+            sin_sb = trig.tile([P, 4, w], F32, name="sin_sb", tag="f32")
+            cos_sb = trig.tile([P, 4, w], F32, name="cos_sb", tag="f32")
+            abs_sb = cos_sb
+            for t in range(4):
+                bank = hps.tile([P, 512], F32, name="h_bank")
+                for ka in range(2):
+                    nc.tensor.matmul_mx(
+                        out=bank[:, :w],
+                        lhsT=w1_c[a, ka][:, P * t : P * t + P].bitcast(FP8X4),
+                        lhsT_scale=w1_s[a, ka][:, P * t : P * t + P],
+                        rhs=v_w[s, ka][:].bitcast(FP8X4),
+                        rhs_scale=v_sc[s][4 * ka : P, :],
+                        start=(ka == 0),
+                        stop=(ka == 1),
+                    )
+                b = vecs["bias"][:, a, t : t + 1]
+                nc.scalar.activation(sin_sb[:, t, :], bank[:, :w], ACT.Sin, bias=b)
+                nc.scalar.activation(abs_sb[:, t, :], bank[:, :w], ACT.Abs, bias=b)
+            nc.scalar.activation(cos_sb[:], abs_sb[:], ACT.Sin, bias=math.pi / 2, scale=-1.0)
+            trig_sb[s, a, "s"] = sin_sb
+            trig_sb[s, a, "c"] = cos_sb
+
+        h_c, h_s = {}, {}
+
+        def scale_quant(s, a, kind):
+            w = SLICES[s]
+            src = trig_sb[s, a, kind]
+            amp = vecs["amps" if kind == "s" else "ampc"]
+            grouped = hq.tile([P, w, 4], BF16, name="h_g", tag="grp", align_bytes=64)
+            mode = SI["%d%d%s" % (s, a, kind)]
+            walk_out = grouped[:].rearrange("p (c i) t -> p c t i", i=4)
+            if len(mode) == 1:
+                eng = nc.vector if mode == "V" else nc.gpsimd
+                eng.tensor_tensor(
+                    walk_out,
+                    src[:].rearrange("p t (c i) -> p c t i", i=4),
+                    amp[:, a, :].unsqueeze(1).unsqueeze(3).to_broadcast([P, w // 4, 4, 4]),
+                    ALU.mult,
+                )
+            else:
+                rows = rowp.tile([P, 4, w], BF16, name="h_rows", align_bytes=64)
+                for t in range(4):
+                    if mode[0] == "S":
+                        nc.scalar.activation(rows[:, t, :], src[:, t, :], ACT.Copy, scale=amp[:, a, t : t + 1])
+                    else:
+                        nc.gpsimd.tensor_scalar(rows[:, t, :], src[:, t, :], amp[:, a, t : t + 1], 0.0, ALU.mult, ALU.add)
+                copy_on(mode[1], walk_out, rows[:].rearrange("p t (c i) -> p c t i", i=4))
+            h_c[s, a, kind] = keep.tile([P, w], U32, name="h_c%d%d%s" % (s, a, kind), align_bytes=64)
+            h_s[s, a, kind] = keep.tile([P, w], U8, name="h_s%d%d%s" % (s, a, kind), align_bytes=64)
+            nc.vector.quantize_mx(
+                out=h_c[s, a, kind][:].bitcast(FP8X4), scales=h_s[s, a, kind][:], in_=grouped[:].rearrange("p c t -> p (c t)")
+            )
+
+        left = [len(SLICES)] * 4
+
+        y_banks, y_sbs = {}, {}
+
+        def y_mm(s, n):
+            w = SLICES[s]
+            bank = yps.tile([P, 512], F32, name="y_bank")
+            y_banks[s, n] = bank
+            step = 512 if w == 512 else 128
+            half, col = n // 2, P * (n % 2)
+            for c0 in range(0, w, step):
+                cols = slice(c0, c0 + step)
+                for a in range(2):
+                    nc.tensor.matmul_mx(
+                        out=bank[:, cols],
+                        lhsT=w4_w[:, a, 2 * P * n : 2 * P * n + 2 * P].bitcast(FP4X4),
+                        lhsT_scale=w4_sc[:, a, P * n : P * n + P],
+                        rhs=h_c[s, a, "s"][:, cols].bitcast(FP8X4),
+                        rhs_scale=h_s[s, a, "s"][:, cols],
+                        start=(a == 0),
+                        stop=False,
+                    )
+                    nc.tensor.matmul_mx(
+                        out=bank[:, cols],
+                        lhsT=w5_c[half][:, a, col : col + P].bitcast(FP8X4),
+                        lhsT_scale=w5_s[half][:, a, col : col + P],
+                        rhs=h_c[s, a, "c"][:, cols].bitcast(FP8X4),
+                        rhs_scale=h_s[s, a, "c"][:, cols],
+                        start=False,
+                        stop=(a == 1),
+                    )
+
+        def y_ev(s, n):
+            w = SLICES[s]
+            bank = y_banks[s, n]
+            y_sb = ysb.tile([P, w], F32, name="y_sb")
+            y_sbs[s, n] = y_sb
+            nc.scalar.copy(y_sb[:], bank[:, :w])
+
+        def y_sc(s, n):
+            y_sb = y_sbs[s, n]
+            nc.vector.tensor_tensor(win[n][:].indirect(lst(s)), g_sb[n, s][:], y_sb[:], ALU.add)
+            left[n] -= 1
+            if left[n] == 0:
+                nc.sync.dma_start(out[P * n : P * n + P, :], win[n][:])
+
+        def retune(s, n):
+            y_mm(s, n)
+            y_ev(s, n)
+            y_sc(s, n)
+
+        steps = {
+            "ym": y_mm, "ev": y_ev, "sc": y_sc,
+            "gw": gather_words, "gs": gather_scales, "w1": prep_w1, "w5": prep_w5, "gg": gather_g,
+            "ang": angles, "sq": scale_quant, "y": retune,
+        }
+        for step in [["gw",0,0],["gs",0],["gw",0,1],["w1",0,0],["w1",0,1],["w1",1,0],["w1",1,1],["gw",1,0],["gs",1],["gw",1,1],["gw",2,0],["gs",2],["gw",2,1],["w5",0],["w5",1],["ang",0,0],["sq",0,0,"s"],["sq",0,0,"c"],["ang",0,1],["sq",0,1,"s"],["sq",0,1,"c"],["gg",0,0],["gg",0,1],["gg",0,2],["gg",1,0],["gg",1,1],["gg",1,2],["gg",2,0],["gg",2,1],["gg",2,2],["gg",3,0],["gg",3,1],["gg",3,2],["ang",1,0],["sq",1,0,"s"],["sq",1,0,"c"],["y",0,0],["ang",1,1],["sq",1,1,"s"],["sq",1,1,"c"],["y",0,1],["y",0,2],["ang",2,0],["sq",2,0,"s"],["sq",2,0,"c"],["y",0,3],["y",1,0],["ang",2,1],["sq",2,1,"s"],["sq",2,1,"c"],["y",1,1],["y",2,0],["y",2,1],["y",1,2],["y",2,2],["y",1,3],["y",2,3]]:
+            steps[step[0]](*step[1:])

@@ -18,10 +18,11 @@ ACT = mybir.ActivationFunctionType
 ALU = mybir.AluOpType
 
 P = 128
-SLICES = [256,512,256]
-CAST = {"w1_00":"S","w1_01":"SV","w1_10":"V","w1_11":"V","w5_0":"VV","w5_1":"VV"}
-SI = {"00s":"V","00c":"V","01s":"V","01c":"V","10s":"SS","10c":"V","11s":"SS","11c":"V","20s":"V","20c":"V","21s":"SS","21c":"V"}
-Y_ORDER = []
+PACK = 4
+PASS = P * PACK
+BANK = 512
+SLICES = (256, 512, 256)
+ON_SCALAR = ((1, 0, "sin"), (1, 1, "sin"), (2, 0, "sin"), (2, 1, "sin"))
 
 
 def tile_list_choir_phase_retune_kernel(
@@ -30,12 +31,12 @@ def tile_list_choir_phase_retune_kernel(
     nc = tc.nc
     with ExitStack() as ctx:
         keep = ctx.enter_context(tc.tile_pool(name="keep", bufs=1))
-        trig = ctx.enter_context(tc.tile_pool(name="trig", bufs=10))
-        hq = ctx.enter_context(tc.tile_pool(name="hq", bufs=4))
-        rowp = ctx.enter_context(tc.tile_pool(name="rowp", bufs=2))
-        ysb = ctx.enter_context(tc.tile_pool(name="ysb", bufs=6))
-        hps = ctx.enter_context(tc.psum_pool(name="hps", bufs=5))
-        yps = ctx.enter_context(tc.psum_pool(name="yps", bufs=3))
+        wide = ctx.enter_context(tc.tile_pool(name="wide", bufs=10))
+        woven = ctx.enter_context(tc.tile_pool(name="woven", bufs=4))
+        stage = ctx.enter_context(tc.tile_pool(name="stage", bufs=1))
+        sums = ctx.enter_context(tc.tile_pool(name="sums", bufs=6))
+        h_psum = ctx.enter_context(tc.psum_pool(name="h_psum", bufs=5))
+        y_psum = ctx.enter_context(tc.psum_pool(name="y_psum", bufs=3))
 
         offsets = keep.tile([P, S // 16], U16, name="offsets")
         nc.sync.dma_start(offsets[:], offs)
@@ -44,234 +45,195 @@ def tile_list_choir_phase_retune_kernel(
         nc.vector.memset(tab_sc[:].bitcast(I32), 0)
         w4_sc = keep.tile([P, 2, N], U8, name="w4_sc", align_bytes=64)
         nc.gpsimd.memset(w4_sc[:].rearrange("p a c -> p (a c)").bitcast(I32), 0)
-        vecs = {}
-        tab_w = [keep.tile([P, T], I32, name="tab_w%d" % ka, align_bytes=64) for ka in range(2)]
-        w1_raw = {}
-        w5_raw = {}
-        win = [keep.tile([P, T], F32, name="win%d" % n, align_bytes=64) for n in range(4)]
+
+        def load_table_words(a):
+            words = keep.tile([P, T], I32, name="tab_w%d" % a, align_bytes=64)
+            nc.sync.dma_start(words[:], tab_words[a].rearrange("p t i -> p (t i)").bitcast(I32))
+            return words
+
+        def load_weight(w, a, b, name):
+            raw = wide.tile([P, PACK, PASS], F32, name=name, tag="wide")
+            block = w[PASS * a : PASS * (a + 1), PASS * b : PASS * (b + 1)]
+            nc.sync.dma_start(raw[:], block.rearrange("(p j) c -> p j c", j=PACK))
+            return raw
+
+        def load_channel_vector(vec, name):
+            tile = keep.tile([P, 2, PACK], F32, name=name)
+            nc.sync.dma_start(tile[:], vec.rearrange("(b p t) -> p b t", b=2, t=PACK))
+            return tile
+
+        tab_w = [load_table_words(0)]
+        for q in range(4):
+            nc.sync.dma_start(
+                tab_sc[32 * q : 32 * q + 8, :].bitcast(I32), tab_scales[:, 4 * q : 4 * q + 4, :].bitcast(I32)
+            )
+        tab_w.append(load_table_words(1))
+        w1_raw = {(a, 0): load_weight(w1, a, 0, "w1_raw%d0" % a) for a in range(2)}
+        bias_sb = load_channel_vector(bias, "bias_sb")
+        w1_raw[0, 1] = load_weight(w1, 0, 1, "w1_raw01")
+        amp_sb = {"sin": load_channel_vector(amps, "amps_sb"), "cos": load_channel_vector(ampc, "ampc_sb")}
+        w1_raw[1, 1] = load_weight(w1, 1, 1, "w1_raw11")
+        for q in range(4):
+            nc.sync.dma_start(
+                w4_sc[32 * q : 32 * q + 4, :, :].bitcast(I32),
+                w4_scales[:, 4 * q : 4 * q + 4, :].rearrange("a r c -> r a c").bitcast(I32),
+            )
         w4_w = keep.tile([P, 2, 2 * N], U8, name="w4_w", align_bytes=64)
+        nc.sync.dma_start(w4_w[:].bitcast(I32), w4_words.rearrange("a p c -> p a c").bitcast(I32))
+        w5_raw = [load_weight(w5, b, 0, "w5_raw%d" % b) for b in range(2)]
+        phases = []
+        for n in range(N // P):
+            phases.append(keep.tile([P, T], F32, name="phases%d" % n, align_bytes=64))
+            nc.sync.dma_start(phases[n][:], gT[P * n : P * (n + 1), :])
 
-        def load(what):
-            if what[0] == "tab":
-                ka = what[1]
-                nc.sync.dma_start(tab_w[ka][:], tab_words[ka].rearrange("p t i -> p (t i)").bitcast(I32))
-            elif what[0] == "w1":
-                a, ka = what[1], what[2]
-                w1_raw[a, ka] = trig.tile([P, 4, 512], F32, name="w1_raw%d%d" % (a, ka), tag="f32")
-                nc.sync.dma_start(
-                    w1_raw[a, ka][:],
-                    w1[512 * ka : 512 * ka + 512, 512 * a : 512 * a + 512].rearrange("(p j) c -> p j c", j=4),
+        def quantise(grouped, width, name):
+            codes = keep.tile([P, width], U32, name=name + "_codes", align_bytes=64)
+            scales = keep.tile([P, width], U8, name=name + "_scales", align_bytes=64)
+            nc.vector.quantize_mx(out=codes[:].bitcast(FP8X4), scales=scales[:], in_=grouped)
+            return codes, scales
+
+        v_w = [keep.tile([P, S], U32, name="v_w%d" % a, align_bytes=64) for a in range(2)]
+        v_sc = keep.tile([P, S], U8, name="v_sc", align_bytes=64)
+        nc.vector.tensor_copy(v_w[0][:], tab_w[0][:].bitcast(U32).indirect(offsets[:]))
+        nc.vector.tensor_copy(v_sc[:], tab_sc[:].indirect(offsets[:]))
+        nc.vector.tensor_copy(v_w[1][:], tab_w[1][:].bitcast(U32).indirect(offsets[:]))
+
+        def quantise_w1(a, b, copies):
+            grouped = woven.tile([P, PACK, P, PACK], BF16, name="w1_grouped", tag="woven", align_bytes=64)
+            share = P // len(copies)
+            for i, copy in enumerate(copies):
+                copy(
+                    grouped[:, :, share * i : share * (i + 1), :].rearrange("p t m j -> p m j t"),
+                    w1_raw[a, b][:, :, PACK * share * i : PACK * share * (i + 1)].rearrange(
+                        "p j (m t) -> p m j t", t=PACK
+                    ),
                 )
-            elif what[0] == "vec":
-                src = {"bias": bias, "amps": amps, "ampc": ampc}[what[1]]
-                vecs[what[1]] = keep.tile([P, 2, 4], F32, name="vec_" + what[1])
-                nc.sync.dma_start(vecs[what[1]][:], src.rearrange("(a p t) -> p a t", a=2, t=4))
-            elif what[0] == "tsc":
-                for q in range(4):
-                    nc.sync.dma_start(
-                        tab_sc[32 * q : 32 * q + 8, :].bitcast(I32),
-                        tab_scales[:, 4 * q : 4 * q + 4, :].bitcast(I32),
-                    )
-            elif what[0] == "w4s":
-                for q in range(4):
-                    nc.sync.dma_start(
-                        w4_sc[32 * q : 32 * q + 4, :, :].bitcast(I32),
-                        w4_scales[:, 4 * q : 4 * q + 4, :].rearrange("a r c -> r a c").bitcast(I32),
-                    )
-            elif what[0] == "w4":
-                nc.sync.dma_start(w4_w[:].bitcast(I32), w4_words.rearrange("a p c -> p a c").bitcast(I32))
-            elif what[0] == "w5":
-                half = what[1]
-                w5_raw[half] = trig.tile([P, 2, 4, 256], F32, name="w5_raw%d" % half, tag="f32")
+            return quantise(grouped[:].rearrange("p t m j -> p (t m j)"), PASS, "w1_%d%d" % (a, b))
+
+        w1_q = {
+            (0, 0): quantise_w1(0, 0, [nc.scalar.copy]),
+            (1, 0): quantise_w1(1, 0, [nc.scalar.copy, nc.vector.tensor_copy]),
+            (0, 1): quantise_w1(0, 1, [nc.vector.tensor_copy]),
+            (1, 1): quantise_w1(1, 1, [nc.vector.tensor_copy]),
+        }
+
+        w5_q = {}
+
+        def quantise_w5(b):
+            grouped = woven.tile([P, N, PACK], BF16, name="w5_grouped", tag="woven", align_bytes=64)
+            nc.vector.tensor_copy(
+                grouped[:].rearrange("p (c i) j -> p c j i", i=2),
+                w5_raw[b][:].rearrange("p j (c i) -> p c j i", i=2),
+            )
+            w5_q[b] = quantise(grouped[:].rearrange("p c j -> p (c j)"), N, "w5_%d" % b)
+
+        old = [keep.tile([P, S], F32, name="old%d" % n) for n in range(N // P)]
+
+        def entries(s):
+            first = sum(SLICES[:s])
+            return slice(first, first + SLICES[s])
+
+        h_q = {}
+
+        def angles(s, b):
+            width, cols = SLICES[s], entries(s)
+            trig = {
+                "sin": wide.tile([P, PACK, width], F32, name="sin_sb", tag="wide"),
+                "cos": wide.tile([P, PACK, width], F32, name="cos_sb", tag="wide"),
+            }
+            for t in range(PACK):
+                bank = h_psum.tile([P, BANK], F32, name="h_bank")
                 for a in range(2):
-                    nc.sync.dma_start(
-                        w5_raw[half][:, a, :, :],
-                        w5[512 * a : 512 * a + 512, 256 * half : 256 * half + 256].rearrange("(p j) c -> p j c", j=4),
-                    )
-            else:
-                n = what[1]
-                nc.sync.dma_start(win[n][:], gT[P * n : P * n + P, :])
-
-        for what in [["tab",0],["tsc"],["tab",1],["w1",0,0],["w1",0,1],["vec","bias"],["w1",1,0],["vec","amps"],["vec","ampc"],["w1",1,1],["w4s"],["w4"],["w5",0],["w5",1],["g",0],["g",1],["g",2],["g",3]]:
-            load(what)
-
-        def copy_on(eng, out, in_):
-            if eng == "S":
-                nc.scalar.copy(out, in_)
-            elif eng == "V":
-                nc.vector.tensor_copy(out, in_)
-            else:
-                nc.gpsimd.tensor_scalar(out, in_, 1.0, 0.0, ALU.mult, ALU.add)
-
-        starts = [sum(SLICES[:s]) for s in range(len(SLICES))]
-
-        def lst(s):
-            return offsets[:, starts[s] // 16 : (starts[s] + SLICES[s]) // 16]
-
-        v_w, v_sc = {}, {}
-
-        def gather_words(s, ka):
-            v_w[s, ka] = keep.tile([P, SLICES[s]], U32, name="v_w%d%d" % (s, ka), align_bytes=64)
-            nc.vector.tensor_copy(v_w[s, ka][:], tab_w[ka][:].bitcast(U32).indirect(lst(s)))
-
-        def gather_scales(s):
-            v_sc[s] = keep.tile([P, SLICES[s]], U8, name="v_sc%d" % s, align_bytes=64)
-            nc.vector.tensor_copy(v_sc[s][:], tab_sc[:].indirect(lst(s)))
-
-        w1_c, w1_s = {}, {}
-
-        def prep_w1(a, ka):
-            grouped = hq.tile([P, 4, 128, 4], BF16, name="w1_g%d%d" % (a, ka), tag="grp", align_bytes=64)
-            engs = CAST["w1_%d%d" % (a, ka)]
-            w = 128 // len(engs)
-            for i, eng in enumerate(engs):
-                copy_on(
-                    eng,
-                    grouped[:, :, i * w : (i + 1) * w, :].rearrange("p t m j -> p m j t"),
-                    w1_raw[a, ka][:, :, 4 * i * w : 4 * (i + 1) * w].rearrange("p j (m t) -> p m j t", t=4),
-                )
-            w1_c[a, ka] = keep.tile([P, 512], U32, name="w1_c%d%d" % (a, ka), align_bytes=64)
-            w1_s[a, ka] = keep.tile([P, 512], U8, name="w1_s%d%d" % (a, ka), align_bytes=64)
-            nc.vector.quantize_mx(
-                out=w1_c[a, ka][:].bitcast(FP8X4), scales=w1_s[a, ka][:], in_=grouped[:].rearrange("p t m j -> p (t m j)")
-            )
-
-        w5_c, w5_s = {}, {}
-
-        def prep_w5(half):
-            grouped = hq.tile([P, 2, 256, 4], BF16, name="w5_g%d" % half, tag="grp", align_bytes=64)
-            for a in range(2):
-                copy_on(
-                    CAST["w5_%d" % half][a],
-                    grouped[:, a, :, :].rearrange("p (c i) j -> p c j i", i=4),
-                    w5_raw[half][:, a, :, :].rearrange("p j (c i) -> p c j i", i=4),
-                )
-            w5_c[half] = keep.tile([P, 2, 256], U32, name="w5_c%d" % half, align_bytes=64)
-            w5_s[half] = keep.tile([P, 2, 256], U8, name="w5_s%d" % half, align_bytes=64)
-            nc.vector.quantize_mx(
-                out=w5_c[half][:].rearrange("p a c -> p (a c)").bitcast(FP8X4),
-                scales=w5_s[half][:].rearrange("p a c -> p (a c)"),
-                in_=grouped[:].rearrange("p a c j -> p (a c j)"),
-            )
-
-        g_sb = {}
-
-        def gather_g(n, s):
-            g_sb[n, s] = keep.tile([P, SLICES[s]], F32, name="g_sb%d%d" % (n, s))
-            nc.vector.tensor_copy(g_sb[n, s][:], win[n][:].indirect(lst(s)))
-
-        trig_sb = {}
-
-        def angles(s, a):
-            w = SLICES[s]
-            sin_sb = trig.tile([P, 4, w], F32, name="sin_sb", tag="f32")
-            cos_sb = trig.tile([P, 4, w], F32, name="cos_sb", tag="f32")
-            abs_sb = cos_sb
-            for t in range(4):
-                bank = hps.tile([P, 512], F32, name="h_bank")
-                for ka in range(2):
+                    codes, scales = w1_q[a, b]
                     nc.tensor.matmul_mx(
-                        out=bank[:, :w],
-                        lhsT=w1_c[a, ka][:, P * t : P * t + P].bitcast(FP8X4),
-                        lhsT_scale=w1_s[a, ka][:, P * t : P * t + P],
-                        rhs=v_w[s, ka][:].bitcast(FP8X4),
-                        rhs_scale=v_sc[s][4 * ka : P, :],
-                        start=(ka == 0),
-                        stop=(ka == 1),
-                    )
-                b = vecs["bias"][:, a, t : t + 1]
-                nc.scalar.activation(sin_sb[:, t, :], bank[:, :w], ACT.Sin, bias=b)
-                nc.scalar.activation(abs_sb[:, t, :], bank[:, :w], ACT.Abs, bias=b)
-            nc.scalar.activation(cos_sb[:], abs_sb[:], ACT.Sin, bias=math.pi / 2, scale=-1.0)
-            trig_sb[s, a, "s"] = sin_sb
-            trig_sb[s, a, "c"] = cos_sb
-
-        h_c, h_s = {}, {}
-
-        def scale_quant(s, a, kind):
-            w = SLICES[s]
-            src = trig_sb[s, a, kind]
-            amp = vecs["amps" if kind == "s" else "ampc"]
-            grouped = hq.tile([P, w, 4], BF16, name="h_g", tag="grp", align_bytes=64)
-            mode = SI["%d%d%s" % (s, a, kind)]
-            walk_out = grouped[:].rearrange("p (c i) t -> p c t i", i=4)
-            if len(mode) == 1:
-                eng = nc.vector if mode == "V" else nc.gpsimd
-                eng.tensor_tensor(
-                    walk_out,
-                    src[:].rearrange("p t (c i) -> p c t i", i=4),
-                    amp[:, a, :].unsqueeze(1).unsqueeze(3).to_broadcast([P, w // 4, 4, 4]),
-                    ALU.mult,
-                )
-            else:
-                rows = rowp.tile([P, 4, w], BF16, name="h_rows", align_bytes=64)
-                for t in range(4):
-                    if mode[0] == "S":
-                        nc.scalar.activation(rows[:, t, :], src[:, t, :], ACT.Copy, scale=amp[:, a, t : t + 1])
-                    else:
-                        nc.gpsimd.tensor_scalar(rows[:, t, :], src[:, t, :], amp[:, a, t : t + 1], 0.0, ALU.mult, ALU.add)
-                copy_on(mode[1], walk_out, rows[:].rearrange("p t (c i) -> p c t i", i=4))
-            h_c[s, a, kind] = keep.tile([P, w], U32, name="h_c%d%d%s" % (s, a, kind), align_bytes=64)
-            h_s[s, a, kind] = keep.tile([P, w], U8, name="h_s%d%d%s" % (s, a, kind), align_bytes=64)
-            nc.vector.quantize_mx(
-                out=h_c[s, a, kind][:].bitcast(FP8X4), scales=h_s[s, a, kind][:], in_=grouped[:].rearrange("p c t -> p (c t)")
-            )
-
-        left = [len(SLICES)] * 4
-
-        y_banks, y_sbs = {}, {}
-
-        def y_mm(s, n):
-            w = SLICES[s]
-            bank = yps.tile([P, 512], F32, name="y_bank")
-            y_banks[s, n] = bank
-            step = 512 if w == 512 else 128
-            half, col = n // 2, P * (n % 2)
-            for c0 in range(0, w, step):
-                cols = slice(c0, c0 + step)
-                for a in range(2):
-                    nc.tensor.matmul_mx(
-                        out=bank[:, cols],
-                        lhsT=w4_w[:, a, 2 * P * n : 2 * P * n + 2 * P].bitcast(FP4X4),
-                        lhsT_scale=w4_sc[:, a, P * n : P * n + P],
-                        rhs=h_c[s, a, "s"][:, cols].bitcast(FP8X4),
-                        rhs_scale=h_s[s, a, "s"][:, cols],
+                        out=bank[:, :width],
+                        lhsT=codes[:, P * t : P * (t + 1)].bitcast(FP8X4),
+                        lhsT_scale=scales[:, P * t : P * (t + 1)],
+                        rhs=v_w[a][:, cols].bitcast(FP8X4),
+                        rhs_scale=v_sc[4 * a : P, cols],
                         start=(a == 0),
+                        stop=(a == 1),
+                    )
+                column = bias_sb[:, b, t : t + 1]
+                nc.scalar.activation(trig["sin"][:, t, :], bank[:, :width], ACT.Sin, bias=column)
+                nc.scalar.activation(trig["cos"][:, t, :], bank[:, :width], ACT.Abs, bias=column)
+            nc.scalar.activation(trig["cos"][:], trig["cos"][:], ACT.Sin, bias=math.pi / 2, scale=-1.0)
+
+            for kind in ("sin", "cos"):
+                grouped = woven.tile([P, width, PACK], BF16, name="h_grouped", tag="woven", align_bytes=64)
+                if (s, b, kind) in ON_SCALAR:
+                    rows = stage.tile([P, PACK, width], BF16, name="rows", tag="stage", align_bytes=64)
+                    for t in range(PACK):
+                        nc.scalar.activation(
+                            rows[:, t, :], trig[kind][:, t, :], ACT.Copy, scale=amp_sb[kind][:, b, t : t + 1]
+                        )
+                    nc.scalar.copy(
+                        grouped[:].rearrange("p (c i) t -> p c t i", i=4),
+                        rows[:].rearrange("p t (c i) -> p c t i", i=4),
+                    )
+                else:
+                    nc.vector.tensor_tensor(
+                        grouped[:].rearrange("p (c i) t -> p c t i", i=2),
+                        trig[kind][:].rearrange("p t (c i) -> p c t i", i=2),
+                        amp_sb[kind][:, b, :].unsqueeze(1).unsqueeze(3).to_broadcast([P, width // 2, PACK, 2]),
+                        ALU.mult,
+                    )
+                h_q[s, b, kind] = quantise(grouped[:].rearrange("p c t -> p (c t)"), width, "h%d%d%s" % (s, b, kind))
+
+        def retune(s, n):
+            width, cols = SLICES[s], entries(s)
+            bank = y_psum.tile([P, BANK], F32, name="y_bank")
+            step = BANK if width == BANK else P
+            for first in range(0, width, step):
+                part = slice(first, first + step)
+                for b in range(2):
+                    nc.tensor.matmul_mx(
+                        out=bank[:, part],
+                        lhsT=w4_w[:, b, 2 * P * n : 2 * P * (n + 1)].bitcast(FP4X4),
+                        lhsT_scale=w4_sc[:, b, P * n : P * (n + 1)],
+                        rhs=h_q[s, b, "sin"][0][:, part].bitcast(FP8X4),
+                        rhs_scale=h_q[s, b, "sin"][1][:, part],
+                        start=(b == 0),
                         stop=False,
                     )
                     nc.tensor.matmul_mx(
-                        out=bank[:, cols],
-                        lhsT=w5_c[half][:, a, col : col + P].bitcast(FP8X4),
-                        lhsT_scale=w5_s[half][:, a, col : col + P],
-                        rhs=h_c[s, a, "c"][:, cols].bitcast(FP8X4),
-                        rhs_scale=h_s[s, a, "c"][:, cols],
+                        out=bank[:, part],
+                        lhsT=w5_q[b][0][:, P * n : P * (n + 1)].bitcast(FP8X4),
+                        lhsT_scale=w5_q[b][1][:, P * n : P * (n + 1)],
+                        rhs=h_q[s, b, "cos"][0][:, part].bitcast(FP8X4),
+                        rhs_scale=h_q[s, b, "cos"][1][:, part],
                         start=False,
-                        stop=(a == 1),
+                        stop=(b == 1),
                     )
+            if (s, n) == (1, 2):
+                y_sb = stage.tile([P, width], F32, name="y_held", tag="stage", align_bytes=64)
+            else:
+                y_sb = sums.tile([P, width], F32, name="y_sb")
+            nc.scalar.copy(y_sb[:], bank[:, :width])
+            window = phases[n][:].indirect(offsets[:, cols.start // 16 : cols.stop // 16])
+            nc.vector.tensor_tensor(window, old[n][:, cols], y_sb[:], ALU.add)
+            if s == len(SLICES) - 1:
+                nc.sync.dma_start(out[P * n : P * (n + 1), :], phases[n][:])
 
-        def y_ev(s, n):
-            w = SLICES[s]
-            bank = y_banks[s, n]
-            y_sb = ysb.tile([P, w], F32, name="y_sb")
-            y_sbs[s, n] = y_sb
-            nc.scalar.copy(y_sb[:], bank[:, :w])
-
-        def y_sc(s, n):
-            y_sb = y_sbs[s, n]
-            nc.vector.tensor_tensor(win[n][:].indirect(lst(s)), g_sb[n, s][:], y_sb[:], ALU.add)
-            left[n] -= 1
-            if left[n] == 0:
-                nc.sync.dma_start(out[P * n : P * n + P, :], win[n][:])
-
-        def retune(s, n):
-            y_mm(s, n)
-            y_ev(s, n)
-            y_sc(s, n)
-
-        steps = {
-            "ym": y_mm, "ev": y_ev, "sc": y_sc,
-            "gw": gather_words, "gs": gather_scales, "w1": prep_w1, "w5": prep_w5, "gg": gather_g,
-            "ang": angles, "sq": scale_quant, "y": retune,
-        }
-        for step in [["gw",0,0],["gs",0],["gw",0,1],["w1",0,0],["w1",0,1],["w1",1,0],["w1",1,1],["gw",1,0],["gs",1],["gw",1,1],["gw",2,0],["gs",2],["gw",2,1],["w5",0],["w5",1],["ang",0,0],["sq",0,0,"s"],["sq",0,0,"c"],["ang",0,1],["sq",0,1,"s"],["sq",0,1,"c"],["gg",0,0],["gg",0,1],["gg",0,2],["gg",1,0],["gg",1,1],["gg",1,2],["gg",2,0],["gg",2,1],["gg",2,2],["gg",3,0],["gg",3,1],["gg",3,2],["ang",1,0],["sq",1,0,"s"],["sq",1,0,"c"],["y",0,0],["ang",1,1],["sq",1,1,"s"],["sq",1,1,"c"],["y",0,1],["y",0,2],["ang",2,0],["sq",2,0,"s"],["sq",2,0,"c"],["y",0,3],["y",1,0],["ang",2,1],["sq",2,1,"s"],["sq",2,1,"c"],["y",1,1],["y",2,0],["y",2,1],["y",1,2],["y",2,2],["y",1,3],["y",2,3]]:
-            steps[step[0]](*step[1:])
+        angles(0, 0)
+        quantise_w5(0)
+        angles(0, 1)
+        quantise_w5(1)
+        for n in range(N // P):
+            nc.vector.tensor_copy(old[n][:], phases[n][:].indirect(offsets[:]))
+        angles(1, 0)
+        retune(0, 0)
+        retune(0, 1)
+        angles(1, 1)
+        retune(0, 2)
+        retune(0, 3)
+        angles(2, 0)
+        retune(1, 0)
+        retune(1, 1)
+        angles(2, 1)
+        retune(1, 2)
+        retune(2, 0)
+        retune(2, 1)
+        retune(2, 2)
+        retune(1, 3)
+        retune(2, 3)

@@ -62,17 +62,20 @@ def tile_list_choir_phase_retune_kernel(
             nc.sync.dma_start(tile[:], vec.rearrange("(b p t) -> p b t", b=2, t=PACK))
             return tile
 
-        tab_w = [load_table_words(0)]
-        for q in range(4):
-            nc.sync.dma_start(
-                tab_sc[32 * q : 32 * q + 8, :].bitcast(I32), tab_scales[:, 4 * q : 4 * q + 4, :].bitcast(I32)
-            )
-        tab_w.append(load_table_words(1))
-        w1_raw = {(a, 0): load_weight(w1, a, 0, "w1_raw%d0" % a) for a in range(2)}
+        def load_table_scales(a):
+            for q in range(4):
+                rows = tab_sc[32 * q + 4 * a : 32 * q + 4 * a + 4, :]
+                nc.sync.dma_start(rows.bitcast(I32), tab_scales[a, 4 * q : 4 * q + 4, :].bitcast(I32))
+
+        tab_w = [load_table_words(a) for a in range(2)]
+        w1_raw = {}
+        for a in range(2):
+            load_table_scales(a)
+            w1_raw[a, 0] = load_weight(w1, a, 0, "w1_raw%d0" % a)
         bias_sb = load_channel_vector(bias, "bias_sb")
-        w1_raw[0, 1] = load_weight(w1, 0, 1, "w1_raw01")
+        for a in range(2):
+            w1_raw[a, 1] = load_weight(w1, a, 1, "w1_raw%d1" % a)
         amp_sb = {"sin": load_channel_vector(amps, "amps_sb"), "cos": load_channel_vector(ampc, "ampc_sb")}
-        w1_raw[1, 1] = load_weight(w1, 1, 1, "w1_raw11")
         for q in range(4):
             nc.sync.dma_start(
                 w4_sc[32 * q : 32 * q + 4, :, :].bitcast(I32),
@@ -94,18 +97,18 @@ def tile_list_choir_phase_retune_kernel(
 
         v_w = [keep.tile([P, S], U32, name="v_w%d" % a, align_bytes=64) for a in range(2)]
         v_sc = keep.tile([P, S], U8, name="v_sc", align_bytes=64)
-        nc.vector.tensor_copy(v_w[0][:], tab_w[0][:].bitcast(U32).indirect(offsets[:]))
+        for a in range(2):
+            nc.vector.tensor_copy(v_w[a][:], tab_w[a][:].bitcast(U32).indirect(offsets[:]))
         nc.vector.tensor_copy(v_sc[:], tab_sc[:].indirect(offsets[:]))
-        nc.vector.tensor_copy(v_w[1][:], tab_w[1][:].bitcast(U32).indirect(offsets[:]))
 
         def quantise_w1(a, b, copies):
             grouped = woven.tile([P, PACK, P, PACK], BF16, name="w1_grouped", tag="woven", align_bytes=64)
             share = P // len(copies)
             for i, copy in enumerate(copies):
                 copy(
-                    grouped[:, :, share * i : share * (i + 1), :].rearrange("p t m j -> p m j t"),
+                    grouped[:, :, share * i : share * (i + 1), :].rearrange("p t m j -> p m t j"),
                     w1_raw[a, b][:, :, PACK * share * i : PACK * share * (i + 1)].rearrange(
-                        "p j (m t) -> p m j t", t=PACK
+                        "p j (m t) -> p m t j", t=PACK
                     ),
                 )
             return quantise(grouped[:].rearrange("p t m j -> p (t m j)"), PASS, "w1_%d%d" % (a, b))
@@ -213,7 +216,8 @@ def tile_list_choir_phase_retune_kernel(
             window = phases[n][:].indirect(offsets[:, cols.start // 16 : cols.stop // 16])
             nc.vector.tensor_tensor(window, old[n][:, cols], y_sb[:], ALU.add)
             if s == len(SLICES) - 1:
-                nc.sync.dma_start(out[P * n : P * (n + 1), :], phases[n][:])
+                for half in (slice(0, T // 2), slice(T // 2, T)):
+                    nc.sync.dma_start(out[P * n : P * (n + 1), half], phases[n][:, half])
 
         angles(0, 0)
         quantise_w5(0)

@@ -20,98 +20,105 @@ ALU = mybir.AluOpType
 P = 128
 PACK = 4
 PASS = P * PACK
+PASSES = K // PASS
 BANK = 512
+ROW_TILES = N // P
+ENTRIES_PER_COLUMN = 16
+
 SLICES = (256, 512, 256)
-ON_SCALAR = ((1, 0, "sin"), (1, 1, "sin"), (2, 0, "sin"), (2, 1, "sin"))
+H_BANKS, Y_BANKS = 5, 3
+WIDE_BUFS, WOVEN_BUFS, SUMS_BUFS = 9, 3, 6
 
 
 def tile_list_choir_phase_retune_kernel(
     tc, tab_words, tab_scales, offs, gT, w1, bias, w4_words, w4_scales, w5, amps, ampc, out
 ):
     nc = tc.nc
+    last = len(SLICES) - 1
     with ExitStack() as ctx:
         keep = ctx.enter_context(tc.tile_pool(name="keep", bufs=1))
-        wide = ctx.enter_context(tc.tile_pool(name="wide", bufs=10))
-        woven = ctx.enter_context(tc.tile_pool(name="woven", bufs=4))
+        wide = ctx.enter_context(tc.tile_pool(name="wide", bufs=WIDE_BUFS))
+        woven = ctx.enter_context(tc.tile_pool(name="woven", bufs=WOVEN_BUFS))
         stage = ctx.enter_context(tc.tile_pool(name="stage", bufs=1))
-        sums = ctx.enter_context(tc.tile_pool(name="sums", bufs=6))
-        h_psum = ctx.enter_context(tc.psum_pool(name="h_psum", bufs=5))
-        y_psum = ctx.enter_context(tc.psum_pool(name="y_psum", bufs=3))
+        sums = ctx.enter_context(tc.tile_pool(name="sums", bufs=SUMS_BUFS))
+        h_psum = ctx.enter_context(tc.psum_pool(name="h_psum", bufs=H_BANKS))
+        y_psum = ctx.enter_context(tc.psum_pool(name="y_psum", bufs=Y_BANKS))
 
-        offsets = keep.tile([P, S // 16], U16, name="offsets")
+        offsets = keep.tile([P, S // ENTRIES_PER_COLUMN], U16, name="offsets")
         nc.sync.dma_start(offsets[:], offs)
 
         tab_sc = keep.tile([P, T], U8, name="tab_sc", align_bytes=64)
         nc.vector.memset(tab_sc[:].bitcast(I32), 0)
-        w4_sc = keep.tile([P, 2, N], U8, name="w4_sc", align_bytes=64)
-        nc.gpsimd.memset(w4_sc[:].rearrange("p a c -> p (a c)").bitcast(I32), 0)
+        w4_sc = keep.tile([P, PASSES, N], U8, name="w4_sc", align_bytes=64)
+        nc.gpsimd.memset(w4_sc[:].rearrange("p b c -> p (b c)").bitcast(I32), 0)
 
         def load_table_words(a):
             words = keep.tile([P, T], I32, name="tab_w%d" % a, align_bytes=64)
-            nc.sync.dma_start(words[:], tab_words[a].rearrange("p t i -> p (t i)").bitcast(I32))
+            nc.sync.dma_start(words[:], tab_words[a].rearrange("p e j -> p (e j)").bitcast(I32))
             return words
 
-        def load_weight(w, a, b, name):
+        def load_table_scales(a):
+            for quadrant in range(4):
+                first = 32 * quadrant + 4 * a
+                blocks = tab_scales[a, 4 * quadrant : 4 * quadrant + 4, :]
+                nc.sync.dma_start(tab_sc[first : first + 4, :].bitcast(I32), blocks.bitcast(I32))
+
+        def load_weight(weight, rows, cols, name):
             raw = wide.tile([P, PACK, PASS], F32, name=name, tag="wide")
-            block = w[PASS * a : PASS * (a + 1), PASS * b : PASS * (b + 1)]
+            block = weight[PASS * rows : PASS * (rows + 1), PASS * cols : PASS * (cols + 1)]
             nc.sync.dma_start(raw[:], block.rearrange("(p j) c -> p j c", j=PACK))
             return raw
 
         def load_channel_vector(vec, name):
-            tile = keep.tile([P, 2, PACK], F32, name=name)
-            nc.sync.dma_start(tile[:], vec.rearrange("(b p t) -> p b t", b=2, t=PACK))
+            tile = keep.tile([P, PASSES, PACK], F32, name=name)
+            nc.sync.dma_start(tile[:], vec.rearrange("(b p t) -> p b t", b=PASSES, t=PACK))
             return tile
 
-        def load_table_scales(a):
-            for q in range(4):
-                rows = tab_sc[32 * q + 4 * a : 32 * q + 4 * a + 4, :]
-                nc.sync.dma_start(rows.bitcast(I32), tab_scales[a, 4 * q : 4 * q + 4, :].bitcast(I32))
-
-        tab_w = [load_table_words(a) for a in range(2)]
+        tab_w = [load_table_words(a) for a in range(PASSES)]
         w1_raw = {}
-        for a in range(2):
+        for a in range(PASSES):
             load_table_scales(a)
             w1_raw[a, 0] = load_weight(w1, a, 0, "w1_raw%d0" % a)
         bias_sb = load_channel_vector(bias, "bias_sb")
-        for a in range(2):
+        for a in range(PASSES):
             w1_raw[a, 1] = load_weight(w1, a, 1, "w1_raw%d1" % a)
         amp_sb = {"sin": load_channel_vector(amps, "amps_sb"), "cos": load_channel_vector(ampc, "ampc_sb")}
-        for q in range(4):
+        for quadrant in range(4):
             nc.sync.dma_start(
-                w4_sc[32 * q : 32 * q + 4, :, :].bitcast(I32),
-                w4_scales[:, 4 * q : 4 * q + 4, :].rearrange("a r c -> r a c").bitcast(I32),
+                w4_sc[32 * quadrant : 32 * quadrant + 4, :, :].bitcast(I32),
+                w4_scales[:, 4 * quadrant : 4 * quadrant + 4, :].rearrange("b q c -> q b c").bitcast(I32),
             )
-        w4_w = keep.tile([P, 2, 2 * N], U8, name="w4_w", align_bytes=64)
-        nc.sync.dma_start(w4_w[:].bitcast(I32), w4_words.rearrange("a p c -> p a c").bitcast(I32))
-        w5_raw = [load_weight(w5, b, 0, "w5_raw%d" % b) for b in range(2)]
+        w4_w = keep.tile([P, PASSES, 2 * N], U8, name="w4_w", align_bytes=64)
+        nc.sync.dma_start(w4_w[:].bitcast(I32), w4_words.rearrange("b p c -> p b c").bitcast(I32))
+        w5_raw = [load_weight(w5, b, 0, "w5_raw%d" % b) for b in range(PASSES)]
         phases = []
-        for n in range(N // P):
+        for n in range(ROW_TILES):
             phases.append(keep.tile([P, T], F32, name="phases%d" % n, align_bytes=64))
             nc.sync.dma_start(phases[n][:], gT[P * n : P * (n + 1), :])
 
-        def quantise(grouped, width, name):
-            codes = keep.tile([P, width], U32, name=name + "_codes", align_bytes=64)
-            scales = keep.tile([P, width], U8, name=name + "_scales", align_bytes=64)
-            nc.vector.quantize_mx(out=codes[:].bitcast(FP8X4), scales=scales[:], in_=grouped)
+        def quantise(values, columns, name):
+            codes = keep.tile([P, columns], U32, name=name + "_codes", align_bytes=64)
+            scales = keep.tile([P, columns], U8, name=name + "_scales", align_bytes=64)
+            nc.vector.quantize_mx(out=codes[:].bitcast(FP8X4), scales=scales[:], in_=values)
             return codes, scales
 
-        v_w = [keep.tile([P, S], U32, name="v_w%d" % a, align_bytes=64) for a in range(2)]
+        v_w = [keep.tile([P, S], U32, name="v_w%d" % a, align_bytes=64) for a in range(PASSES)]
         v_sc = keep.tile([P, S], U8, name="v_sc", align_bytes=64)
-        for a in range(2):
+        for a in range(PASSES):
             nc.vector.tensor_copy(v_w[a][:], tab_w[a][:].bitcast(U32).indirect(offsets[:]))
         nc.vector.tensor_copy(v_sc[:], tab_sc[:].indirect(offsets[:]))
 
         def quantise_w1(a, b, copies):
-            grouped = woven.tile([P, PACK, P, PACK], BF16, name="w1_grouped", tag="woven", align_bytes=64)
+            values = woven.tile([P, PACK, P, PACK], BF16, name="w1_woven", tag="woven", align_bytes=64)
             share = P // len(copies)
             for i, copy in enumerate(copies):
                 copy(
-                    grouped[:, :, share * i : share * (i + 1), :].rearrange("p t m j -> p m t j"),
+                    values[:, :, share * i : share * (i + 1), :].rearrange("p t m j -> p m t j"),
                     w1_raw[a, b][:, :, PACK * share * i : PACK * share * (i + 1)].rearrange(
                         "p j (m t) -> p m t j", t=PACK
                     ),
                 )
-            return quantise(grouped[:].rearrange("p t m j -> p (t m j)"), PASS, "w1_%d%d" % (a, b))
+            return quantise(values[:].rearrange("p t m j -> p (t m j)"), PASS, "w1_%d%d" % (a, b))
 
         w1_q = {
             (0, 0): quantise_w1(0, 0, [nc.scalar.copy]),
@@ -120,17 +127,13 @@ def tile_list_choir_phase_retune_kernel(
             (1, 1): quantise_w1(1, 1, [nc.vector.tensor_copy]),
         }
 
-        w5_q = {}
-
         def quantise_w5(b):
-            grouped = woven.tile([P, N, PACK], BF16, name="w5_grouped", tag="woven", align_bytes=64)
+            values = woven.tile([P, N, PACK], BF16, name="w5_woven", tag="woven", align_bytes=64)
             nc.vector.tensor_copy(
-                grouped[:].rearrange("p (c i) j -> p c j i", i=2),
+                values[:].rearrange("p (c i) j -> p c j i", i=2),
                 w5_raw[b][:].rearrange("p j (c i) -> p c j i", i=2),
             )
-            w5_q[b] = quantise(grouped[:].rearrange("p c j -> p (c j)"), N, "w5_%d" % b)
-
-        old = [keep.tile([P, S], F32, name="old%d" % n) for n in range(N // P)]
+            return quantise(values[:].rearrange("p c j -> p (c j)"), N, "w5_%d" % b)
 
         def entries(s):
             first = sum(SLICES[:s])
@@ -146,7 +149,7 @@ def tile_list_choir_phase_retune_kernel(
             }
             for t in range(PACK):
                 bank = h_psum.tile([P, BANK], F32, name="h_bank")
-                for a in range(2):
+                for a in range(PASSES):
                     codes, scales = w1_q[a, b]
                     nc.tensor.matmul_mx(
                         out=bank[:, :width],
@@ -155,89 +158,90 @@ def tile_list_choir_phase_retune_kernel(
                         rhs=v_w[a][:, cols].bitcast(FP8X4),
                         rhs_scale=v_sc[4 * a : P, cols],
                         start=(a == 0),
-                        stop=(a == 1),
+                        stop=(a == PASSES - 1),
                     )
-                column = bias_sb[:, b, t : t + 1]
-                nc.scalar.activation(trig["sin"][:, t, :], bank[:, :width], ACT.Sin, bias=column)
-                nc.scalar.activation(trig["cos"][:, t, :], bank[:, :width], ACT.Abs, bias=column)
+                bias_t = bias_sb[:, b, t : t + 1]
+                nc.scalar.activation(trig["sin"][:, t, :], bank[:, :width], ACT.Sin, bias=bias_t)
+                nc.scalar.activation(trig["cos"][:, t, :], bank[:, :width], ACT.Abs, bias=bias_t)
             nc.scalar.activation(trig["cos"][:], trig["cos"][:], ACT.Sin, bias=math.pi / 2, scale=-1.0)
 
-            for kind in ("sin", "cos"):
-                grouped = woven.tile([P, width, PACK], BF16, name="h_grouped", tag="woven", align_bytes=64)
-                if (s, b, kind) in ON_SCALAR:
-                    rows = stage.tile([P, PACK, width], BF16, name="rows", tag="stage", align_bytes=64)
+            values = woven.tile([P, 2, width, PACK], BF16, name="h_woven", tag="woven", align_bytes=64)
+            for half, kind in enumerate(("sin", "cos")):
+                target = values[:, half, :, :]
+                if kind == "sin" and s > 0:
+                    rounded = stage.tile([P, PACK, width], BF16, name="rounded", tag="stage", align_bytes=64)
                     for t in range(PACK):
-                        nc.scalar.activation(
-                            rows[:, t, :], trig[kind][:, t, :], ACT.Copy, scale=amp_sb[kind][:, b, t : t + 1]
-                        )
+                        amp_t = amp_sb[kind][:, b, t : t + 1]
+                        nc.scalar.activation(rounded[:, t, :], trig[kind][:, t, :], ACT.Copy, scale=amp_t)
                     nc.scalar.copy(
-                        grouped[:].rearrange("p (c i) t -> p c t i", i=4),
-                        rows[:].rearrange("p t (c i) -> p c t i", i=4),
+                        target.rearrange("p (c i) t -> p c t i", i=4),
+                        rounded[:].rearrange("p t (c i) -> p c t i", i=4),
                     )
                 else:
+                    amp = amp_sb[kind][:, b, :].unsqueeze(1).unsqueeze(3)
                     nc.vector.tensor_tensor(
-                        grouped[:].rearrange("p (c i) t -> p c t i", i=2),
+                        target.rearrange("p (c i) t -> p c t i", i=2),
                         trig[kind][:].rearrange("p t (c i) -> p c t i", i=2),
-                        amp_sb[kind][:, b, :].unsqueeze(1).unsqueeze(3).to_broadcast([P, width // 2, PACK, 2]),
+                        amp.to_broadcast([P, width // 2, PACK, 2]),
                         ALU.mult,
                     )
-                h_q[s, b, kind] = quantise(grouped[:].rearrange("p c t -> p (c t)"), width, "h%d%d%s" % (s, b, kind))
+            h_q[s, b] = quantise(values[:].rearrange("p h c t -> p (h c t)"), 2 * width, "h%d%d" % (s, b))
 
         def retune(s, n):
             width, cols = SLICES[s], entries(s)
             bank = y_psum.tile([P, BANK], F32, name="y_bank")
-            step = BANK if width == BANK else P
-            for first in range(0, width, step):
-                part = slice(first, first + step)
-                for b in range(2):
+            group = BANK if width == BANK else P
+            for first in range(0, width, group):
+                hs_cols = slice(first, first + group)
+                hc_cols = slice(width + first, width + first + group)
+                for b in range(PASSES):
+                    codes, scales = h_q[s, b]
                     nc.tensor.matmul_mx(
-                        out=bank[:, part],
+                        out=bank[:, hs_cols],
                         lhsT=w4_w[:, b, 2 * P * n : 2 * P * (n + 1)].bitcast(FP4X4),
                         lhsT_scale=w4_sc[:, b, P * n : P * (n + 1)],
-                        rhs=h_q[s, b, "sin"][0][:, part].bitcast(FP8X4),
-                        rhs_scale=h_q[s, b, "sin"][1][:, part],
+                        rhs=codes[:, hs_cols].bitcast(FP8X4),
+                        rhs_scale=scales[:, hs_cols],
                         start=(b == 0),
                         stop=False,
                     )
                     nc.tensor.matmul_mx(
-                        out=bank[:, part],
+                        out=bank[:, hs_cols],
                         lhsT=w5_q[b][0][:, P * n : P * (n + 1)].bitcast(FP8X4),
                         lhsT_scale=w5_q[b][1][:, P * n : P * (n + 1)],
-                        rhs=h_q[s, b, "cos"][0][:, part].bitcast(FP8X4),
-                        rhs_scale=h_q[s, b, "cos"][1][:, part],
+                        rhs=codes[:, hc_cols].bitcast(FP8X4),
+                        rhs_scale=scales[:, hc_cols],
                         start=False,
-                        stop=(b == 1),
+                        stop=(b == PASSES - 1),
                     )
-            if (s, n) == (1, 2):
+            if (s, n) == (last - 1, ROW_TILES - 2):
                 y_sb = stage.tile([P, width], F32, name="y_held", tag="stage", align_bytes=64)
             else:
                 y_sb = sums.tile([P, width], F32, name="y_sb")
             nc.scalar.copy(y_sb[:], bank[:, :width])
-            window = phases[n][:].indirect(offsets[:, cols.start // 16 : cols.stop // 16])
-            nc.vector.tensor_tensor(window, old[n][:, cols], y_sb[:], ALU.add)
-            if s == len(SLICES) - 1:
-                for half in (slice(0, T // 2), slice(T // 2, T)):
-                    nc.sync.dma_start(out[P * n : P * (n + 1), half], phases[n][:, half])
+            places = offsets[:, cols.start // ENTRIES_PER_COLUMN : cols.stop // ENTRIES_PER_COLUMN]
+            nc.vector.tensor_tensor(phases[n][:].indirect(places), old[n][:, cols], y_sb[:], ALU.add)
+            if s == last:
+                for part in (slice(0, T // 2), slice(T // 2, T)):
+                    nc.sync.dma_start(out[P * n : P * (n + 1), part], phases[n][:, part])
 
-        angles(0, 0)
-        quantise_w5(0)
-        angles(0, 1)
-        quantise_w5(1)
-        for n in range(N // P):
+        w5_q = []
+        for b in range(PASSES):
+            angles(0, b)
+            w5_q.append(quantise_w5(b))
+
+        old = [keep.tile([P, S], F32, name="old%d" % n) for n in range(ROW_TILES)]
+        for n in range(ROW_TILES):
             nc.vector.tensor_copy(old[n][:], phases[n][:].indirect(offsets[:]))
-        angles(1, 0)
-        retune(0, 0)
-        retune(0, 1)
-        angles(1, 1)
-        retune(0, 2)
-        retune(0, 3)
-        angles(2, 0)
-        retune(1, 0)
-        retune(1, 1)
-        angles(2, 1)
-        retune(1, 2)
-        retune(2, 0)
-        retune(2, 1)
-        retune(2, 2)
-        retune(1, 3)
-        retune(2, 3)
+
+        kept_back = (last - 1, ROW_TILES - 1)
+        for s in range(1, last + 1):
+            for b in range(PASSES):
+                angles(s, b)
+                for n in (2 * b, 2 * b + 1):
+                    if (s - 1, n) != kept_back:
+                        retune(s - 1, n)
+        for n in range(ROW_TILES - 1):
+            retune(last, n)
+        retune(*kept_back)
+        retune(last, ROW_TILES - 1)

@@ -26,6 +26,7 @@ ROW_TILES = N // P
 ENTRIES_PER_COLUMN = 16
 
 SLICES = (256, 512, 256)
+SCALAR_GROUPS = 48
 H_BANKS, Y_BANKS = 5, 3
 WIDE_BUFS, WOVEN_BUFS, SUMS_BUFS = 9, 3, 6
 
@@ -48,7 +49,7 @@ def tile_list_choir_phase_retune_kernel(
         nc.sync.dma_start(offsets[:], offs)
 
         tab_sc = keep.tile([P, T], U8, name="tab_sc", align_bytes=64)
-        nc.vector.memset(tab_sc[:].bitcast(I32), 0)
+        nc.gpsimd.memset(tab_sc[:].bitcast(I32), 0)
         w4_sc = keep.tile([P, PASSES, N], U8, name="w4_sc", align_bytes=64)
         nc.gpsimd.memset(w4_sc[:].rearrange("p b c -> p (b c)").bitcast(I32), 0)
 
@@ -56,12 +57,6 @@ def tile_list_choir_phase_retune_kernel(
             words = keep.tile([P, T], I32, name="tab_w%d" % a, align_bytes=64)
             nc.sync.dma_start(words[:], tab_words[a].rearrange("p e j -> p (e j)").bitcast(I32))
             return words
-
-        def load_table_scales(a):
-            for quadrant in range(4):
-                first = 32 * quadrant + 4 * a
-                blocks = tab_scales[a, 4 * quadrant : 4 * quadrant + 4, :]
-                nc.sync.dma_start(tab_sc[first : first + 4, :].bitcast(I32), blocks.bitcast(I32))
 
         def load_weight(weight, rows, cols, name):
             raw = wide.tile([P, PACK, PASS], F32, name=name, tag="wide")
@@ -74,12 +69,12 @@ def tile_list_choir_phase_retune_kernel(
             nc.sync.dma_start(tile[:], vec.rearrange("(b p t) -> p b t", b=PASSES, t=PACK))
             return tile
 
-        tab_w = [load_table_words(a) for a in range(PASSES)]
-        w1_raw = {}
-        for a in range(PASSES):
-            load_table_scales(a)
-            w1_raw[a, 0] = load_weight(w1, a, 0, "w1_raw%d0" % a)
         bias_sb = load_channel_vector(bias, "bias_sb")
+        for quadrant in range(4):
+            blocks = tab_scales[:, 4 * quadrant : 4 * quadrant + 4, :]
+            nc.sync.dma_start(tab_sc[32 * quadrant : 32 * quadrant + 8, :].bitcast(I32), blocks.bitcast(I32))
+        tab_w = [load_table_words(a) for a in range(PASSES)]
+        w1_raw = {(a, 0): load_weight(w1, a, 0, "w1_raw%d0" % a) for a in range(PASSES)}
         for a in range(PASSES):
             w1_raw[a, 1] = load_weight(w1, a, 1, "w1_raw%d1" % a)
         amp_sb = {"sin": load_channel_vector(amps, "amps_sb"), "cos": load_channel_vector(ampc, "ampc_sb")}
@@ -104,17 +99,20 @@ def tile_list_choir_phase_retune_kernel(
 
         v_w = [keep.tile([P, S], U32, name="v_w%d" % a, align_bytes=64) for a in range(PASSES)]
         v_sc = keep.tile([P, S], U8, name="v_sc", align_bytes=64)
+        nc.vector.tensor_copy(v_sc[:], tab_sc[:].indirect(offsets[:]))
         for a in range(PASSES):
             nc.vector.tensor_copy(v_w[a][:], tab_w[a][:].bitcast(U32).indirect(offsets[:]))
-        nc.vector.tensor_copy(v_sc[:], tab_sc[:].indirect(offsets[:]))
+
+        def places(cols):
+            return offsets[:, cols.start // ENTRIES_PER_COLUMN : cols.stop // ENTRIES_PER_COLUMN]
 
         def quantise_w1(a, b, copies):
             values = woven.tile([P, PACK, P, PACK], BF16, name="w1_woven", tag="woven", align_bytes=64)
-            share = P // len(copies)
+            cuts = (0, P) if len(copies) == 1 else (0, SCALAR_GROUPS, P)
             for i, copy in enumerate(copies):
                 copy(
-                    values[:, :, share * i : share * (i + 1), :].rearrange("p t m j -> p m t j"),
-                    w1_raw[a, b][:, :, PACK * share * i : PACK * share * (i + 1)].rearrange(
+                    values[:, :, cuts[i] : cuts[i + 1], :].rearrange("p t m j -> p m t j"),
+                    w1_raw[a, b][:, :, PACK * cuts[i] : PACK * cuts[i + 1]].rearrange(
                         "p j (m t) -> p m t j", t=PACK
                     ),
                 )
@@ -123,9 +121,9 @@ def tile_list_choir_phase_retune_kernel(
         w1_q = {
             (0, 0): quantise_w1(0, 0, [nc.scalar.copy]),
             (1, 0): quantise_w1(1, 0, [nc.scalar.copy, nc.vector.tensor_copy]),
-            (0, 1): quantise_w1(0, 1, [nc.vector.tensor_copy]),
-            (1, 1): quantise_w1(1, 1, [nc.vector.tensor_copy]),
         }
+        for a in range(PASSES):
+            w1_q[a, 1] = quantise_w1(a, 1, [nc.vector.tensor_copy])
 
         def quantise_w5(b):
             values = woven.tile([P, N, PACK], BF16, name="w5_woven", tag="woven", align_bytes=64)
@@ -219,8 +217,7 @@ def tile_list_choir_phase_retune_kernel(
             else:
                 y_sb = sums.tile([P, width], F32, name="y_sb")
             nc.scalar.copy(y_sb[:], bank[:, :width])
-            places = offsets[:, cols.start // ENTRIES_PER_COLUMN : cols.stop // ENTRIES_PER_COLUMN]
-            nc.vector.tensor_tensor(phases[n][:].indirect(places), old[n][:, cols], y_sb[:], ALU.add)
+            nc.vector.tensor_tensor(phases[n][:].indirect(places(cols)), old[n][:, cols], y_sb[:], ALU.add)
             if s == last:
                 for part in (slice(0, T // 2), slice(T // 2, T)):
                     nc.sync.dma_start(out[P * n : P * (n + 1), part], phases[n][:, part])

@@ -27,6 +27,7 @@ ENTRIES_PER_COLUMN = 16
 
 SLICES = (256, 512, 256)
 SCALAR_GROUPS = 48
+GPSIMD_COLUMNS = 256
 H_BANKS, Y_BANKS = 5, 3
 WIDE_BUFS, WOVEN_BUFS, SUMS_BUFS = 9, 3, 6
 
@@ -69,15 +70,17 @@ def tile_list_choir_phase_retune_kernel(
             nc.sync.dma_start(tile[:], vec.rearrange("(b p t) -> p b t", b=PASSES, t=PACK))
             return tile
 
-        bias_sb = load_channel_vector(bias, "bias_sb")
+        tab_w = [load_table_words(0)]
         for quadrant in range(4):
             blocks = tab_scales[:, 4 * quadrant : 4 * quadrant + 4, :]
             nc.sync.dma_start(tab_sc[32 * quadrant : 32 * quadrant + 8, :].bitcast(I32), blocks.bitcast(I32))
-        tab_w = [load_table_words(a) for a in range(PASSES)]
+        tab_w.append(load_table_words(1))
         w1_raw = {(a, 0): load_weight(w1, a, 0, "w1_raw%d0" % a) for a in range(PASSES)}
+        bias_sb = load_channel_vector(bias, "bias_sb")
         for a in range(PASSES):
             w1_raw[a, 1] = load_weight(w1, a, 1, "w1_raw%d1" % a)
         amp_sb = {"sin": load_channel_vector(amps, "amps_sb"), "cos": load_channel_vector(ampc, "ampc_sb")}
+        w5_raw = [load_weight(w5, 0, 0, "w5_raw0")]
         for quadrant in range(4):
             nc.sync.dma_start(
                 w4_sc[32 * quadrant : 32 * quadrant + 4, :, :].bitcast(I32),
@@ -85,7 +88,7 @@ def tile_list_choir_phase_retune_kernel(
             )
         w4_w = keep.tile([P, PASSES, 2 * N], U8, name="w4_w", align_bytes=64)
         nc.sync.dma_start(w4_w[:].bitcast(I32), w4_words.rearrange("b p c -> p b c").bitcast(I32))
-        w5_raw = [load_weight(w5, b, 0, "w5_raw%d" % b) for b in range(PASSES)]
+        w5_raw.append(load_weight(w5, 1, 0, "w5_raw1"))
         phases = []
         for n in range(ROW_TILES):
             phases.append(keep.tile([P, T], F32, name="phases%d" % n, align_bytes=64))
@@ -167,14 +170,25 @@ def tile_list_choir_phase_retune_kernel(
             for half, kind in enumerate(("sin", "cos")):
                 target = values[:, half, :, :]
                 if kind == "sin" and s > 0:
-                    rounded = stage.tile([P, PACK, width], BF16, name="rounded", tag="stage", align_bytes=64)
+                    if (s, b) == (1, 0):
+                        rounded = keep.tile([P, PACK, width], BF16, name="rounded%d%d" % (s, b), align_bytes=64)
+                    else:
+                        rounded = stage.tile([P, PACK, width], BF16, name="rounded", tag="stage", align_bytes=64)
                     for t in range(PACK):
                         amp_t = amp_sb[kind][:, b, t : t + 1]
                         nc.scalar.activation(rounded[:, t, :], trig[kind][:, t, :], ACT.Copy, scale=amp_t)
-                    nc.scalar.copy(
-                        target.rearrange("p (c i) t -> p c t i", i=4),
-                        rounded[:].rearrange("p t (c i) -> p c t i", i=4),
-                    )
+                    if (s, b) == (1, 0):
+                        for first in range(0, width, GPSIMD_COLUMNS):
+                            part = slice(first, first + GPSIMD_COLUMNS)
+                            nc.gpsimd.tensor_scalar(
+                                target[:, part, :], rounded[:, :, part].rearrange("p t c -> p c t"),
+                                1.0, 1.0, ALU.mult, ALU.mult,
+                            )
+                    else:
+                        nc.scalar.copy(
+                            target.rearrange("p (c i) t -> p c t i", i=4),
+                            rounded[:].rearrange("p t (c i) -> p c t i", i=4),
+                        )
                 else:
                     amp = amp_sb[kind][:, b, :].unsqueeze(1).unsqueeze(3)
                     nc.vector.tensor_tensor(
@@ -231,14 +245,18 @@ def tile_list_choir_phase_retune_kernel(
         for n in range(ROW_TILES):
             nc.vector.tensor_copy(old[n][:], phases[n][:].indirect(offsets[:]))
 
-        kept_back = (last - 1, ROW_TILES - 1)
-        for s in range(1, last + 1):
-            for b in range(PASSES):
-                angles(s, b)
-                for n in (2 * b, 2 * b + 1):
-                    if (s - 1, n) != kept_back:
-                        retune(s - 1, n)
+        angles(1, 0)
+        retune(0, 0)
+        retune(0, 1)
+        angles(1, 1)
+        retune(0, 2)
+        retune(0, 3)
+        angles(2, 0)
+        retune(1, 0)
+        retune(1, 1)
+        angles(2, 1)
+        retune(1, 2)
         for n in range(ROW_TILES - 1):
             retune(last, n)
-        retune(*kept_back)
+        retune(1, 3)
         retune(last, ROW_TILES - 1)

@@ -29,7 +29,7 @@ SLICES = (256, 512, 256)
 SCALAR_GROUPS = 48
 GPSIMD_COLUMNS = 256
 H_BANKS, Y_BANKS = 5, 3
-WIDE_BUFS, WOVEN_BUFS, SUMS_BUFS = 9, 3, 6
+WIDE_BUFS, WOVEN_BUFS, SUMS_BUFS = 9, 3, 5
 
 
 def tile_list_choir_phase_retune_kernel(
@@ -166,10 +166,13 @@ def tile_list_choir_phase_retune_kernel(
                 nc.scalar.activation(trig["cos"][:, t, :], bank[:, :width], ACT.Abs, bias=bias_t)
             nc.scalar.activation(trig["cos"][:], trig["cos"][:], ACT.Sin, bias=math.pi / 2, scale=-1.0)
 
-            values = woven.tile([P, 2, width, PACK], BF16, name="h_woven", tag="woven", align_bytes=64)
+            if (s, b) in ((0, 1), (1, 0)):
+                values = stage.tile([P, 2, width, PACK], BF16, name="h_woven", tag="handover", align_bytes=64)
+            else:
+                values = woven.tile([P, 2, width, PACK], BF16, name="h_woven", tag="woven", align_bytes=64)
             for half, kind in enumerate(("sin", "cos")):
                 target = values[:, half, :, :]
-                if kind == "sin" and s > 0:
+                if kind == ("cos" if (s, b) == (1, 0) else "sin") and s > 0:
                     if (s, b) == (1, 0):
                         rounded = keep.tile([P, PACK, width], BF16, name="rounded%d%d" % (s, b), align_bytes=64)
                     else:
@@ -191,12 +194,14 @@ def tile_list_choir_phase_retune_kernel(
                         )
                 else:
                     amp = amp_sb[kind][:, b, :].unsqueeze(1).unsqueeze(3)
-                    nc.vector.tensor_tensor(
-                        target.rearrange("p (c i) t -> p c t i", i=2),
-                        trig[kind][:].rearrange("p t (c i) -> p c t i", i=2),
-                        amp.to_broadcast([P, width // 2, PACK, 2]),
-                        ALU.mult,
-                    )
+                    engine, piece = (nc.gpsimd, GPSIMD_COLUMNS) if (s, b) == (1, 0) else (nc.vector, width)
+                    for first in range(0, width, piece):
+                        engine.tensor_tensor(
+                            target[:, first : first + piece, :].rearrange("p (c i) t -> p c t i", i=2),
+                            trig[kind][:, :, first : first + piece].rearrange("p t (c i) -> p c t i", i=2),
+                            amp.to_broadcast([P, piece // 2, PACK, 2]),
+                            ALU.mult,
+                        )
             h_q[s, b] = quantise(values[:].rearrange("p h c t -> p (h c t)"), 2 * width, "h%d%d" % (s, b))
 
         def retune(s, n):

@@ -172,7 +172,7 @@ def tile_list_choir_phase_retune_kernel(
                 values = woven.tile([P, 2, width, PACK], BF16, name="h_woven", tag="woven", align_bytes=64)
             for half, kind in enumerate(("sin", "cos")):
                 target = values[:, half, :, :]
-                if kind == ("cos" if (s, b) == (1, 0) else "sin") and s > 0:
+                if kind == ("sin" if (s, b) == (1, 1) else "cos") and s > 0:
                     if (s, b) == (1, 0):
                         rounded = keep.tile([P, PACK, width], BF16, name="rounded%d%d" % (s, b), align_bytes=64)
                     else:
@@ -194,7 +194,7 @@ def tile_list_choir_phase_retune_kernel(
                         )
                 else:
                     amp = amp_sb[kind][:, b, :].unsqueeze(1).unsqueeze(3)
-                    engine, piece = (nc.gpsimd, GPSIMD_COLUMNS) if (s, b) == (1, 0) else (nc.vector, width)
+                    engine, piece = (nc.gpsimd, GPSIMD_COLUMNS) if kind == "sin" and s > 0 else (nc.vector, width)
                     for first in range(0, width, piece):
                         engine.tensor_tensor(
                             target[:, first : first + piece, :].rearrange("p (c i) t -> p c t i", i=2),
@@ -235,8 +235,12 @@ def tile_list_choir_phase_retune_kernel(
                 y_sb = stage.tile([P, width], F32, name="y_held", tag="stage", align_bytes=64)
             else:
                 y_sb = sums.tile([P, width], F32, name="y_sb")
-            nc.scalar.copy(y_sb[:], bank[:, :width])
-            nc.vector.tensor_tensor(phases[n][:].indirect(places(cols)), old[n][:, cols], y_sb[:], ALU.add)
+            if s == 1 and n < 2:
+                nc.vector.tensor_tensor(y_sb[:], bank[:, :width], old[n][:, cols], ALU.add)
+                nc.vector.tensor_copy(phases[n][:].indirect(places(cols)), y_sb[:])
+            else:
+                nc.scalar.copy(y_sb[:], bank[:, :width])
+                nc.vector.tensor_tensor(phases[n][:].indirect(places(cols)), old[n][:, cols], y_sb[:], ALU.add)
             if s == last:
                 for part in (slice(0, T // 2), slice(T // 2, T)):
                     nc.sync.dma_start(out[P * n : P * (n + 1), part], phases[n][:, part])

@@ -25,26 +25,25 @@ BANK = 512
 ROW_TILES = N // P
 ENTRIES_PER_COLUMN = 16
 
-SLICES = (256, 512, 256)
-SCALAR_GROUPS = 48
-GPSIMD_COLUMNS = 256
-H_BANKS, Y_BANKS = 5, 3
-WIDE_BUFS, WOVEN_BUFS, SUMS_BUFS = 9, 3, 5
+SLICES = 4
+WIDTH = S // SLICES
+KIB = 1024
+H_BANKS, Y_BANKS = 4, 4
 
 
 def tile_list_choir_phase_retune_kernel(
     tc, tab_words, tab_scales, offs, gT, w1, bias, w4_words, w4_scales, w5, amps, ampc, out
 ):
     nc = tc.nc
-    last = len(SLICES) - 1
+    last = SLICES - 1
     with ExitStack() as ctx:
         keep = ctx.enter_context(tc.tile_pool(name="keep", bufs=1))
-        wide = ctx.enter_context(tc.tile_pool(name="wide", bufs=WIDE_BUFS))
-        woven = ctx.enter_context(tc.tile_pool(name="woven", bufs=WOVEN_BUFS))
-        stage = ctx.enter_context(tc.tile_pool(name="stage", bufs=1))
-        sums = ctx.enter_context(tc.tile_pool(name="sums", bufs=SUMS_BUFS))
+        arena = ctx.enter_context(tc.tile_pool(name="arena", bufs=1))
         h_psum = ctx.enter_context(tc.psum_pool(name="h_psum", bufs=H_BANKS))
         y_psum = ctx.enter_context(tc.psum_pool(name="y_psum", bufs=Y_BANKS))
+
+        def place(shape, dtype, name, kib):
+            return arena.tile(shape, dtype, name=name, align_bytes=64, offset=kib * KIB)
 
         offsets = keep.tile([P, S // ENTRIES_PER_COLUMN], U16, name="offsets")
         nc.sync.dma_start(offsets[:], offs)
@@ -55,12 +54,12 @@ def tile_list_choir_phase_retune_kernel(
         nc.gpsimd.memset(w4_sc[:].rearrange("p b c -> p (b c)").bitcast(I32), 0)
 
         def load_table_words(a):
-            words = keep.tile([P, T], I32, name="tab_w%d" % a, align_bytes=64)
+            words = place([P, T], I32, "tab_w%d" % a, 8 * a)
             nc.sync.dma_start(words[:], tab_words[a].rearrange("p e j -> p (e j)").bitcast(I32))
             return words
 
-        def load_weight(weight, rows, cols, name):
-            raw = wide.tile([P, PACK, PASS], F32, name=name, tag="wide")
+        def load_weight(weight, rows, cols, name, kib):
+            raw = place([P, PACK, PASS], F32, name, kib)
             block = weight[PASS * rows : PASS * (rows + 1), PASS * cols : PASS * (cols + 1)]
             nc.sync.dma_start(raw[:], block.rearrange("(p j) c -> p j c", j=PACK))
             return raw
@@ -70,17 +69,24 @@ def tile_list_choir_phase_retune_kernel(
             nc.sync.dma_start(tile[:], vec.rearrange("(b p t) -> p b t", b=PASSES, t=PACK))
             return tile
 
+        def load_phases(n):
+            tile = keep.tile([P, T], F32, name="phases%d" % n, align_bytes=64)
+            nc.sync.dma_start(tile[:], gT[P * n : P * (n + 1), :])
+            return tile
+
         tab_w = [load_table_words(0)]
         for quadrant in range(4):
             blocks = tab_scales[:, 4 * quadrant : 4 * quadrant + 4, :]
             nc.sync.dma_start(tab_sc[32 * quadrant : 32 * quadrant + 8, :].bitcast(I32), blocks.bitcast(I32))
+        w1_raw = {(a, 0): load_weight(w1, a, 0, "w1_raw%d0" % a, 16 + 8 * a) for a in range(PASSES)}
         tab_w.append(load_table_words(1))
-        w1_raw = {(a, 0): load_weight(w1, a, 0, "w1_raw%d0" % a) for a in range(PASSES)}
         bias_sb = load_channel_vector(bias, "bias_sb")
         for a in range(PASSES):
-            w1_raw[a, 1] = load_weight(w1, a, 1, "w1_raw%d1" % a)
+            w1_raw[a, 1] = load_weight(w1, a, 1, "w1_raw%d1" % a, 32 + 8 * a)
         amp_sb = {"sin": load_channel_vector(amps, "amps_sb"), "cos": load_channel_vector(ampc, "ampc_sb")}
-        w5_raw = [load_weight(w5, 0, 0, "w5_raw0")]
+        w5_raw = [load_weight(w5, b, 0, "w5_raw%d" % b, 48 + 8 * b) for b in range(PASSES)]
+        phases = [load_phases(0), load_phases(1)]
+        phases.extend([load_phases(2), load_phases(3)])
         for quadrant in range(4):
             nc.sync.dma_start(
                 w4_sc[32 * quadrant : 32 * quadrant + 4, :, :].bitcast(I32),
@@ -88,14 +94,12 @@ def tile_list_choir_phase_retune_kernel(
             )
         w4_w = keep.tile([P, PASSES, 2 * N], U8, name="w4_w", align_bytes=64)
         nc.sync.dma_start(w4_w[:].bitcast(I32), w4_words.rearrange("b p c -> p b c").bitcast(I32))
-        w5_raw.append(load_weight(w5, 1, 0, "w5_raw1"))
-        phases = []
-        for n in range(ROW_TILES):
-            phases.append(keep.tile([P, T], F32, name="phases%d" % n, align_bytes=64))
-            nc.sync.dma_start(phases[n][:], gT[P * n : P * (n + 1), :])
 
-        def quantise(values, columns, name):
-            codes = keep.tile([P, columns], U32, name=name + "_codes", align_bytes=64)
+        def quantise(values, columns, name, kib=None):
+            if kib is None:
+                codes = keep.tile([P, columns], U32, name=name + "_codes", align_bytes=64)
+            else:
+                codes = place([P, columns], U32, name + "_codes", kib)
             scales = keep.tile([P, columns], U8, name=name + "_scales", align_bytes=64)
             nc.vector.quantize_mx(out=codes[:].bitcast(FP8X4), scales=scales[:], in_=values)
             return codes, scales
@@ -103,15 +107,16 @@ def tile_list_choir_phase_retune_kernel(
         v_w = [keep.tile([P, S], U32, name="v_w%d" % a, align_bytes=64) for a in range(PASSES)]
         v_sc = keep.tile([P, S], U8, name="v_sc", align_bytes=64)
         nc.vector.tensor_copy(v_sc[:], tab_sc[:].indirect(offsets[:]))
-        for a in range(PASSES):
-            nc.vector.tensor_copy(v_w[a][:], tab_w[a][:].bitcast(U32).indirect(offsets[:]))
+        nc.vector.tensor_copy(v_w[0][:], tab_w[0][:].bitcast(U32).indirect(offsets[:]))
 
-        def places(cols):
-            return offsets[:, cols.start // ENTRIES_PER_COLUMN : cols.stop // ENTRIES_PER_COLUMN]
+        def entries(s):
+            return slice(WIDTH * s, WIDTH * (s + 1))
 
-        def quantise_w1(a, b, copies):
-            values = woven.tile([P, PACK, P, PACK], BF16, name="w1_woven", tag="woven", align_bytes=64)
-            cuts = (0, P) if len(copies) == 1 else (0, SCALAR_GROUPS, P)
+        def places(s):
+            return offsets[:, WIDTH * s // ENTRIES_PER_COLUMN : WIDTH * (s + 1) // ENTRIES_PER_COLUMN]
+
+        def quantise_w1(a, b, cuts, copies):
+            values = place([P, PACK, P, PACK], BF16, "w1_woven%d%d" % (a, b), 64 + 4 * a)
             for i, copy in enumerate(copies):
                 copy(
                     values[:, :, cuts[i] : cuts[i + 1], :].rearrange("p t m j -> p m t j"),
@@ -122,150 +127,174 @@ def tile_list_choir_phase_retune_kernel(
             return quantise(values[:].rearrange("p t m j -> p (t m j)"), PASS, "w1_%d%d" % (a, b))
 
         w1_q = {
-            (0, 0): quantise_w1(0, 0, [nc.scalar.copy]),
-            (1, 0): quantise_w1(1, 0, [nc.scalar.copy, nc.vector.tensor_copy]),
+            (0, 0): quantise_w1(0, 0, (0, 64, P), [nc.scalar.copy, nc.vector.tensor_copy]),
+            (1, 0): quantise_w1(1, 0, (0, 48, P), [nc.scalar.copy, nc.vector.tensor_copy]),
         }
+        nc.vector.tensor_copy(v_w[1][:, entries(0)], tab_w[1][:].bitcast(U32).indirect(places(0)))
+        nc.vector.tensor_copy(
+            v_w[1][:, WIDTH:], tab_w[1][:].bitcast(U32).indirect(offsets[:, WIDTH // ENTRIES_PER_COLUMN :])
+        )
         for a in range(PASSES):
-            w1_q[a, 1] = quantise_w1(a, 1, [nc.vector.tensor_copy])
+            w1_q[a, 1] = quantise_w1(a, 1, (0, P), [nc.vector.tensor_copy])
 
         def quantise_w5(b):
-            values = woven.tile([P, N, PACK], BF16, name="w5_woven", tag="woven", align_bytes=64)
+            values = place([P, N, PACK], BF16, "w5_woven%d" % b, 64 + 10 * b)
             nc.vector.tensor_copy(
                 values[:].rearrange("p (c i) j -> p c j i", i=2),
                 w5_raw[b][:].rearrange("p j (c i) -> p c j i", i=2),
             )
             return quantise(values[:].rearrange("p c j -> p (c j)"), N, "w5_%d" % b)
 
-        def entries(s):
-            first = sum(SLICES[:s])
-            return slice(first, first + SLICES[s])
+        def cos_place(s, b):
+            return 98 if s == 0 else 4 * (PASSES * (s - 1) + b)
+
+        def angles(s, b, target):
+            unit = PASSES * s + b
+            sines = place([P, PACK, WIDTH], F32, "sines%d" % unit, 80 + 4 * b)
+            folded = place([P, PACK, WIDTH], F32, "folded%d" % unit, 88 + 4 * b)
+            for pair in range(PACK // 2):
+                bank = h_psum.tile([P, 2, WIDTH], F32, name="h_bank")
+                for i in range(2):
+                    t = 2 * pair + i
+                    for a in range(PASSES):
+                        codes, scales = w1_q[a, b]
+                        nc.tensor.matmul_mx(
+                            out=bank[:, i, :],
+                            lhsT=codes[:, P * t : P * (t + 1)].bitcast(FP8X4),
+                            lhsT_scale=scales[:, P * t : P * (t + 1)],
+                            rhs=v_w[a][:, entries(s)].bitcast(FP8X4),
+                            rhs_scale=v_sc[4 * a : P, entries(s)],
+                            start=(a == 0),
+                            stop=(a == PASSES - 1),
+                        )
+                for i in range(2):
+                    t = 2 * pair + i
+                    bias_t = bias_sb[:, b, t : t + 1]
+                    nc.scalar.activation(sines[:, t, :], bank[:, i, :], ACT.Sin, bias=bias_t)
+                    nc.scalar.activation(folded[:, t, :], bank[:, i, :], ACT.Abs, bias=bias_t)
+            rounded = place([P, PACK, WIDTH], BF16, "rounded%d" % unit, 104 + 2 * b if s == 0 else 20 + 2 * unit)
+
+            def scale_sines():
+                for t in range(PACK):
+                    amp_t = amp_sb["sin"][:, b, t : t + 1]
+                    nc.scalar.activation(rounded[:, t, :], sines[:, t, :], ACT.Copy, scale=amp_t)
+
+            if unit < PASSES * SLICES - 1:
+                scale_sines()
+            if unit == 0:
+                nc.scalar.activation(folded[:], folded[:], ACT.Sin, bias=math.pi / 2, scale=-1.0)
+                nc.vector.tensor_copy(
+                    target[:, 0, :, :].rearrange("p (c i) t -> p c t i", i=2),
+                    rounded[:].rearrange("p t (c i) -> p c t i", i=2),
+                )
+                nc.vector.tensor_tensor(
+                    target[:, 1, :, :].rearrange("p (c i) t -> p c t i", i=2),
+                    folded[:].rearrange("p t (c i) -> p c t i", i=2),
+                    amp_sb["cos"][:, b, :].unsqueeze(1).unsqueeze(3).to_broadcast([P, WIDTH // 2, PACK, 2]),
+                    ALU.mult,
+                )
+                return
+            cosines = place([P, WIDTH, PACK], F32, "cosines%d" % unit, cos_place(s, b))
+            nc.scalar.activation(
+                cosines[:].rearrange("p (c i) t -> p c t i", i=2),
+                folded[:].rearrange("p t (c i) -> p c t i", i=2),
+                ACT.Sin, bias=math.pi / 2, scale=-1.0,
+            )
+            if unit < PASSES * SLICES - 1:
+                nc.gpsimd.tensor_scalar(
+                    target[:, 0, :, :], rounded[:].rearrange("p t c -> p c t"), 1.0, 1.0, ALU.mult, ALU.mult
+                )
+            else:
+                scale_sines()
+                nc.scalar.copy(
+                    target[:, 0, :, :].rearrange("p (c i) t -> p c t i", i=4),
+                    rounded[:].rearrange("p t (c i) -> p c t i", i=4),
+                )
+            nc.gpsimd.tensor_tensor(
+                target[:, 1, :, :], cosines[:],
+                amp_sb["cos"][:, b, :].unsqueeze(1).to_broadcast([P, WIDTH, PACK]), ALU.mult,
+            )
 
         h_q = {}
 
-        def angles(s, b):
-            width, cols = SLICES[s], entries(s)
-            trig = {
-                "sin": wide.tile([P, PACK, width], F32, name="sin_sb", tag="wide"),
-                "cos": wide.tile([P, PACK, width], F32, name="cos_sb", tag="wide"),
-            }
-            for t in range(PACK):
-                bank = h_psum.tile([P, BANK], F32, name="h_bank")
-                for a in range(PASSES):
-                    codes, scales = w1_q[a, b]
-                    nc.tensor.matmul_mx(
-                        out=bank[:, :width],
-                        lhsT=codes[:, P * t : P * (t + 1)].bitcast(FP8X4),
-                        lhsT_scale=scales[:, P * t : P * (t + 1)],
-                        rhs=v_w[a][:, cols].bitcast(FP8X4),
-                        rhs_scale=v_sc[4 * a : P, cols],
-                        start=(a == 0),
-                        stop=(a == PASSES - 1),
-                    )
-                bias_t = bias_sb[:, b, t : t + 1]
-                nc.scalar.activation(trig["sin"][:, t, :], bank[:, :width], ACT.Sin, bias=bias_t)
-                nc.scalar.activation(trig["cos"][:, t, :], bank[:, :width], ACT.Abs, bias=bias_t)
-            nc.scalar.activation(trig["cos"][:], trig["cos"][:], ACT.Sin, bias=math.pi / 2, scale=-1.0)
+        def products(s, n, bank):
+            for b in range(PASSES):
+                codes, scales, first = h_q[s, b]
+                hs_cols = slice(first, first + WIDTH)
+                hc_cols = slice(first + WIDTH, first + 2 * WIDTH)
+                nc.tensor.matmul_mx(
+                    out=bank,
+                    lhsT=w4_w[:, b, 2 * P * n : 2 * P * (n + 1)].bitcast(FP4X4),
+                    lhsT_scale=w4_sc[:, b, P * n : P * (n + 1)],
+                    rhs=codes[:, hs_cols].bitcast(FP8X4),
+                    rhs_scale=scales[:, hs_cols],
+                    start=(b == 0),
+                    stop=False,
+                )
+                nc.tensor.matmul_mx(
+                    out=bank,
+                    lhsT=w5_q[b][0][:, P * n : P * (n + 1)].bitcast(FP8X4),
+                    lhsT_scale=w5_q[b][1][:, P * n : P * (n + 1)],
+                    rhs=codes[:, hc_cols].bitcast(FP8X4),
+                    rhs_scale=scales[:, hc_cols],
+                    start=False,
+                    stop=(b == PASSES - 1),
+                )
 
-            if (s, b) in ((0, 1), (1, 0)):
-                values = stage.tile([P, 2, width, PACK], BF16, name="h_woven", tag="handover", align_bytes=64)
-            else:
-                values = woven.tile([P, 2, width, PACK], BF16, name="h_woven", tag="woven", align_bytes=64)
-            for half, kind in enumerate(("sin", "cos")):
-                target = values[:, half, :, :]
-                if kind == ("sin" if (s, b) == (1, 1) else "cos") and s > 0:
-                    if (s, b) == (1, 0):
-                        rounded = keep.tile([P, PACK, width], BF16, name="rounded%d%d" % (s, b), align_bytes=64)
-                    else:
-                        rounded = stage.tile([P, PACK, width], BF16, name="rounded", tag="stage", align_bytes=64)
-                    for t in range(PACK):
-                        amp_t = amp_sb[kind][:, b, t : t + 1]
-                        nc.scalar.activation(rounded[:, t, :], trig[kind][:, t, :], ACT.Copy, scale=amp_t)
-                    if (s, b) == (1, 0):
-                        for first in range(0, width, GPSIMD_COLUMNS):
-                            part = slice(first, first + GPSIMD_COLUMNS)
-                            nc.gpsimd.tensor_scalar(
-                                target[:, part, :], rounded[:, :, part].rearrange("p t c -> p c t"),
-                                1.0, 1.0, ALU.mult, ALU.mult,
-                            )
-                    else:
-                        nc.scalar.copy(
-                            target.rearrange("p (c i) t -> p c t i", i=4),
-                            rounded[:].rearrange("p t (c i) -> p c t i", i=4),
-                        )
-                else:
-                    amp = amp_sb[kind][:, b, :].unsqueeze(1).unsqueeze(3)
-                    engine, piece = (nc.gpsimd, GPSIMD_COLUMNS) if kind == "sin" and s > 0 else (nc.vector, width)
-                    for first in range(0, width, piece):
-                        engine.tensor_tensor(
-                            target[:, first : first + piece, :].rearrange("p (c i) t -> p c t i", i=2),
-                            trig[kind][:, :, first : first + piece].rearrange("p t (c i) -> p c t i", i=2),
-                            amp.to_broadcast([P, piece // 2, PACK, 2]),
-                            ALU.mult,
-                        )
-            h_q[s, b] = quantise(values[:].rearrange("p h c t -> p (h c t)"), 2 * width, "h%d%d" % (s, b))
+        def pair_of_products(s, half):
+            bank = y_psum.tile([P, 2, WIDTH], F32, name="y_bank")
+            for i in range(2):
+                products(s, 2 * half + i, bank[:, i, :])
+            return bank
 
-        def retune(s, n):
-            width, cols = SLICES[s], entries(s)
-            bank = y_psum.tile([P, BANK], F32, name="y_bank")
-            group = BANK if width == BANK else P
-            for first in range(0, width, group):
-                hs_cols = slice(first, first + group)
-                hc_cols = slice(width + first, width + first + group)
-                for b in range(PASSES):
-                    codes, scales = h_q[s, b]
-                    nc.tensor.matmul_mx(
-                        out=bank[:, hs_cols],
-                        lhsT=w4_w[:, b, 2 * P * n : 2 * P * (n + 1)].bitcast(FP4X4),
-                        lhsT_scale=w4_sc[:, b, P * n : P * (n + 1)],
-                        rhs=codes[:, hs_cols].bitcast(FP8X4),
-                        rhs_scale=scales[:, hs_cols],
-                        start=(b == 0),
-                        stop=False,
-                    )
-                    nc.tensor.matmul_mx(
-                        out=bank[:, hs_cols],
-                        lhsT=w5_q[b][0][:, P * n : P * (n + 1)].bitcast(FP8X4),
-                        lhsT_scale=w5_q[b][1][:, P * n : P * (n + 1)],
-                        rhs=codes[:, hc_cols].bitcast(FP8X4),
-                        rhs_scale=scales[:, hc_cols],
-                        start=False,
-                        stop=(b == PASSES - 1),
-                    )
-            if (s, n) == (last - 1, ROW_TILES - 2):
-                y_sb = stage.tile([P, width], F32, name="y_held", tag="stage", align_bytes=64)
-            else:
-                y_sb = sums.tile([P, width], F32, name="y_sb")
-            if s == 1 and n < 2:
-                nc.vector.tensor_tensor(y_sb[:], bank[:, :width], old[n][:, cols], ALU.add)
-                nc.vector.tensor_copy(phases[n][:].indirect(places(cols)), y_sb[:])
-            else:
-                nc.scalar.copy(y_sb[:], bank[:, :width])
-                nc.vector.tensor_tensor(phases[n][:].indirect(places(cols)), old[n][:, cols], y_sb[:], ALU.add)
+        def retune_pair(s, half, bank, kibs):
+            new = [place([P, WIDTH], F32, "new%d%d" % (s, 2 * half + i), kibs[i]) for i in range(2)]
+            for i in range(2):
+                nc.vector.tensor_tensor(new[i][:], bank[:, i, :], old[2 * half + i][:, entries(s)], ALU.add)
+            for i in range(2):
+                nc.vector.tensor_copy(phases[2 * half + i][:].indirect(places(s)), new[i][:])
+
+        def retune_fused(s, n, y_bank, kib):
+            y_sb = place([P, WIDTH], F32, "y_sb%d%d" % (s, n), kib)
+            nc.scalar.copy(y_sb[:], y_bank)
+            nc.vector.tensor_tensor(phases[n][:].indirect(places(s)), old[n][:, entries(s)], y_sb[:], ALU.add)
             if s == last:
                 for part in (slice(0, T // 2), slice(T // 2, T)):
                     nc.sync.dma_start(out[P * n : P * (n + 1), part], phases[n][:, part])
 
         w5_q = []
         for b in range(PASSES):
-            angles(0, b)
-            w5_q.append(quantise_w5(b))
+            if b == 1:
+                w5_q.extend([quantise_w5(0), quantise_w5(1)])
+            woven = place([P, 2, WIDTH, PACK], BF16, "h_woven0%d" % b, 108 if b == 0 else 72)
+            angles(0, b, woven)
+            h_q[0, b] = quantise(woven[:].rearrange("p h c t -> p (h c t)"), 2 * WIDTH, "h0%d" % b) + (0,)
 
-        old = [keep.tile([P, S], F32, name="old%d" % n) for n in range(ROW_TILES)]
+        old = [place([P, S], F32, "old0", 76), keep.tile([P, S], F32, name="old1")]
+        old.extend([place([P, S], F32, "old2", 96), place([P, S], F32, "old3", 100)])
         for n in range(ROW_TILES):
             nc.vector.tensor_copy(old[n][:], phases[n][:].indirect(offsets[:]))
 
-        angles(1, 0)
-        retune(0, 0)
-        retune(0, 1)
-        angles(1, 1)
-        retune(0, 2)
-        retune(0, 3)
-        angles(2, 0)
-        retune(1, 0)
-        retune(1, 1)
-        angles(2, 1)
-        retune(1, 2)
-        for n in range(ROW_TILES - 1):
-            retune(last, n)
-        retune(1, 3)
-        retune(last, ROW_TILES - 1)
+        held = None
+        for s in range(SLICES):
+            if s > 0:
+                woven = place([P, PASSES, 2, WIDTH, PACK], BF16, "h_woven%d" % s, 68)
+                for b in range(PASSES):
+                    angles(s, b, woven[:, b, :, :, :])
+                codes, scales = quantise(woven[:].rearrange("p b h c t -> p (b h c t)"), 4 * WIDTH, "h%d" % s, 36 + 4 * s)
+                for b in range(PASSES):
+                    h_q[s, b] = (codes, scales, 2 * WIDTH * b)
+            if s == last:
+                break
+            if s > 0:
+                retune_pair(s - 1, 1, held, (cos_place(s, 1), cos_place(s, 1) + 1))
+            retune_pair(s, 0, pair_of_products(s, 0), (40 + 4 * s, 52 + s))
+            held = pair_of_products(s, 1)
+
+        retune_fused(last - 1, 2, held[:, 0, :], cos_place(last, 1))
+        for n in range(ROW_TILES):
+            if n == ROW_TILES - 1:
+                retune_fused(last - 1, n, held[:, 1, :], 57)
+            bank = y_psum.tile([P, 2, WIDTH], F32, name="y_bank")
+            products(last, n, bank[:, 0, :])
+            retune_fused(last, n, bank[:, 0, :], 56 + n if n < ROW_TILES - 1 else 60)

@@ -69,6 +69,11 @@ def tile_list_choir_phase_retune_kernel(
             nc.sync.dma_start(tile[:], vec.rearrange("(b p t) -> p b t", b=PASSES, t=PACK))
             return tile
 
+        def load_pass_of_vector(vec, b, name):
+            tile = keep.tile([P, PACK], F32, name=name)
+            nc.sync.dma_start(tile[:], vec[PASS * b : PASS * (b + 1)].rearrange("(p t) -> p t", t=PACK))
+            return tile
+
         def load_phases(n):
             tile = keep.tile([P, T], F32, name="phases%d" % n, align_bytes=64)
             nc.sync.dma_start(tile[:], gT[P * n : P * (n + 1), :])
@@ -83,17 +88,19 @@ def tile_list_choir_phase_retune_kernel(
         bias_sb = load_channel_vector(bias, "bias_sb")
         for a in range(PASSES):
             w1_raw[a, 1] = load_weight(w1, a, 1, "w1_raw%d1" % a, 32 + 8 * a)
-        amp_sb = {"sin": load_channel_vector(amps, "amps_sb"), "cos": load_channel_vector(ampc, "ampc_sb")}
+        amp_sin = load_channel_vector(amps, "amps_sb")
+        amp_cos = [load_pass_of_vector(ampc, 0, "ampc_sb0")]
         w5_raw = [load_weight(w5, b, 0, "w5_raw%d" % b, 48 + 8 * b) for b in range(PASSES)]
         phases = [load_phases(0), load_phases(1)]
+        w4_w = keep.tile([P, PASSES, 2 * N], U8, name="w4_w", align_bytes=64)
+        nc.sync.dma_start(w4_w[:].bitcast(I32), w4_words.rearrange("b p c -> p b c").bitcast(I32))
+        amp_cos.append(load_pass_of_vector(ampc, 1, "ampc_sb1"))
         phases.extend([load_phases(2), load_phases(3)])
         for quadrant in range(4):
-            nc.sync.dma_start(
+            nc.gpsimd.dma_start(
                 w4_sc[32 * quadrant : 32 * quadrant + 4, :, :].bitcast(I32),
                 w4_scales[:, 4 * quadrant : 4 * quadrant + 4, :].rearrange("b q c -> q b c").bitcast(I32),
             )
-        w4_w = keep.tile([P, PASSES, 2 * N], U8, name="w4_w", align_bytes=64)
-        nc.sync.dma_start(w4_w[:].bitcast(I32), w4_words.rearrange("b p c -> p b c").bitcast(I32))
 
         def quantise(values, columns, name, kib=None):
             if kib is None:
@@ -127,8 +134,8 @@ def tile_list_choir_phase_retune_kernel(
             return quantise(values[:].rearrange("p t m j -> p (t m j)"), PASS, "w1_%d%d" % (a, b))
 
         w1_q = {
-            (0, 0): quantise_w1(0, 0, (0, 64, P), [nc.scalar.copy, nc.vector.tensor_copy]),
-            (1, 0): quantise_w1(1, 0, (0, 48, P), [nc.scalar.copy, nc.vector.tensor_copy]),
+            (0, 0): quantise_w1(0, 0, (0, 96, P), [nc.scalar.copy, nc.vector.tensor_copy]),
+            (1, 0): quantise_w1(1, 0, (0, 64, P), [nc.scalar.copy, nc.vector.tensor_copy]),
         }
         nc.vector.tensor_copy(v_w[1][:, entries(0)], tab_w[1][:].bitcast(U32).indirect(places(0)))
         nc.vector.tensor_copy(
@@ -176,22 +183,25 @@ def tile_list_choir_phase_retune_kernel(
 
             def scale_sines():
                 for t in range(PACK):
-                    amp_t = amp_sb["sin"][:, b, t : t + 1]
+                    amp_t = amp_sin[:, b, t : t + 1]
                     nc.scalar.activation(rounded[:, t, :], sines[:, t, :], ACT.Copy, scale=amp_t)
 
-            if unit < PASSES * SLICES - 1:
+            if 0 < unit < PASSES * SLICES - 1:
                 scale_sines()
             if unit == 0:
                 nc.scalar.activation(folded[:], folded[:], ACT.Sin, bias=math.pi / 2, scale=-1.0)
-                nc.vector.tensor_copy(
-                    target[:, 0, :, :].rearrange("p (c i) t -> p c t i", i=2),
-                    rounded[:].rearrange("p t (c i) -> p c t i", i=2),
+                rounded_cos = place([P, PACK, WIDTH], BF16, "rounded_cos", 112)
+                for t in range(PACK):
+                    amp_t = amp_cos[b][:, t : t + 1]
+                    nc.scalar.activation(rounded_cos[:, t, :], folded[:, t, :], ACT.Copy, scale=amp_t)
+                scale_sines()
+                nc.scalar.copy(
+                    target[:, 0, :, :].rearrange("p (c i) t -> p c t i", i=4),
+                    rounded[:].rearrange("p t (c i) -> p c t i", i=4),
                 )
-                nc.vector.tensor_tensor(
+                nc.vector.tensor_copy(
                     target[:, 1, :, :].rearrange("p (c i) t -> p c t i", i=2),
-                    folded[:].rearrange("p t (c i) -> p c t i", i=2),
-                    amp_sb["cos"][:, b, :].unsqueeze(1).unsqueeze(3).to_broadcast([P, WIDTH // 2, PACK, 2]),
-                    ALU.mult,
+                    rounded_cos[:].rearrange("p t (c i) -> p c t i", i=2),
                 )
                 return
             cosines = place([P, WIDTH, PACK], F32, "cosines%d" % unit, cos_place(s, b))
@@ -200,19 +210,21 @@ def tile_list_choir_phase_retune_kernel(
                 folded[:].rearrange("p t (c i) -> p c t i", i=2),
                 ACT.Sin, bias=math.pi / 2, scale=-1.0,
             )
-            if unit < PASSES * SLICES - 1:
-                nc.gpsimd.tensor_scalar(
-                    target[:, 0, :, :], rounded[:].rearrange("p t c -> p c t"), 1.0, 1.0, ALU.mult, ALU.mult
-                )
-            else:
+            if unit == PASSES * SLICES - 1:
                 scale_sines()
+            cut = {5: WIDTH // 2, 7: 0}.get(unit, WIDTH)
+            if cut > 0:
+                nc.gpsimd.tensor_scalar(
+                    target[:, 0, :cut, :], rounded[:, :, :cut].rearrange("p t c -> p c t"), 1.0, 1.0, ALU.mult, ALU.mult
+                )
+            if cut < WIDTH:
                 nc.scalar.copy(
-                    target[:, 0, :, :].rearrange("p (c i) t -> p c t i", i=4),
-                    rounded[:].rearrange("p t (c i) -> p c t i", i=4),
+                    target[:, 0, cut:, :].rearrange("p (c i) t -> p c t i", i=4),
+                    rounded[:, :, cut:].rearrange("p t (c i) -> p c t i", i=4),
                 )
             nc.gpsimd.tensor_tensor(
                 target[:, 1, :, :], cosines[:],
-                amp_sb["cos"][:, b, :].unsqueeze(1).to_broadcast([P, WIDTH, PACK]), ALU.mult,
+                amp_cos[b][:].unsqueeze(1).to_broadcast([P, WIDTH, PACK]), ALU.mult,
             )
 
         h_q = {}
@@ -268,7 +280,7 @@ def tile_list_choir_phase_retune_kernel(
                 w5_q.extend([quantise_w5(0), quantise_w5(1)])
             woven = place([P, 2, WIDTH, PACK], BF16, "h_woven0%d" % b, 108 if b == 0 else 72)
             angles(0, b, woven)
-            h_q[0, b] = quantise(woven[:].rearrange("p h c t -> p (h c t)"), 2 * WIDTH, "h0%d" % b) + (0,)
+            h_q[0, b] = quantise(woven[:].rearrange("p h c t -> p (h c t)"), 2 * WIDTH, "h0%d" % b, None if b else 54) + (0,)
 
         old = [place([P, S], F32, "old0", 76), keep.tile([P, S], F32, name="old1")]
         old.extend([place([P, S], F32, "old2", 96), place([P, S], F32, "old3", 100)])

@@ -122,6 +122,9 @@ def tile_list_choir_phase_retune_kernel(
         def places(s):
             return offsets[:, WIDTH * s // ENTRIES_PER_COLUMN : WIDTH * (s + 1) // ENTRIES_PER_COLUMN]
 
+        def gpsimd_copy(dst, src):
+            nc.gpsimd.tensor_scalar(dst, src, 1.0, 1.0, ALU.mult, ALU.mult)
+
         def quantise_w1(a, b, cuts, copies):
             values = place([P, PACK, P, PACK], BF16, "w1_woven%d%d" % (a, b), 64 + 4 * a)
             for i, copy in enumerate(copies):
@@ -134,8 +137,8 @@ def tile_list_choir_phase_retune_kernel(
             return quantise(values[:].rearrange("p t m j -> p (t m j)"), PASS, "w1_%d%d" % (a, b))
 
         w1_q = {
-            (0, 0): quantise_w1(0, 0, (0, 96, P), [nc.scalar.copy, nc.vector.tensor_copy]),
-            (1, 0): quantise_w1(1, 0, (0, 64, P), [nc.scalar.copy, nc.vector.tensor_copy]),
+            (0, 0): quantise_w1(0, 0, (0, 72, P), [nc.scalar.copy, gpsimd_copy]),
+            (1, 0): quantise_w1(1, 0, (0, 48, P), [nc.scalar.copy, nc.vector.tensor_copy]),
         }
         nc.vector.tensor_copy(v_w[1][:, entries(0)], tab_w[1][:].bitcast(U32).indirect(places(0)))
         nc.vector.tensor_copy(
@@ -186,22 +189,19 @@ def tile_list_choir_phase_retune_kernel(
                     amp_t = amp_sin[:, b, t : t + 1]
                     nc.scalar.activation(rounded[:, t, :], sines[:, t, :], ACT.Copy, scale=amp_t)
 
-            if 0 < unit < PASSES * SLICES - 1:
+            if unit < PASSES * SLICES - 1:
                 scale_sines()
             if unit == 0:
                 nc.scalar.activation(folded[:], folded[:], ACT.Sin, bias=math.pi / 2, scale=-1.0)
-                rounded_cos = place([P, PACK, WIDTH], BF16, "rounded_cos", 112)
-                for t in range(PACK):
-                    amp_t = amp_cos[b][:, t : t + 1]
-                    nc.scalar.activation(rounded_cos[:, t, :], folded[:, t, :], ACT.Copy, scale=amp_t)
-                scale_sines()
-                nc.scalar.copy(
-                    target[:, 0, :, :].rearrange("p (c i) t -> p c t i", i=4),
-                    rounded[:].rearrange("p t (c i) -> p c t i", i=4),
-                )
                 nc.vector.tensor_copy(
+                    target[:, 0, :, :].rearrange("p (c i) t -> p c t i", i=2),
+                    rounded[:].rearrange("p t (c i) -> p c t i", i=2),
+                )
+                nc.vector.tensor_tensor(
                     target[:, 1, :, :].rearrange("p (c i) t -> p c t i", i=2),
-                    rounded_cos[:].rearrange("p t (c i) -> p c t i", i=2),
+                    folded[:].rearrange("p t (c i) -> p c t i", i=2),
+                    amp_cos[b][:].unsqueeze(1).unsqueeze(3).to_broadcast([P, WIDTH // 2, PACK, 2]),
+                    ALU.mult,
                 )
                 return
             cosines = place([P, WIDTH, PACK], F32, "cosines%d" % unit, cos_place(s, b))

@@ -28,7 +28,6 @@ ENTRIES_PER_COLUMN = 16
 SLICES = 4
 WIDTH = S // SLICES
 KIB = 1024
-H_BANKS, Y_BANKS = 4, 4
 
 
 def tile_list_choir_phase_retune_kernel(
@@ -39,8 +38,10 @@ def tile_list_choir_phase_retune_kernel(
     with ExitStack() as ctx:
         keep = ctx.enter_context(tc.tile_pool(name="keep", bufs=1))
         arena = ctx.enter_context(tc.tile_pool(name="arena", bufs=1))
-        h_psum = ctx.enter_context(tc.psum_pool(name="h_psum", bufs=H_BANKS))
-        y_psum = ctx.enter_context(tc.psum_pool(name="y_psum", bufs=Y_BANKS))
+        psum = ctx.enter_context(tc.psum_pool(name="psum", bufs=1))
+
+        def psum_bank(name, index):
+            return psum.tile([P, 2, WIDTH], F32, name=name, offset=index * 2 * KIB)
 
         def place(shape, dtype, name, kib):
             return arena.tile(shape, dtype, name=name, align_bytes=64, offset=kib * KIB)
@@ -148,7 +149,7 @@ def tile_list_choir_phase_retune_kernel(
             w1_q[a, 1] = quantise_w1(a, 1, (0, P), [nc.vector.tensor_copy])
 
         def quantise_w5(b):
-            values = place([P, N, PACK], BF16, "w5_woven%d" % b, 64 + 10 * b)
+            values = place([P, N, PACK], BF16, "w5_woven%d" % b, 64 + 8 * b)
             nc.vector.tensor_copy(
                 values[:].rearrange("p (c i) j -> p c j i", i=2),
                 w5_raw[b][:].rearrange("p j (c i) -> p c j i", i=2),
@@ -162,10 +163,16 @@ def tile_list_choir_phase_retune_kernel(
             unit = PASSES * s + b
             sines = place([P, PACK, WIDTH], F32, "sines%d" % unit, 80 + 4 * b)
             folded = place([P, PACK, WIDTH], F32, "folded%d" % unit, 88 + 4 * b)
-            for pair in range(PACK // 2):
-                bank = h_psum.tile([P, 2, WIDTH], F32, name="h_bank")
-                for i in range(2):
-                    t = 2 * pair + i
+            group = 1 if unit == 0 else 2
+            for first in range(0, PACK, group):
+                index = 2 * b + first // 2
+                if unit == 0:
+                    index = 4 + first
+                elif index == 3 and s > 1:
+                    index = 6
+                bank = psum_bank("h_bank%d%d" % (unit, first), index)
+                for i in range(group):
+                    t = first + i
                     for a in range(PASSES):
                         codes, scales = w1_q[a, b]
                         nc.tensor.matmul_mx(
@@ -177,8 +184,8 @@ def tile_list_choir_phase_retune_kernel(
                             start=(a == 0),
                             stop=(a == PASSES - 1),
                         )
-                for i in range(2):
-                    t = 2 * pair + i
+                for i in range(group):
+                    t = first + i
                     bias_t = bias_sb[:, b, t : t + 1]
                     nc.scalar.activation(sines[:, t, :], bank[:, i, :], ACT.Sin, bias=bias_t)
                     nc.scalar.activation(folded[:, t, :], bank[:, i, :], ACT.Abs, bias=bias_t)
@@ -254,7 +261,7 @@ def tile_list_choir_phase_retune_kernel(
                 )
 
         def pair_of_products(s, half):
-            bank = y_psum.tile([P, 2, WIDTH], F32, name="y_bank")
+            bank = psum_bank("y_bank%d%d" % (s, half), ((4, 5), (3, 7))[s % 2][half])
             for i in range(2):
                 products(s, 2 * half + i, bank[:, i, :])
             return bank
@@ -280,9 +287,9 @@ def tile_list_choir_phase_retune_kernel(
                 w5_q.extend([quantise_w5(0), quantise_w5(1)])
             woven = place([P, 2, WIDTH, PACK], BF16, "h_woven0%d" % b, 108 if b == 0 else 72)
             angles(0, b, woven)
-            h_q[0, b] = quantise(woven[:].rearrange("p h c t -> p (h c t)"), 2 * WIDTH, "h0%d" % b, None if b else 54) + (0,)
+            h_q[0, b] = quantise(woven[:].rearrange("p h c t -> p (h c t)"), 2 * WIDTH, "h0%d" % b, None if b else 62) + (0,)
 
-        old = [place([P, S], F32, "old0", 76), keep.tile([P, S], F32, name="old1")]
+        old = [place([P, S], F32, "old0", 108), keep.tile([P, S], F32, name="old1")]
         old.extend([place([P, S], F32, "old2", 96), place([P, S], F32, "old3", 100)])
         for n in range(ROW_TILES):
             nc.vector.tensor_copy(old[n][:], phases[n][:].indirect(offsets[:]))
@@ -307,6 +314,6 @@ def tile_list_choir_phase_retune_kernel(
         for n in range(ROW_TILES):
             if n == ROW_TILES - 1:
                 retune_fused(last - 1, n, held[:, 1, :], 57)
-            bank = y_psum.tile([P, 2, WIDTH], F32, name="y_bank")
+            bank = psum_bank("y_last%d" % n, (3, 7, 0, 1)[n])
             products(last, n, bank[:, 0, :])
             retune_fused(last, n, bank[:, 0, :], 56 + n if n < ROW_TILES - 1 else 60)

@@ -123,30 +123,38 @@ def tile_list_choir_phase_retune_kernel(
         def places(s):
             return offsets[:, WIDTH * s // ENTRIES_PER_COLUMN : WIDTH * (s + 1) // ENTRIES_PER_COLUMN]
 
-        def gpsimd_copy(dst, src):
-            nc.gpsimd.tensor_scalar(dst, src, 1.0, 1.0, ALU.mult, ALU.mult)
+        def gpsimd_weave(dst, src):
+            nc.gpsimd.tensor_scalar(
+                dst.rearrange("p t m j -> p m t j"), src.rearrange("p j (m t) -> p m t j", t=PACK),
+                1.0, 1.0, ALU.mult, ALU.mult,
+            )
+
+        def paired_weave(copy):
+            return lambda dst, src: copy(
+                dst.rearrange("p (u i) m j -> p m u j i", i=2),
+                src.rearrange("p j (m u i) -> p m u j i", u=2, i=2),
+            )
+
+        scalar_weave, vector_weave = paired_weave(nc.scalar.copy), paired_weave(nc.vector.tensor_copy)
 
         def quantise_w1(a, b, cuts, copies):
             values = place([P, PACK, P, PACK], BF16, "w1_woven%d%d" % (a, b), 64 + 4 * a)
-            for i, copy in enumerate(copies):
-                copy(
-                    values[:, :, cuts[i] : cuts[i + 1], :].rearrange("p t m j -> p m t j"),
-                    w1_raw[a, b][:, :, PACK * cuts[i] : PACK * cuts[i + 1]].rearrange(
-                        "p j (m t) -> p m t j", t=PACK
-                    ),
-                )
+            for k, copy in enumerate(copies):
+                dst = values[:, :, cuts[k] : cuts[k + 1], :]
+                src = w1_raw[a, b][:, :, PACK * cuts[k] : PACK * cuts[k + 1]]
+                copy(dst, src)
             return quantise(values[:].rearrange("p t m j -> p (t m j)"), PASS, "w1_%d%d" % (a, b))
 
         w1_q = {
-            (0, 0): quantise_w1(0, 0, (0, 72, P), [nc.scalar.copy, gpsimd_copy]),
-            (1, 0): quantise_w1(1, 0, (0, 48, P), [nc.scalar.copy, nc.vector.tensor_copy]),
+            (0, 0): quantise_w1(0, 0, (0, 72, P), [scalar_weave, gpsimd_weave]),
+            (1, 0): quantise_w1(1, 0, (0, 48, P), [scalar_weave, vector_weave]),
         }
         nc.vector.tensor_copy(v_w[1][:, entries(0)], tab_w[1][:].bitcast(U32).indirect(places(0)))
         nc.vector.tensor_copy(
             v_w[1][:, WIDTH:], tab_w[1][:].bitcast(U32).indirect(offsets[:, WIDTH // ENTRIES_PER_COLUMN :])
         )
         for a in range(PASSES):
-            w1_q[a, 1] = quantise_w1(a, 1, (0, P), [nc.vector.tensor_copy])
+            w1_q[a, 1] = quantise_w1(a, 1, (0, P), [vector_weave])
 
         def quantise_w5(b):
             values = place([P, N, PACK], BF16, "w5_woven%d" % b, 64 + 8 * b)
@@ -201,8 +209,8 @@ def tile_list_choir_phase_retune_kernel(
             if unit == 0:
                 nc.scalar.activation(folded[:], folded[:], ACT.Sin, bias=math.pi / 2, scale=-1.0)
                 nc.vector.tensor_copy(
-                    target[:, 0, :, :].rearrange("p (c i) t -> p c t i", i=2),
-                    rounded[:].rearrange("p t (c i) -> p c t i", i=2),
+                    target[:, 0, :, :].rearrange("p (c i) t -> p c t i", i=4),
+                    rounded[:].rearrange("p t (c i) -> p c t i", i=4),
                 )
                 nc.vector.tensor_tensor(
                     target[:, 1, :, :].rearrange("p (c i) t -> p c t i", i=2),
@@ -260,9 +268,9 @@ def tile_list_choir_phase_retune_kernel(
                     stop=(b == PASSES - 1),
                 )
 
-        def pair_of_products(s, half):
+        def pair_of_products(s, half, count=2):
             bank = psum_bank("y_bank%d%d" % (s, half), ((4, 5), (3, 7))[s % 2][half])
-            for i in range(2):
+            for i in range(count):
                 products(s, 2 * half + i, bank[:, i, :])
             return bank
 
@@ -308,9 +316,11 @@ def tile_list_choir_phase_retune_kernel(
             if s > 0:
                 retune_pair(s - 1, 1, held, (cos_place(s, 1), cos_place(s, 1) + 1))
             retune_pair(s, 0, pair_of_products(s, 0), (40 + 4 * s, 52 + s))
-            held = pair_of_products(s, 1)
+            held = pair_of_products(s, 1, 2 if s < last - 1 else 1)
 
         retune_fused(last - 1, 2, held[:, 0, :], cos_place(last, 1))
+        held = psum_bank("y_held", 5)
+        products(last - 1, ROW_TILES - 1, held[:, 1, :])
         for n in range(ROW_TILES):
             if n == ROW_TILES - 1:
                 retune_fused(last - 1, n, held[:, 1, :], 57)

@@ -103,13 +103,19 @@ def tile_list_choir_phase_retune_kernel(
                 w4_scales[:, 4 * quadrant : 4 * quadrant + 4, :].rearrange("b q c -> q b c").bitcast(I32),
             )
 
-        def quantise(values, columns, name, kib=None):
+        def quantise(values, columns, name, kib=None, parts=1):
             if kib is None:
                 codes = keep.tile([P, columns], U32, name=name + "_codes", align_bytes=64)
             else:
                 codes = place([P, columns], U32, name + "_codes", kib)
             scales = keep.tile([P, columns], U8, name=name + "_scales", align_bytes=64)
-            nc.vector.quantize_mx(out=codes[:].bitcast(FP8X4), scales=scales[:], in_=values)
+            step = columns // parts
+            for first in range(0, columns, step):
+                cols = slice(first, first + step)
+                nc.vector.quantize_mx(
+                    out=codes[:, cols].bitcast(FP8X4), scales=scales[:, cols],
+                    in_=values[:, PACK * first : PACK * (first + step)],
+                )
             return codes, scales
 
         v_w = [keep.tile([P, S], U32, name="v_w%d" % a, align_bytes=64) for a in range(PASSES)]
@@ -153,16 +159,26 @@ def tile_list_choir_phase_retune_kernel(
         nc.vector.tensor_copy(
             v_w[1][:, WIDTH:], tab_w[1][:].bitcast(U32).indirect(offsets[:, WIDTH // ENTRIES_PER_COLUMN :])
         )
+        def quantise_w1_in_halves(a, b):
+            values = place([P, PACK, P, PACK], BF16, "w1_woven%d%d" % (a, b), 64 + 4 * a)
+            src = w1_raw[a, b][:].rearrange("p j (m u i) -> p u m j i", u=2, i=2)
+            for u in range(2):
+                nc.vector.tensor_copy(values[:, 2 * u : 2 * u + 2, :, :].rearrange("p i m j -> p m j i"), src[:, u, :, :, :])
+            return quantise(values[:].rearrange("p t m j -> p (t m j)"), PASS, "w1_%d%d" % (a, b), None, 2)
+
         for a in range(PASSES):
-            w1_q[a, 1] = quantise_w1(a, 1, (0, P), [vector_weave])
+            w1_q[a, 1] = quantise_w1_in_halves(a, 1)
 
         def quantise_w5(b):
             values = place([P, N, PACK], BF16, "w5_woven%d" % b, 64 + 8 * b)
-            nc.vector.tensor_copy(
-                values[:].rearrange("p (c i) j -> p c j i", i=2),
-                w5_raw[b][:].rearrange("p j (c i) -> p c j i", i=2),
-            )
-            return quantise(values[:].rearrange("p c j -> p (c j)"), N, "w5_%d" % b)
+            parts = 2 if b == 0 else 1
+            for first in range(0, N, N // parts):
+                cols = slice(first, first + N // parts)
+                nc.vector.tensor_copy(
+                    values[:, cols, :].rearrange("p (c i) j -> p c j i", i=2),
+                    w5_raw[b][:, :, cols].rearrange("p j (c i) -> p c j i", i=2),
+                )
+            return quantise(values[:].rearrange("p c j -> p (c j)"), N, "w5_%d" % b, None, parts)
 
         def cos_place(s, b):
             return 98 if s == 0 else 4 * (PASSES * (s - 1) + b)
@@ -286,8 +302,7 @@ def tile_list_choir_phase_retune_kernel(
             nc.scalar.copy(y_sb[:], y_bank)
             nc.vector.tensor_tensor(phases[n][:].indirect(places(s)), old[n][:, entries(s)], y_sb[:], ALU.add)
             if s == last:
-                for part in (slice(0, T // 2), slice(T // 2, T)):
-                    nc.sync.dma_start(out[P * n : P * (n + 1), part], phases[n][:, part])
+                nc.sync.dma_start(out[P * n : P * (n + 1), :], phases[n][:])
 
         w5_q = []
         for b in range(PASSES):
@@ -321,9 +336,17 @@ def tile_list_choir_phase_retune_kernel(
         retune_fused(last - 1, 2, held[:, 0, :], cos_place(last, 1))
         held = psum_bank("y_held", 5)
         products(last - 1, ROW_TILES - 1, held[:, 1, :])
-        for n in range(ROW_TILES):
-            if n == ROW_TILES - 1:
-                retune_fused(last - 1, n, held[:, 1, :], 57)
-            bank = psum_bank("y_last%d" % n, (3, 7, 0, 1)[n])
+        for n in range(ROW_TILES - 1):
+            bank = psum_bank("y_last%d" % n, (3, 7, 0)[n])
             products(last, n, bank[:, 0, :])
-            retune_fused(last, n, bank[:, 0, :], 56 + n if n < ROW_TILES - 1 else 60)
+            retune_fused(last, n, bank[:, 0, :], 56 + n)
+        n = ROW_TILES - 1
+        y_sb = place([P, 2 * WIDTH], F32, "y_sb_last", 60)
+        nc.scalar.copy(y_sb[:, :WIDTH], held[:, 1, :])
+        bank = psum_bank("y_last%d" % n, 1)
+        products(last, n, bank[:, 0, :])
+        nc.scalar.copy(y_sb[:, WIDTH:], bank[:, 0, :])
+        nc.vector.tensor_tensor(
+            phases[n][:].indirect(offsets[:, 2 * WIDTH // ENTRIES_PER_COLUMN :]), old[n][:, 2 * WIDTH :], y_sb[:], ALU.add
+        )
+        nc.sync.dma_start(out[P * n : P * (n + 1), :], phases[n][:])

@@ -44,7 +44,7 @@ def tile_list_choir_phase_retune_kernel(
             return psum.tile([P, 2, WIDTH], F32, name=name, offset=index * 2 * KIB)
 
         def place(shape, dtype, name, kib):
-            return arena.tile(shape, dtype, name=name, align_bytes=64, offset=kib * KIB)
+            return arena.tile(shape, dtype, name=name, align_bytes=64, offset=int(kib * KIB))
 
         offsets = keep.tile([P, S // ENTRIES_PER_COLUMN], U16, name="offsets")
         nc.sync.dma_start(offsets[:], offs)
@@ -93,10 +93,10 @@ def tile_list_choir_phase_retune_kernel(
         amp_cos = [load_pass_of_vector(ampc, 0, "ampc_sb0")]
         w5_raw = [load_weight(w5, b, 0, "w5_raw%d" % b, 48 + 8 * b) for b in range(PASSES)]
         phases = [load_phases(0), load_phases(1)]
-        w4_w = keep.tile([P, PASSES, 2 * N], U8, name="w4_w", align_bytes=64)
-        nc.sync.dma_start(w4_w[:].bitcast(I32), w4_words.rearrange("b p c -> p b c").bitcast(I32))
         amp_cos.append(load_pass_of_vector(ampc, 1, "ampc_sb1"))
         phases.extend([load_phases(2), load_phases(3)])
+        w4_w = keep.tile([P, PASSES, 2 * N], U8, name="w4_w", align_bytes=64)
+        nc.sync.dma_start(w4_w[:].bitcast(I32), w4_words.rearrange("b p c -> p b c").bitcast(I32))
         for quadrant in range(4):
             nc.gpsimd.dma_start(
                 w4_sc[32 * quadrant : 32 * quadrant + 4, :, :].bitcast(I32),
@@ -118,16 +118,16 @@ def tile_list_choir_phase_retune_kernel(
                 )
             return codes, scales
 
+        def entries(s, count=1):
+            return slice(WIDTH * s, WIDTH * (s + count))
+
+        def places(s, count=1):
+            return offsets[:, WIDTH * s // ENTRIES_PER_COLUMN : WIDTH * (s + count) // ENTRIES_PER_COLUMN]
+
         v_w = [keep.tile([P, S], U32, name="v_w%d" % a, align_bytes=64) for a in range(PASSES)]
         v_sc = keep.tile([P, S], U8, name="v_sc", align_bytes=64)
         nc.vector.tensor_copy(v_sc[:], tab_sc[:].indirect(offsets[:]))
         nc.vector.tensor_copy(v_w[0][:], tab_w[0][:].bitcast(U32).indirect(offsets[:]))
-
-        def entries(s):
-            return slice(WIDTH * s, WIDTH * (s + 1))
-
-        def places(s):
-            return offsets[:, WIDTH * s // ENTRIES_PER_COLUMN : WIDTH * (s + 1) // ENTRIES_PER_COLUMN]
 
         def gpsimd_weave(dst, src):
             nc.gpsimd.tensor_scalar(
@@ -143,22 +143,12 @@ def tile_list_choir_phase_retune_kernel(
 
         scalar_weave, vector_weave = paired_weave(nc.scalar.copy), paired_weave(nc.vector.tensor_copy)
 
-        def quantise_w1(a, b, cuts, copies):
+        def quantise_w1_shared(a, b, cut, copies):
             values = place([P, PACK, P, PACK], BF16, "w1_woven%d%d" % (a, b), 64 + 4 * a)
-            for k, copy in enumerate(copies):
-                dst = values[:, :, cuts[k] : cuts[k + 1], :]
-                src = w1_raw[a, b][:, :, PACK * cuts[k] : PACK * cuts[k + 1]]
-                copy(dst, src)
+            for first, end, copy in ((0, cut, copies[0]), (cut, P, copies[1])):
+                copy(values[:, :, first:end, :], w1_raw[a, b][:, :, PACK * first : PACK * end])
             return quantise(values[:].rearrange("p t m j -> p (t m j)"), PASS, "w1_%d%d" % (a, b))
 
-        w1_q = {
-            (0, 0): quantise_w1(0, 0, (0, 72, P), [scalar_weave, gpsimd_weave]),
-            (1, 0): quantise_w1(1, 0, (0, 48, P), [scalar_weave, vector_weave]),
-        }
-        nc.vector.tensor_copy(v_w[1][:, entries(0)], tab_w[1][:].bitcast(U32).indirect(places(0)))
-        nc.vector.tensor_copy(
-            v_w[1][:, WIDTH:], tab_w[1][:].bitcast(U32).indirect(offsets[:, WIDTH // ENTRIES_PER_COLUMN :])
-        )
         def quantise_w1_in_halves(a, b):
             values = place([P, PACK, P, PACK], BF16, "w1_woven%d%d" % (a, b), 64 + 4 * a)
             src = w1_raw[a, b][:].rearrange("p j (m u i) -> p u m j i", u=2, i=2)
@@ -166,38 +156,41 @@ def tile_list_choir_phase_retune_kernel(
                 nc.vector.tensor_copy(values[:, 2 * u : 2 * u + 2, :, :].rearrange("p i m j -> p m j i"), src[:, u, :, :, :])
             return quantise(values[:].rearrange("p t m j -> p (t m j)"), PASS, "w1_%d%d" % (a, b), None, 2)
 
+        def quantise_w5(b, kibs):
+            codes = keep.tile([P, N], U32, name="w5_%d_codes" % b, align_bytes=64)
+            scales = keep.tile([P, N], U8, name="w5_%d_scales" % b, align_bytes=64)
+            halves = []
+            for half, kib in enumerate(kibs):
+                cols = slice(N // 2 * half, N // 2 * (half + 1))
+                values = place([P, N // 2, PACK], BF16, "w5_woven%d%d" % (b, half), kib)
+                nc.vector.tensor_copy(
+                    values[:].rearrange("p (c i) j -> p c j i", i=2),
+                    w5_raw[b][:, :, cols].rearrange("p j (c i) -> p c j i", i=2),
+                )
+                halves.append((cols, values))
+            for cols, values in halves:
+                nc.vector.quantize_mx(
+                    out=codes[:, cols].bitcast(FP8X4), scales=scales[:, cols], in_=values[:].rearrange("p c j -> p (c j)")
+                )
+            return codes, scales
+
+        w1_q = {
+            (0, 0): quantise_w1_shared(0, 0, 72, [scalar_weave, gpsimd_weave]),
+            (1, 0): quantise_w1_shared(1, 0, 48, [scalar_weave, vector_weave]),
+        }
+        nc.vector.tensor_copy(v_w[1][:, entries(0)], tab_w[1][:].bitcast(U32).indirect(places(0)))
+        nc.vector.tensor_copy(v_w[1][:, entries(1, last)], tab_w[1][:].bitcast(U32).indirect(places(1, last)))
         for a in range(PASSES):
             w1_q[a, 1] = quantise_w1_in_halves(a, 1)
 
-        def quantise_w5(b):
-            values = place([P, N, PACK], BF16, "w5_woven%d" % b, 64 + 8 * b)
-            parts = 2 if b == 0 else 1
-            for first in range(0, N, N // parts):
-                cols = slice(first, first + N // parts)
-                nc.vector.tensor_copy(
-                    values[:, cols, :].rearrange("p (c i) j -> p c j i", i=2),
-                    w5_raw[b][:, :, cols].rearrange("p j (c i) -> p c j i", i=2),
-                )
-            return quantise(values[:].rearrange("p c j -> p (c j)"), N, "w5_%d" % b, None, parts)
-
-        def cos_place(s, b):
-            return 98 if s == 0 else 4 * (PASSES * (s - 1) + b)
-
-        def angles(s, b, target):
-            unit = PASSES * s + b
-            sines = place([P, PACK, WIDTH], F32, "sines%d" % unit, 80 + 4 * b)
-            folded = place([P, PACK, WIDTH], F32, "folded%d" % unit, 88 + 4 * b)
-            group = 1 if unit == 0 else 2
-            for first in range(0, PACK, group):
-                index = 2 * b + first // 2
-                if unit == 0:
-                    index = 4 + first
-                elif index == 3 and s > 1:
-                    index = 6
-                bank = psum_bank("h_bank%d%d" % (unit, first), index)
+        def angle_products(s, b, banks, order=(0, 1)):
+            group = PACK // len(banks)
+            tiles = []
+            for k, index in enumerate(banks):
+                bank = psum_bank("h_bank%d%d%d" % (s, b, k), index)
                 for i in range(group):
-                    t = first + i
-                    for a in range(PASSES):
+                    t = group * k + i
+                    for a in order:
                         codes, scales = w1_q[a, b]
                         nc.tensor.matmul_mx(
                             out=bank[:, i, :],
@@ -205,45 +198,46 @@ def tile_list_choir_phase_retune_kernel(
                             lhsT_scale=scales[:, P * t : P * (t + 1)],
                             rhs=v_w[a][:, entries(s)].bitcast(FP8X4),
                             rhs_scale=v_sc[4 * a : P, entries(s)],
-                            start=(a == 0),
-                            stop=(a == PASSES - 1),
+                            start=(a == order[0]),
+                            stop=(a == order[-1]),
                         )
-                for i in range(group):
-                    t = first + i
-                    bias_t = bias_sb[:, b, t : t + 1]
-                    nc.scalar.activation(sines[:, t, :], bank[:, i, :], ACT.Sin, bias=bias_t)
-                    nc.scalar.activation(folded[:, t, :], bank[:, i, :], ACT.Abs, bias=bias_t)
-            rounded = place([P, PACK, WIDTH], BF16, "rounded%d" % unit, 104 + 2 * b if s == 0 else 20 + 2 * unit)
+                    tiles.append(bank[:, i, :])
+            return tiles
 
-            def scale_sines():
-                for t in range(PACK):
-                    amp_t = amp_sin[:, b, t : t + 1]
-                    nc.scalar.activation(rounded[:, t, :], sines[:, t, :], ACT.Copy, scale=amp_t)
+        def read_angles(s, b, tiles, kibs, sines_first=False):
+            sines = place([P, PACK, WIDTH], F32, "sines%d%d" % (s, b), kibs[0])
+            folded = place([P, PACK, WIDTH], F32, "folded%d%d" % (s, b), kibs[1])
+            for t in range(PACK):
+                bias_t = bias_sb[:, b, t : t + 1]
+                steps = [(folded, ACT.Abs), (sines, ACT.Sin)]
+                for tile, func in reversed(steps) if sines_first else steps:
+                    nc.scalar.activation(tile[:, t, :], tiles[t], func, bias=bias_t)
+            return sines, folded
 
-            if unit < PASSES * SLICES - 1:
-                scale_sines()
-            if unit == 0:
-                nc.scalar.activation(folded[:], folded[:], ACT.Sin, bias=math.pi / 2, scale=-1.0)
-                nc.vector.tensor_copy(
-                    target[:, 0, :, :].rearrange("p (c i) t -> p c t i", i=4),
-                    rounded[:].rearrange("p t (c i) -> p c t i", i=4),
-                )
-                nc.vector.tensor_tensor(
-                    target[:, 1, :, :].rearrange("p (c i) t -> p c t i", i=2),
-                    folded[:].rearrange("p t (c i) -> p c t i", i=2),
-                    amp_cos[b][:].unsqueeze(1).unsqueeze(3).to_broadcast([P, WIDTH // 2, PACK, 2]),
-                    ALU.mult,
-                )
-                return
-            cosines = place([P, WIDTH, PACK], F32, "cosines%d" % unit, cos_place(s, b))
+        def vector_scale(dst, src, amp):
+            nc.vector.tensor_tensor(
+                dst.rearrange("p (c i) t -> p c t i", i=2),
+                src.rearrange("p t (c i) -> p c t i", i=2),
+                amp.unsqueeze(1).unsqueeze(3).to_broadcast([P, WIDTH // 2, PACK, 2]),
+                ALU.mult,
+            )
+
+        def scale_sines(s, b, sines, kib):
+            rounded = place([P, PACK, WIDTH], BF16, "rounded%d%d" % (s, b), kib)
+            for t in range(PACK):
+                nc.scalar.activation(rounded[:, t, :], sines[:, t, :], ACT.Copy, scale=amp_sin[:, b, t : t + 1])
+            return rounded
+
+        def woven_cosines(s, b, folded, kib):
+            cosines = place([P, WIDTH, PACK], F32, "cosines%d%d" % (s, b), kib)
             nc.scalar.activation(
                 cosines[:].rearrange("p (c i) t -> p c t i", i=2),
                 folded[:].rearrange("p t (c i) -> p c t i", i=2),
                 ACT.Sin, bias=math.pi / 2, scale=-1.0,
             )
-            if unit == PASSES * SLICES - 1:
-                scale_sines()
-            cut = {5: WIDTH // 2, 7: 0}.get(unit, WIDTH)
+            return cosines
+
+        def weave(b, rounded, cosines, target, cut=WIDTH):
             if cut > 0:
                 nc.gpsimd.tensor_scalar(
                     target[:, 0, :cut, :], rounded[:, :, :cut].rearrange("p t c -> p c t"), 1.0, 1.0, ALU.mult, ALU.mult
@@ -260,93 +254,110 @@ def tile_list_choir_phase_retune_kernel(
 
         h_q = {}
 
-        def products(s, n, bank):
+        def quantise_slice(s, woven):
+            codes, scales = quantise(woven[:].rearrange("p b h c t -> p (b h c t)"), 4 * WIDTH, "h%d" % s, 36 + 4 * s)
             for b in range(PASSES):
-                codes, scales, first = h_q[s, b]
-                hs_cols = slice(first, first + WIDTH)
-                hc_cols = slice(first + WIDTH, first + 2 * WIDTH)
-                nc.tensor.matmul_mx(
-                    out=bank,
-                    lhsT=w4_w[:, b, 2 * P * n : 2 * P * (n + 1)].bitcast(FP4X4),
-                    lhsT_scale=w4_sc[:, b, P * n : P * (n + 1)],
-                    rhs=codes[:, hs_cols].bitcast(FP8X4),
-                    rhs_scale=scales[:, hs_cols],
-                    start=(b == 0),
-                    stop=False,
-                )
-                nc.tensor.matmul_mx(
-                    out=bank,
-                    lhsT=w5_q[b][0][:, P * n : P * (n + 1)].bitcast(FP8X4),
-                    lhsT_scale=w5_q[b][1][:, P * n : P * (n + 1)],
-                    rhs=codes[:, hc_cols].bitcast(FP8X4),
-                    rhs_scale=scales[:, hc_cols],
-                    start=False,
-                    stop=(b == PASSES - 1),
-                )
+                h_q[s, b] = (codes, scales, 2 * WIDTH * b)
 
-        def pair_of_products(s, half, count=2):
-            bank = psum_bank("y_bank%d%d" % (s, half), ((4, 5), (3, 7))[s % 2][half])
-            for i in range(count):
-                products(s, 2 * half + i, bank[:, i, :])
-            return bank
+        def product_pass(s, n, sums, step):
+            b, half = divmod(step, 2)
+            codes, scales, first = h_q[s, b]
+            cols = slice(first + WIDTH * half, first + WIDTH * (half + 1))
+            if half == 0:
+                words, planes = w4_w[:, b, 2 * P * n : 2 * P * (n + 1)].bitcast(FP4X4), w4_sc[:, b, P * n : P * (n + 1)]
+            else:
+                words, planes = w5_q[b][0][:, P * n : P * (n + 1)].bitcast(FP8X4), w5_q[b][1][:, P * n : P * (n + 1)]
+            nc.tensor.matmul_mx(
+                out=sums, lhsT=words, lhsT_scale=planes, rhs=codes[:, cols].bitcast(FP8X4), rhs_scale=scales[:, cols],
+                start=(step == 0), stop=(step == 2 * PASSES - 1),
+            )
 
-        def retune_pair(s, half, bank, kibs):
+        def products(s, n, sums):
+            for step in range(2 * PASSES):
+                product_pass(s, n, sums, step)
+            return sums
+
+        def pair_of_products(s, half, index):
+            bank = psum_bank("y_bank%d%d" % (s, half), index)
+            return [products(s, 2 * half + i, bank[:, i, :]) for i in range(2)]
+
+        def retune_pair(s, half, sums, kibs):
             new = [place([P, WIDTH], F32, "new%d%d" % (s, 2 * half + i), kibs[i]) for i in range(2)]
             for i in range(2):
-                nc.vector.tensor_tensor(new[i][:], bank[:, i, :], old[2 * half + i][:, entries(s)], ALU.add)
+                nc.vector.tensor_tensor(new[i][:], sums[i], old[2 * half + i][:, entries(s)], ALU.add)
             for i in range(2):
                 nc.vector.tensor_copy(phases[2 * half + i][:].indirect(places(s)), new[i][:])
 
-        def retune_fused(s, n, y_bank, kib):
-            y_sb = place([P, WIDTH], F32, "y_sb%d%d" % (s, n), kib)
-            nc.scalar.copy(y_sb[:], y_bank)
-            nc.vector.tensor_tensor(phases[n][:].indirect(places(s)), old[n][:, entries(s)], y_sb[:], ALU.add)
-            if s == last:
-                nc.sync.dma_start(out[P * n : P * (n + 1), :], phases[n][:])
+        def scatter_sum(s, n, y_sb, count=1):
+            nc.vector.tensor_tensor(phases[n][:].indirect(places(s, count)), old[n][:, entries(s, count)], y_sb, ALU.add)
 
-        w5_q = []
-        for b in range(PASSES):
-            if b == 1:
-                w5_q.extend([quantise_w5(0), quantise_w5(1)])
-            woven = place([P, 2, WIDTH, PACK], BF16, "h_woven0%d" % b, 108 if b == 0 else 72)
-            angles(0, b, woven)
-            h_q[0, b] = quantise(woven[:].rearrange("p h c t -> p (h c t)"), 2 * WIDTH, "h0%d" % b, None if b else 62) + (0,)
+        def gather_phases(tile, n):
+            nc.vector.tensor_copy(tile[:], phases[n][:].indirect(offsets[:]))
+            return tile
 
-        old = [place([P, S], F32, "old0", 108), keep.tile([P, S], F32, name="old1")]
-        old.extend([place([P, S], F32, "old2", 96), place([P, S], F32, "old3", 100)])
-        for n in range(ROW_TILES):
-            nc.vector.tensor_copy(old[n][:], phases[n][:].indirect(offsets[:]))
-
-        held = None
-        for s in range(SLICES):
-            if s > 0:
-                woven = place([P, PASSES, 2, WIDTH, PACK], BF16, "h_woven%d" % s, 68)
-                for b in range(PASSES):
-                    angles(s, b, woven[:, b, :, :, :])
-                codes, scales = quantise(woven[:].rearrange("p b h c t -> p (b h c t)"), 4 * WIDTH, "h%d" % s, 36 + 4 * s)
-                for b in range(PASSES):
-                    h_q[s, b] = (codes, scales, 2 * WIDTH * b)
-            if s == last:
-                break
-            if s > 0:
-                retune_pair(s - 1, 1, held, (cos_place(s, 1), cos_place(s, 1) + 1))
-            retune_pair(s, 0, pair_of_products(s, 0), (40 + 4 * s, 52 + s))
-            held = pair_of_products(s, 1, 2 if s < last - 1 else 1)
-
-        retune_fused(last - 1, 2, held[:, 0, :], cos_place(last, 1))
-        held = psum_bank("y_held", 5)
-        products(last - 1, ROW_TILES - 1, held[:, 1, :])
+        EVEN, ODD = (84, 88), (130, 134)
+        woven = place([P, 2, WIDTH, PACK], BF16, "h_woven00", 40)
+        sines, folded = read_angles(0, 0, angle_products(0, 0, (4, 5, 6, 7)), (76, 80))
+        nc.scalar.activation(folded[:], folded[:], ACT.Sin, bias=math.pi / 2, scale=-1.0)
+        vector_scale(woven[:, 0, :, :], sines[:], amp_sin[:, 0, :])
+        vector_scale(woven[:, 1, :, :], folded[:], amp_cos[0][:])
+        read = {(1, 0): read_angles(1, 0, angle_products(1, 0, (0, 1)), EVEN)}
+        w5_q = [quantise_w5(0, (64, 66))]
+        h_q[0, 0] = quantise(woven[:].rearrange("p h c t -> p (h c t)"), 2 * WIDTH, "h00", 54) + (0,)
+        w5_q.append(quantise_w5(1, (124, 72)))
+        old = [gather_phases(place([P, S], F32, "old0", 124), 0), gather_phases(keep.tile([P, S], F32, name="old1"), 1)]
+        woven = place([P, 2, WIDTH, PACK], BF16, "h_woven01", 72)
+        sines, folded = read_angles(0, 1, angle_products(0, 1, (2, 3)), (96, 103))
+        weave(1, scale_sines(0, 1, sines, 114), woven_cosines(0, 1, folded, 118), woven)
+        h_q[0, 1] = quantise(woven[:].rearrange("p h c t -> p (h c t)"), 2 * WIDTH, "h01") + (0,)
+        old.append(gather_phases(place([P, S], F32, "old2", 116), 2))
+        old.append(gather_phases(place([P, S], F32, "old3", 120), 3))
+        read[1, 1] = read_angles(1, 1, angle_products(1, 1, (0, 1), (1, 0)), (93, 103), True)
+        tiles = {(2, 0): angle_products(2, 0, (2, 3)), (3, 0): angle_products(3, 0, (0, 1))}
+        woven = place([P, PASSES, 2, WIDTH, PACK], BF16, "h_woven1", 68)
+        weave(0, scale_sines(1, 0, read[1, 0][0], 97), woven_cosines(1, 0, read[1, 0][1], 99), woven[:, 0])
+        weave(1, scale_sines(1, 1, read[1, 1][0], 24), woven_cosines(1, 1, read[1, 1][1], 0), woven[:, 1])
+        sums = [psum_bank("y_first%d" % i, 4 + 2 * i)[:, 0, :] for i in range(2)]
+        for step in range(2 * PASSES):
+            for i in range(2):
+                product_pass(0, i, sums[i], step)
+        held = pair_of_products(0, 1, 5)
+        retune_pair(0, 0, sums, (40, 52))
+        quantise_slice(1, woven)
+        retune_pair(0, 1, held, (0, 1))
+        woven = place([P, PASSES, 2, WIDTH, PACK], BF16, "h_woven2", 68)
+        sines, folded = read_angles(2, 0, tiles[2, 0], EVEN)
+        weave(0, scale_sines(2, 0, sines, 26), woven_cosines(2, 0, folded, 4), woven[:, 0])
+        sines, folded = read_angles(2, 1, angle_products(2, 1, (4, 6)), ODD)
+        tiles[3, 1] = angle_products(3, 1, (4, 6))
+        weave(1, scale_sines(2, 1, sines, 28), woven_cosines(2, 1, folded, 8), woven[:, 1], WIDTH // 2)
+        sums = pair_of_products(1, 0, 2)
+        held = pair_of_products(1, 1, 3)
+        retune_pair(1, 0, sums, (44, 53))
+        quantise_slice(2, woven)
+        retune_pair(1, 1, held, (8, 9))
+        woven = place([P, PASSES, 2, WIDTH, PACK], BF16, "h_woven3", 68)
+        sines, folded = read_angles(3, 0, tiles[3, 0], (132, 128))
+        weave(0, scale_sines(3, 0, sines, 30), woven_cosines(3, 0, folded, 12), woven[:, 0])
+        sines, folded = read_angles(3, 1, tiles[3, 1], ODD)
+        cosines = woven_cosines(3, 1, folded, 16)
+        weave(1, scale_sines(3, 1, sines, 20), cosines, woven[:, 1], 0)
+        sums = pair_of_products(2, 0, 5)
+        kept = products(2, 2, psum_bank("y_kept2", 7)[:, 0, :])
+        retune_pair(2, 0, sums, (48, 54))
+        quantise_slice(3, woven)
+        y_sb = place([P, WIDTH], F32, "y_sb22", 19.5)
+        nc.scalar.copy(y_sb[:], kept)
+        scatter_sum(2, 2, y_sb[:])
+        kept = products(2, 3, psum_bank("y_kept3", 7)[:, 1, :])
         for n in range(ROW_TILES - 1):
-            bank = psum_bank("y_last%d" % n, (3, 7, 0)[n])
-            products(last, n, bank[:, 0, :])
-            retune_fused(last, n, bank[:, 0, :], 56 + n)
+            y_sb = place([P, WIDTH], F32, "y_sb3%d" % n, 60 + n)
+            nc.scalar.copy(y_sb[:], products(last, n, psum_bank("y_last%d" % n, n)[:, 0, :]))
+            scatter_sum(last, n, y_sb[:])
+            nc.sync.dma_start(out[P * n : P * (n + 1), :], phases[n][:])
         n = ROW_TILES - 1
-        y_sb = place([P, 2 * WIDTH], F32, "y_sb_last", 60)
-        nc.scalar.copy(y_sb[:, :WIDTH], held[:, 1, :])
-        bank = psum_bank("y_last%d" % n, 1)
-        products(last, n, bank[:, 0, :])
-        nc.scalar.copy(y_sb[:, WIDTH:], bank[:, 0, :])
-        nc.vector.tensor_tensor(
-            phases[n][:].indirect(offsets[:, 2 * WIDTH // ENTRIES_PER_COLUMN :]), old[n][:, 2 * WIDTH :], y_sb[:], ALU.add
-        )
+        y_sb = place([P, 2 * WIDTH], F32, "y_sb_last", 76)
+        nc.scalar.copy(y_sb[:, :WIDTH], kept)
+        nc.scalar.copy(y_sb[:, WIDTH:], products(last, n, psum_bank("y_last%d" % n, n)[:, 0, :]))
+        scatter_sum(last - 1, n, y_sb[:], 2)
         nc.sync.dma_start(out[P * n : P * (n + 1), :], phases[n][:])

@@ -70,11 +70,6 @@ def tile_list_choir_phase_retune_kernel(
             nc.sync.dma_start(tile[:], vec.rearrange("(b p t) -> p b t", b=PASSES, t=PACK))
             return tile
 
-        def load_pass_of_vector(vec, b, name):
-            tile = keep.tile([P, PACK], F32, name=name)
-            nc.sync.dma_start(tile[:], vec[PASS * b : PASS * (b + 1)].rearrange("(p t) -> p t", t=PACK))
-            return tile
-
         def load_phases(n):
             tile = keep.tile([P, T], F32, name="phases%d" % n, align_bytes=64)
             nc.sync.dma_start(tile[:], gT[P * n : P * (n + 1), :])
@@ -84,17 +79,18 @@ def tile_list_choir_phase_retune_kernel(
         for quadrant in range(4):
             blocks = tab_scales[:, 4 * quadrant : 4 * quadrant + 4, :]
             nc.sync.dma_start(tab_sc[32 * quadrant : 32 * quadrant + 8, :].bitcast(I32), blocks.bitcast(I32))
-        w1_raw = {(a, 0): load_weight(w1, a, 0, "w1_raw%d0" % a, 16 + 8 * a) for a in range(PASSES)}
-        tab_w.append(load_table_words(1))
+        w1_raw = {(0, 0): load_weight(w1, 0, 0, "w1_raw00", 16)}
         bias_sb = load_channel_vector(bias, "bias_sb")
-        for a in range(PASSES):
-            w1_raw[a, 1] = load_weight(w1, a, 1, "w1_raw%d1" % a, 32 + 8 * a)
+        w1_raw[1, 0] = load_weight(w1, 1, 0, "w1_raw10", 24)
+        tab_w.append(load_table_words(1))
+        w1_raw[0, 1] = load_weight(w1, 0, 1, "w1_raw01", 32)
         amp_sin = load_channel_vector(amps, "amps_sb")
-        amp_cos = [load_pass_of_vector(ampc, 0, "ampc_sb0")]
-        w5_raw = [load_weight(w5, b, 0, "w5_raw%d" % b, 48 + 8 * b) for b in range(PASSES)]
-        phases = [load_phases(0), load_phases(1)]
-        amp_cos.append(load_pass_of_vector(ampc, 1, "ampc_sb1"))
-        phases.extend([load_phases(2), load_phases(3)])
+        w1_raw[1, 1] = load_weight(w1, 1, 1, "w1_raw11", 40)
+        amp_cos = load_channel_vector(ampc, "ampc_sb")
+        w5_raw = [load_weight(w5, 0, 0, "w5_raw0", 48)]
+        phases = [load_phases(0)]
+        w5_raw.append(load_weight(w5, 1, 0, "w5_raw1", 56))
+        phases.extend([load_phases(n) for n in range(1, ROW_TILES)])
         w4_w = keep.tile([P, PASSES, 2 * N], U8, name="w4_w", align_bytes=64)
         nc.sync.dma_start(w4_w[:].bitcast(I32), w4_words.rearrange("b p c -> p b c").bitcast(I32))
         for quadrant in range(4):
@@ -249,7 +245,7 @@ def tile_list_choir_phase_retune_kernel(
                 )
             nc.gpsimd.tensor_tensor(
                 target[:, 1, :, :], cosines[:],
-                amp_cos[b][:].unsqueeze(1).to_broadcast([P, WIDTH, PACK]), ALU.mult,
+                amp_cos[:, b, :].unsqueeze(1).to_broadcast([P, WIDTH, PACK]), ALU.mult,
             )
 
         h_q = {}
@@ -300,7 +296,7 @@ def tile_list_choir_phase_retune_kernel(
         sines, folded = read_angles(0, 0, angle_products(0, 0, (4, 5, 6, 7)), (76, 80))
         nc.scalar.activation(folded[:], folded[:], ACT.Sin, bias=math.pi / 2, scale=-1.0)
         vector_scale(woven[:, 0, :, :], sines[:], amp_sin[:, 0, :])
-        vector_scale(woven[:, 1, :, :], folded[:], amp_cos[0][:])
+        vector_scale(woven[:, 1, :, :], folded[:], amp_cos[:, 0, :])
         read = {(1, 0): read_angles(1, 0, angle_products(1, 0, (0, 1)), EVEN)}
         w5_q = [quantise_w5(0, (64, 66))]
         h_q[0, 0] = quantise(woven[:].rearrange("p h c t -> p (h c t)"), 2 * WIDTH, "h00", 54) + (0,)

@@ -2,6 +2,7 @@ import math
 from contextlib import ExitStack
 
 import concourse.mybir as mybir
+from concourse.masks import make_identity
 
 K, H, N, T, S = 1024, 1024, 512, 2048, 1024
 FLOPS = 2 * K * H * S + 2 * 2 * H * N * S
@@ -65,11 +66,6 @@ def tile_list_choir_phase_retune_kernel(
             nc.sync.dma_start(raw[:], block.rearrange("(p j) c -> p j c", j=PACK))
             return raw
 
-        def load_channel_vector(vec, name):
-            tile = keep.tile([P, PASSES, PACK], F32, name=name)
-            nc.sync.dma_start(tile[:], vec.rearrange("(b p t) -> p b t", b=PASSES, t=PACK))
-            return tile
-
         def load_phases(n):
             tile = keep.tile([P, T], F32, name="phases%d" % n, align_bytes=64)
             nc.sync.dma_start(tile[:], gT[P * n : P * (n + 1), :])
@@ -80,13 +76,15 @@ def tile_list_choir_phase_retune_kernel(
             blocks = tab_scales[:, 4 * quadrant : 4 * quadrant + 4, :]
             nc.sync.dma_start(tab_sc[32 * quadrant : 32 * quadrant + 8, :].bitcast(I32), blocks.bitcast(I32))
         w1_raw = {(0, 0): load_weight(w1, 0, 0, "w1_raw00", 16)}
-        bias_sb = load_channel_vector(bias, "bias_sb")
+        vectors = (bias, amps, ampc)
+        rows = keep.tile([P, PASS], F32, name="vector_rows")
+        nc.vector.memset(rows[:], 0.0)
+        for k, vec in enumerate(vectors):
+            nc.sync.dma_start(rows[PASSES * k : PASSES * (k + 1), :], vec.rearrange("(b c) -> b c", b=PASSES))
         w1_raw[1, 0] = load_weight(w1, 1, 0, "w1_raw10", 24)
         tab_w.append(load_table_words(1))
-        w1_raw[0, 1] = load_weight(w1, 0, 1, "w1_raw01", 32)
-        amp_sin = load_channel_vector(amps, "amps_sb")
-        w1_raw[1, 1] = load_weight(w1, 1, 1, "w1_raw11", 40)
-        amp_cos = load_channel_vector(ampc, "ampc_sb")
+        for a in range(PASSES):
+            w1_raw[a, 1] = load_weight(w1, a, 1, "w1_raw%d1" % a, 32 + 8 * a)
         w5_raw = [load_weight(w5, 0, 0, "w5_raw0", 48)]
         phases = [load_phases(0)]
         w5_raw.append(load_weight(w5, 1, 0, "w5_raw1", 56))
@@ -98,6 +96,15 @@ def tile_list_choir_phase_retune_kernel(
                 w4_sc[32 * quadrant : 32 * quadrant + 4, :, :].bitcast(I32),
                 w4_scales[:, 4 * quadrant : 4 * quadrant + 4, :].rearrange("b q c -> q b c").bitcast(I32),
             )
+
+        identity = keep.tile([P, P], F32, name="identity")
+        make_identity(nc, identity[:])
+        turned = psum.tile([P, PACK, P], F32, name="turned", offset=0)
+        for t in range(PACK):
+            nc.tensor.transpose(turned[:, t, :], rows[:, t:PASS:PACK], identity[:])
+        channels = keep.tile([P, len(vectors), PASSES, PACK], F32, name="channels")
+        nc.scalar.copy(channels[:].rearrange("p k b t -> p t (k b)"), turned[:, :, : len(vectors) * PASSES])
+        bias_sb, amp_sin, amp_cos = [channels[:, k, :, :] for k in range(len(vectors))]
 
         def quantise(values, columns, name, kib=None, parts=1):
             if kib is None:

@@ -76,11 +76,13 @@ def tile_list_choir_phase_retune_kernel(
             blocks = tab_scales[:, 4 * quadrant : 4 * quadrant + 4, :]
             nc.sync.dma_start(tab_sc[32 * quadrant : 32 * quadrant + 8, :].bitcast(I32), blocks.bitcast(I32))
         w1_raw = {(0, 0): load_weight(w1, 0, 0, "w1_raw00", 16)}
-        vectors = (bias, amps, ampc)
+        bias_sb = keep.tile([P, PASSES, PACK], F32, name="bias_sb")
+        nc.sync.dma_start(bias_sb[:], bias.rearrange("(b p t) -> p b t", b=PASSES, t=PACK))
+        vectors = (amps, ampc)
         rows = keep.tile([P, PASS], F32, name="vector_rows")
         nc.vector.memset(rows[:], 0.0)
         for k, vec in enumerate(vectors):
-            nc.sync.dma_start(rows[PASSES * k : PASSES * (k + 1), :], vec.rearrange("(b c) -> b c", b=PASSES))
+            nc.gpsimd.dma_start(rows[PASSES * k : PASSES * (k + 1), :], vec.rearrange("(b c) -> b c", b=PASSES))
         w1_raw[1, 0] = load_weight(w1, 1, 0, "w1_raw10", 24)
         tab_w.append(load_table_words(1))
         for a in range(PASSES):
@@ -99,12 +101,8 @@ def tile_list_choir_phase_retune_kernel(
 
         identity = keep.tile([P, P], F32, name="identity")
         make_identity(nc, identity[:])
-        turned = psum.tile([P, PACK, P], F32, name="turned", offset=0)
-        for t in range(PACK):
-            nc.tensor.transpose(turned[:, t, :], rows[:, t:PASS:PACK], identity[:])
         channels = keep.tile([P, len(vectors), PASSES, PACK], F32, name="channels")
-        nc.scalar.copy(channels[:].rearrange("p k b t -> p t (k b)"), turned[:, :, : len(vectors) * PASSES])
-        bias_sb, amp_sin, amp_cos = [channels[:, k, :, :] for k in range(len(vectors))]
+        amp_sin, amp_cos = [channels[:, k, :, :] for k in range(len(vectors))]
 
         def quantise(values, columns, name, kib=None, parts=1):
             if kib is None:
@@ -207,14 +205,16 @@ def tile_list_choir_phase_retune_kernel(
                     tiles.append(bank[:, i, :])
             return tiles
 
+        def read_function(b, tiles, t, func, into):
+            nc.scalar.activation(into[:, t, :], tiles[t], func, bias=bias_sb[:, b, t : t + 1])
+
         def read_angles(s, b, tiles, kibs, sines_first=False):
             sines = place([P, PACK, WIDTH], F32, "sines%d%d" % (s, b), kibs[0])
             folded = place([P, PACK, WIDTH], F32, "folded%d%d" % (s, b), kibs[1])
             for t in range(PACK):
-                bias_t = bias_sb[:, b, t : t + 1]
                 steps = [(folded, ACT.Abs), (sines, ACT.Sin)]
                 for tile, func in reversed(steps) if sines_first else steps:
-                    nc.scalar.activation(tile[:, t, :], tiles[t], func, bias=bias_t)
+                    read_function(b, tiles, t, func, tile)
             return sines, folded
 
         def vector_scale(dst, src, amp):
@@ -243,27 +243,39 @@ def tile_list_choir_phase_retune_kernel(
         def weave(b, rounded, cosines, target, cut=WIDTH):
             if cut > 0:
                 nc.gpsimd.tensor_scalar(
-                    target[:, 0, :cut, :], rounded[:, :, :cut].rearrange("p t c -> p c t"), 1.0, 1.0, ALU.mult, ALU.mult
+                    target[0][:, :cut, :], rounded[:, :, :cut].rearrange("p t c -> p c t"), 1.0, 1.0, ALU.mult, ALU.mult
                 )
             if cut < WIDTH:
                 nc.scalar.copy(
-                    target[:, 0, cut:, :].rearrange("p (c i) t -> p c t i", i=4),
+                    target[0][:, cut:, :].rearrange("p (c i) t -> p c t i", i=4),
                     rounded[:, :, cut:].rearrange("p t (c i) -> p c t i", i=4),
                 )
             nc.gpsimd.tensor_tensor(
-                target[:, 1, :, :], cosines[:],
-                amp_cos[:, b, :].unsqueeze(1).to_broadcast([P, WIDTH, PACK]), ALU.mult,
+                target[1], cosines[:], amp_cos[:, b, :].unsqueeze(1).to_broadcast([P, WIDTH, PACK]), ALU.mult
             )
 
         h_q = {}
 
+        def quantise_parts(parts, name, kib):
+            step = parts[0].shape[1] // PACK
+            codes = place([P, step * len(parts)], U32, name + "_codes", kib)
+            scales = keep.tile([P, step * len(parts)], U8, name=name + "_scales", align_bytes=64)
+            for k, values in enumerate(parts):
+                cols = slice(step * k, step * (k + 1))
+                nc.vector.quantize_mx(out=codes[:, cols].bitcast(FP8X4), scales=scales[:, cols], in_=values)
+            return codes, scales
+
+        def woven_slice(s):
+            tiles = [place([P, 2, WIDTH, PACK], BF16, "h_woven%d%d" % (s, b), 68 + 4 * b) for b in range(PASSES)]
+            return [(tile[:, 0, :, :], tile[:, 1, :, :], tile[:].rearrange("p h c t -> p (h c t)")) for tile in tiles]
+
         def quantise_slice(s, woven):
-            codes, scales = quantise(woven[:].rearrange("p b h c t -> p (b h c t)"), 4 * WIDTH, "h%d" % s, 36 + 4 * s)
+            codes, scales = quantise_parts([unit[2] for unit in woven], "h%d" % s, 36 + 4 * s)
             for b in range(PASSES):
                 h_q[s, b] = (codes, scales, 2 * WIDTH * b)
 
-        def product_pass(s, n, sums, step):
-            b, half = divmod(step, 2)
+        def product_pass(s, n, sums, step, order):
+            b, half = order[step // 2], step % 2
             codes, scales, first = h_q[s, b]
             cols = slice(first + WIDTH * half, first + WIDTH * (half + 1))
             if half == 0:
@@ -275,9 +287,9 @@ def tile_list_choir_phase_retune_kernel(
                 start=(step == 0), stop=(step == 2 * PASSES - 1),
             )
 
-        def products(s, n, sums):
+        def products(s, n, sums, order=(0, 1)):
             for step in range(2 * PASSES):
-                product_pass(s, n, sums, step)
+                product_pass(s, n, sums, step, order)
             return sums
 
         def pair_of_products(s, half, index):
@@ -301,6 +313,10 @@ def tile_list_choir_phase_retune_kernel(
         EVEN, ODD = (84, 88), (130, 134)
         woven = place([P, 2, WIDTH, PACK], BF16, "h_woven00", 40)
         sines, folded = read_angles(0, 0, angle_products(0, 0, (4, 5, 6, 7)), (76, 80))
+        turned = psum.tile([P, PACK, P], F32, name="turned", offset=4 * 2 * KIB)
+        for t in range(PACK):
+            nc.tensor.transpose(turned[:, t, :], rows[:, t:PASS:PACK], identity[:])
+        nc.scalar.copy(channels[:].rearrange("p k b t -> p t (k b)"), turned[:, :, : len(vectors) * PASSES])
         nc.scalar.activation(folded[:], folded[:], ACT.Sin, bias=math.pi / 2, scale=-1.0)
         vector_scale(woven[:, 0, :, :], sines[:], amp_sin[:, 0, :])
         vector_scale(woven[:, 1, :, :], folded[:], amp_cos[:, 0, :])
@@ -309,58 +325,57 @@ def tile_list_choir_phase_retune_kernel(
         h_q[0, 0] = quantise(woven[:].rearrange("p h c t -> p (h c t)"), 2 * WIDTH, "h00", 54) + (0,)
         w5_q.append(quantise_w5(1, (124, 72)))
         old = [gather_phases(place([P, S], F32, "old0", 124), 0), gather_phases(keep.tile([P, S], F32, name="old1"), 1)]
-        woven = place([P, 2, WIDTH, PACK], BF16, "h_woven01", 72)
+        woven = place([P, 2, WIDTH, PACK], BF16, "h_woven01", 70)
         sines, folded = read_angles(0, 1, angle_products(0, 1, (2, 3)), (96, 103))
-        weave(1, scale_sines(0, 1, sines, 114), woven_cosines(0, 1, folded, 118), woven)
+        weave(1, scale_sines(0, 1, sines, 114), woven_cosines(0, 1, folded, 118), (woven[:, 0, :, :], woven[:, 1, :, :]))
         h_q[0, 1] = quantise(woven[:].rearrange("p h c t -> p (h c t)"), 2 * WIDTH, "h01") + (0,)
         old.append(gather_phases(place([P, S], F32, "old2", 116), 2))
         old.append(gather_phases(place([P, S], F32, "old3", 120), 3))
         read[1, 1] = read_angles(1, 1, angle_products(1, 1, (0, 1), (1, 0)), (93, 103), True)
         tiles = {(2, 0): angle_products(2, 0, (2, 3)), (3, 0): angle_products(3, 0, (0, 1))}
-        woven = place([P, PASSES, 2, WIDTH, PACK], BF16, "h_woven1", 68)
-        weave(0, scale_sines(1, 0, read[1, 0][0], 97), woven_cosines(1, 0, read[1, 0][1], 99), woven[:, 0])
-        weave(1, scale_sines(1, 1, read[1, 1][0], 24), woven_cosines(1, 1, read[1, 1][1], 0), woven[:, 1])
+        woven = woven_slice(1)
+        weave(0, scale_sines(1, 0, read[1, 0][0], 97), woven_cosines(1, 0, read[1, 0][1], 99), woven[0])
+        weave(1, scale_sines(1, 1, read[1, 1][0], 24), woven_cosines(1, 1, read[1, 1][1], 0), woven[1])
         sums = [psum_bank("y_first%d" % i, 4 + 2 * i)[:, 0, :] for i in range(2)]
         for step in range(2 * PASSES):
             for i in range(2):
-                product_pass(0, i, sums[i], step)
+                product_pass(0, i, sums[i], step, (0, 1))
         held = pair_of_products(0, 1, 5)
         retune_pair(0, 0, sums, (40, 52))
         quantise_slice(1, woven)
         retune_pair(0, 1, held, (0, 1))
-        woven = place([P, PASSES, 2, WIDTH, PACK], BF16, "h_woven2", 68)
+        woven = woven_slice(2)
         sines, folded = read_angles(2, 0, tiles[2, 0], EVEN)
-        weave(0, scale_sines(2, 0, sines, 26), woven_cosines(2, 0, folded, 4), woven[:, 0])
+        weave(0, scale_sines(2, 0, sines, 26), woven_cosines(2, 0, folded, 4), woven[0])
         sines, folded = read_angles(2, 1, angle_products(2, 1, (4, 6)), ODD)
-        tiles[3, 1] = angle_products(3, 1, (4, 6))
-        weave(1, scale_sines(2, 1, sines, 28), woven_cosines(2, 1, folded, 8), woven[:, 1], WIDTH // 2)
+        weave(1, scale_sines(2, 1, sines, 28), woven_cosines(2, 1, folded, 8), woven[1], WIDTH // 2)
         sums = pair_of_products(1, 0, 2)
         held = pair_of_products(1, 1, 3)
         retune_pair(1, 0, sums, (44, 53))
+        tiles[3, 1] = angle_products(3, 1, (5, 2))
         quantise_slice(2, woven)
         retune_pair(1, 1, held, (8, 9))
-        woven = place([P, PASSES, 2, WIDTH, PACK], BF16, "h_woven3", 68)
+        woven = woven_slice(3)
         sines, folded = read_angles(3, 0, tiles[3, 0], (132, 128))
-        weave(0, scale_sines(3, 0, sines, 30), woven_cosines(3, 0, folded, 12), woven[:, 0])
+        weave(0, scale_sines(3, 0, sines, 30), woven_cosines(3, 0, folded, 12), woven[0])
         sines, folded = read_angles(3, 1, tiles[3, 1], ODD)
         cosines = woven_cosines(3, 1, folded, 16)
-        weave(1, scale_sines(3, 1, sines, 20), cosines, woven[:, 1], 0)
-        sums = pair_of_products(2, 0, 5)
-        kept = products(2, 2, psum_bank("y_kept2", 7)[:, 0, :])
+        weave(1, scale_sines(3, 1, sines, 20), cosines, woven[1], 0)
+        sums = pair_of_products(2, 0, 4)
+        kept = pair_of_products(2, 1, 7)
         retune_pair(2, 0, sums, (48, 54))
         quantise_slice(3, woven)
         y_sb = place([P, WIDTH], F32, "y_sb22", 19.5)
-        nc.scalar.copy(y_sb[:], kept)
+        nc.scalar.copy(y_sb[:], kept[0])
         scatter_sum(2, 2, y_sb[:])
-        kept = products(2, 3, psum_bank("y_kept3", 7)[:, 1, :])
         for n in range(ROW_TILES - 1):
             y_sb = place([P, WIDTH], F32, "y_sb3%d" % n, 60 + n)
-            nc.scalar.copy(y_sb[:], products(last, n, psum_bank("y_last%d" % n, n)[:, 0, :]))
+            nc.scalar.copy(y_sb[:], products(last, n, psum_bank("y_last%d" % n, (0, 1, 6)[n])[:, 0, :], (1, 0) if n else (0, 1)))
             scatter_sum(last, n, y_sb[:])
             nc.sync.dma_start(out[P * n : P * (n + 1), :], phases[n][:])
         n = ROW_TILES - 1
-        y_sb = place([P, 2 * WIDTH], F32, "y_sb_last", 76)
-        nc.scalar.copy(y_sb[:, :WIDTH], kept)
-        nc.scalar.copy(y_sb[:, WIDTH:], products(last, n, psum_bank("y_last%d" % n, n)[:, 0, :]))
+        y_sb = place([P, 2 * WIDTH], F32, "y_sb_last", 21)
+        nc.scalar.copy(y_sb[:, :WIDTH], kept[1])
+        nc.scalar.copy(y_sb[:, WIDTH:], products(last, n, psum_bank("y_last%d" % n, n)[:, 0, :], (1, 0)))
         scatter_sum(last - 1, n, y_sb[:], 2)
         nc.sync.dma_start(out[P * n : P * (n + 1), :], phases[n][:])

@@ -51,9 +51,9 @@ def tile_list_choir_phase_retune_kernel(
         nc.sync.dma_start(offsets[:], offs)
 
         tab_sc = keep.tile([P, T], U8, name="tab_sc", align_bytes=64)
-        nc.gpsimd.memset(tab_sc[:].bitcast(I32), 0)
+        nc.vector.memset(tab_sc[:].bitcast(I32), 0)
         w4_sc = keep.tile([P, PASSES, N], U8, name="w4_sc", align_bytes=64)
-        nc.gpsimd.memset(w4_sc[:].rearrange("p b c -> p (b c)").bitcast(I32), 0)
+        nc.vector.memset(w4_sc[:].rearrange("p b c -> p (b c)").bitcast(I32), 0)
 
         def load_table_words(a):
             words = place([P, T], I32, "tab_w%d" % a, 8 * a)
@@ -70,6 +70,9 @@ def tile_list_choir_phase_retune_kernel(
             tile = keep.tile([P, T], F32, name="phases%d" % n, align_bytes=64)
             nc.sync.dma_start(tile[:], gT[P * n : P * (n + 1), :])
             return tile
+
+        identity = keep.tile([P, P], F32, name="identity")
+        make_identity(nc, identity[:])
 
         tab_w = [load_table_words(0)]
         for quadrant in range(4):
@@ -99,8 +102,6 @@ def tile_list_choir_phase_retune_kernel(
                 w4_scales[:, 4 * quadrant : 4 * quadrant + 4, :].rearrange("b q c -> q b c").bitcast(I32),
             )
 
-        identity = keep.tile([P, P], F32, name="identity")
-        make_identity(nc, identity[:])
         channels = keep.tile([P, len(vectors), PASSES, PACK], F32, name="channels")
         amp_sin, amp_cos = [channels[:, k, :, :] for k in range(len(vectors))]
 
@@ -129,12 +130,6 @@ def tile_list_choir_phase_retune_kernel(
         v_sc = keep.tile([P, S], U8, name="v_sc", align_bytes=64)
         nc.vector.tensor_copy(v_sc[:], tab_sc[:].indirect(offsets[:]))
         nc.vector.tensor_copy(v_w[0][:], tab_w[0][:].bitcast(U32).indirect(offsets[:]))
-
-        def gpsimd_weave(dst, src):
-            nc.gpsimd.tensor_scalar(
-                dst.rearrange("p t m j -> p m t j"), src.rearrange("p j (m t) -> p m t j", t=PACK),
-                1.0, 1.0, ALU.mult, ALU.mult,
-            )
 
         def paired_weave(copy):
             return lambda dst, src: copy(
@@ -176,7 +171,7 @@ def tile_list_choir_phase_retune_kernel(
             return codes, scales
 
         w1_q = {
-            (0, 0): quantise_w1_shared(0, 0, 72, [scalar_weave, gpsimd_weave]),
+            (0, 0): quantise_w1_shared(0, 0, 104, [scalar_weave, vector_weave]),
             (1, 0): quantise_w1_shared(1, 0, 48, [scalar_weave, vector_weave]),
         }
         nc.vector.tensor_copy(v_w[1][:, entries(0)], tab_w[1][:].bitcast(U32).indirect(places(0)))

@@ -52,8 +52,6 @@ def tile_list_choir_phase_retune_kernel(
 
         tab_sc = keep.tile([P, T], U8, name="tab_sc", align_bytes=64)
         nc.vector.memset(tab_sc[:].bitcast(I32), 0)
-        w4_sc = keep.tile([P, PASSES, N], U8, name="w4_sc", align_bytes=64)
-        nc.vector.memset(w4_sc[:].rearrange("p b c -> p (b c)").bitcast(I32), 0)
 
         def load_table_words(a):
             words = place([P, T], I32, "tab_w%d" % a, 8 * a)
@@ -71,6 +69,15 @@ def tile_list_choir_phase_retune_kernel(
             nc.sync.dma_start(tile[:], gT[P * n : P * (n + 1), :])
             return tile
 
+        vectors = (amps, ampc)
+        used = slice(P - len(vectors) * PASSES, P)
+        rows = keep.tile([P, PASS], F32, name="vector_rows")
+        for k, vec in enumerate(vectors):
+            first = used.start + PASSES * k
+            nc.gpsimd.dma_start(rows[first : first + PASSES, :], vec.rearrange("(b c) -> b c", b=PASSES))
+        nc.gpsimd.memset(rows[: used.start, :], 0.0)
+        w4_sc = keep.tile([P, PASSES, N], U8, name="w4_sc", align_bytes=64)
+        nc.gpsimd.memset(w4_sc[:].rearrange("p b c -> p (b c)").bitcast(I32), 0)
         identity = keep.tile([P, P], F32, name="identity")
         make_identity(nc, identity[:])
 
@@ -81,23 +88,20 @@ def tile_list_choir_phase_retune_kernel(
         w1_raw = {(0, 0): load_weight(w1, 0, 0, "w1_raw00", 16)}
         bias_sb = keep.tile([P, PASSES, PACK], F32, name="bias_sb")
         nc.sync.dma_start(bias_sb[:], bias.rearrange("(b p t) -> p b t", b=PASSES, t=PACK))
-        vectors = (amps, ampc)
-        rows = keep.tile([P, PASS], F32, name="vector_rows")
-        nc.vector.memset(rows[:], 0.0)
-        for k, vec in enumerate(vectors):
-            nc.gpsimd.dma_start(rows[PASSES * k : PASSES * (k + 1), :], vec.rearrange("(b c) -> b c", b=PASSES))
         w1_raw[1, 0] = load_weight(w1, 1, 0, "w1_raw10", 24)
         tab_w.append(load_table_words(1))
         for a in range(PASSES):
             w1_raw[a, 1] = load_weight(w1, a, 1, "w1_raw%d1" % a, 32 + 8 * a)
         w5_raw = [load_weight(w5, 0, 0, "w5_raw0", 48)]
-        phases = [load_phases(0)]
+        phases = [keep.tile([P, T], F32, name="phases0", align_bytes=64)]
+        nc.sync.dma_start(phases[0][:, : T // 2], gT[:P, : T // 2])
         w5_raw.append(load_weight(w5, 1, 0, "w5_raw1", 56))
+        nc.sync.dma_start(phases[0][:, T // 2 :], gT[:P, T // 2 :])
         phases.extend([load_phases(n) for n in range(1, ROW_TILES)])
         w4_w = keep.tile([P, PASSES, 2 * N], U8, name="w4_w", align_bytes=64)
         nc.sync.dma_start(w4_w[:].bitcast(I32), w4_words.rearrange("b p c -> p b c").bitcast(I32))
         for quadrant in range(4):
-            nc.gpsimd.dma_start(
+            nc.sync.dma_start(
                 w4_sc[32 * quadrant : 32 * quadrant + 4, :, :].bitcast(I32),
                 w4_scales[:, 4 * quadrant : 4 * quadrant + 4, :].rearrange("b q c -> q b c").bitcast(I32),
             )
@@ -130,6 +134,12 @@ def tile_list_choir_phase_retune_kernel(
         v_sc = keep.tile([P, S], U8, name="v_sc", align_bytes=64)
         nc.vector.tensor_copy(v_sc[:], tab_sc[:].indirect(offsets[:]))
         nc.vector.tensor_copy(v_w[0][:], tab_w[0][:].bitcast(U32).indirect(offsets[:]))
+
+        def gpsimd_weave(dst, src):
+            nc.gpsimd.tensor_scalar(
+                dst.rearrange("p t m j -> p m t j"), src.rearrange("p j (m t) -> p m t j", t=PACK),
+                1.0, 1.0, ALU.mult, ALU.mult,
+            )
 
         def paired_weave(copy):
             return lambda dst, src: copy(
@@ -171,7 +181,7 @@ def tile_list_choir_phase_retune_kernel(
             return codes, scales
 
         w1_q = {
-            (0, 0): quantise_w1_shared(0, 0, 104, [scalar_weave, vector_weave]),
+            (0, 0): quantise_w1_shared(0, 0, 72, [scalar_weave, gpsimd_weave]),
             (1, 0): quantise_w1_shared(1, 0, 48, [scalar_weave, vector_weave]),
         }
         nc.vector.tensor_copy(v_w[1][:, entries(0)], tab_w[1][:].bitcast(U32).indirect(places(0)))
@@ -311,7 +321,7 @@ def tile_list_choir_phase_retune_kernel(
         turned = psum.tile([P, PACK, P], F32, name="turned", offset=4 * 2 * KIB)
         for t in range(PACK):
             nc.tensor.transpose(turned[:, t, :], rows[:, t:PASS:PACK], identity[:])
-        nc.scalar.copy(channels[:].rearrange("p k b t -> p t (k b)"), turned[:, :, : len(vectors) * PASSES])
+        nc.scalar.copy(channels[:].rearrange("p k b t -> p t (k b)"), turned[:, :, used])
         nc.scalar.activation(folded[:], folded[:], ACT.Sin, bias=math.pi / 2, scale=-1.0)
         vector_scale(woven[:, 0, :, :], sines[:], amp_sin[:, 0, :])
         vector_scale(woven[:, 1, :, :], folded[:], amp_cos[:, 0, :])

import math
from contextlib import ExitStack

import concourse.mybir as mybir
from concourse.masks import make_identity

K, H, N, T, S = 1024, 1024, 512, 2048, 1024
FLOPS = 2 * K * H * S + 2 * 2 * H * N * S

F32 = mybir.dt.float32
BF16 = mybir.dt.bfloat16
I32 = mybir.dt.int32
U32 = mybir.dt.uint32
U16 = mybir.dt.uint16
U8 = mybir.dt.uint8
FP8X4 = mybir.dt.float8_e4m3fn_x4
FP4X4 = mybir.dt.float4_e2m1fn_x4
ACT = mybir.ActivationFunctionType
ALU = mybir.AluOpType

P = 128
PACK = 4
PASS = P * PACK
PASSES = K // PASS
BANK = 512
ROW_TILES = N // P
ENTRIES_PER_COLUMN = 16

SLICES = 4
WIDTH = S // SLICES
KIB = 1024


def tile_list_choir_phase_retune_kernel(
    tc, tab_words, tab_scales, offs, gT, w1, bias, w4_words, w4_scales, w5, amps, ampc, out
):
    nc = tc.nc
    last = SLICES - 1
    with ExitStack() as ctx:
        keep = ctx.enter_context(tc.tile_pool(name="keep", bufs=1))
        arena = ctx.enter_context(tc.tile_pool(name="arena", bufs=1))
        psum = ctx.enter_context(tc.psum_pool(name="psum", bufs=1))

        def psum_bank(name, index):
            return psum.tile([P, 2, WIDTH], F32, name=name, offset=index * 2 * KIB)

        def place(shape, dtype, name, kib):
            return arena.tile(shape, dtype, name=name, align_bytes=64, offset=int(kib * KIB))

        offsets = keep.tile([P, S // ENTRIES_PER_COLUMN], U16, name="offsets")
        nc.sync.dma_start(offsets[:], offs)

        tab_sc = keep.tile([P, T], U8, name="tab_sc", align_bytes=64)
        nc.vector.memset(tab_sc[:].bitcast(I32), 0)

        def load_table_words(a):
            words = place([P, T], I32, "tab_w%d" % a, 8 * a)
            nc.sync.dma_start(words[:], tab_words[a].rearrange("p e j -> p (e j)").bitcast(I32))
            return words

        def load_weight(weight, rows, cols, name, kib):
            raw = place([P, PACK, PASS], F32, name, kib)
            block = weight[PASS * rows : PASS * (rows + 1), PASS * cols : PASS * (cols + 1)]
            nc.sync.dma_start(raw[:], block.rearrange("(p j) c -> p j c", j=PACK))
            return raw

        def load_phases(n):
            tile = keep.tile([P, T], F32, name="phases%d" % n, align_bytes=64)
            nc.sync.dma_start(tile[:], gT[P * n : P * (n + 1), :])
            return tile

        vectors = (amps, ampc)
        used = slice(P - len(vectors) * PASSES, P)
        rows = keep.tile([P, PASS], F32, name="vector_rows")
        for k, vec in enumerate(vectors):
            first = used.start + PASSES * k
            nc.gpsimd.dma_start(rows[first : first + PASSES, :], vec.rearrange("(b c) -> b c", b=PASSES))
        nc.gpsimd.memset(rows[: used.start, :], 0.0)
        w4_sc = keep.tile([P, PASSES, N], U8, name="w4_sc", align_bytes=64)
        nc.gpsimd.memset(w4_sc[:].rearrange("p b c -> p (b c)").bitcast(I32), 0)
        identity = keep.tile([P, P], F32, name="identity")
        make_identity(nc, identity[:])

        tab_w = [load_table_words(0)]
        for quadrant in range(4):
            blocks = tab_scales[:, 4 * quadrant : 4 * quadrant + 4, :]
            nc.sync.dma_start(tab_sc[32 * quadrant : 32 * quadrant + 8, :].bitcast(I32), blocks.bitcast(I32))
        w1_raw = {(0, 0): load_weight(w1, 0, 0, "w1_raw00", 16)}
        bias_sb = keep.tile([P, PASSES, PACK], F32, name="bias_sb")
        nc.sync.dma_start(bias_sb[:], bias.rearrange("(b p t) -> p b t", b=PASSES, t=PACK))
        w1_raw[1, 0] = load_weight(w1, 1, 0, "w1_raw10", 24)
        tab_w.append(load_table_words(1))
        for a in range(PASSES):
            w1_raw[a, 1] = load_weight(w1, a, 1, "w1_raw%d1" % a, 32 + 8 * a)
        w5_raw = [load_weight(w5, 0, 0, "w5_raw0", 48)]
        phases = [keep.tile([P, T], F32, name="phases0", align_bytes=64)]
        nc.sync.dma_start(phases[0][:, : T // 2], gT[:P, : T // 2])
        w5_raw.append(load_weight(w5, 1, 0, "w5_raw1", 56))
        nc.sync.dma_start(phases[0][:, T // 2 :], gT[:P, T // 2 :])
        phases.extend([load_phases(n) for n in range(1, ROW_TILES)])
        w4_w = keep.tile([P, PASSES, 2 * N], U8, name="w4_w", align_bytes=64)
        nc.sync.dma_start(w4_w[:].bitcast(I32), w4_words.rearrange("b p c -> p b c").bitcast(I32))
        for quadrant in range(4):
            nc.sync.dma_start(
                w4_sc[32 * quadrant : 32 * quadrant + 4, :, :].bitcast(I32),
                w4_scales[:, 4 * quadrant : 4 * quadrant + 4, :].rearrange("b q c -> q b c").bitcast(I32),
            )

        channels = keep.tile([P, len(vectors), PASSES, PACK], F32, name="channels")
        amp_sin, amp_cos = [channels[:, k, :, :] for k in range(len(vectors))]

        def quantise(values, columns, name, kib=None, parts=1):
            if kib is None:
                codes = keep.tile([P, columns], U32, name=name + "_codes", align_bytes=64)
            else:
                codes = place([P, columns], U32, name + "_codes", kib)
            scales = keep.tile([P, columns], U8, name=name + "_scales", align_bytes=64)
            step = columns // parts
            for first in range(0, columns, step):
                cols = slice(first, first + step)
                nc.vector.quantize_mx(
                    out=codes[:, cols].bitcast(FP8X4), scales=scales[:, cols],
                    in_=values[:, PACK * first : PACK * (first + step)],
                )
            return codes, scales

        def entries(s, count=1):
            return slice(WIDTH * s, WIDTH * (s + count))

        def places(s, count=1):
            return offsets[:, WIDTH * s // ENTRIES_PER_COLUMN : WIDTH * (s + count) // ENTRIES_PER_COLUMN]

        v_w = [keep.tile([P, S], U32, name="v_w%d" % a, align_bytes=64) for a in range(PASSES)]
        v_sc = keep.tile([P, S], U8, name="v_sc", align_bytes=64)
        nc.vector.tensor_copy(v_sc[:], tab_sc[:].indirect(offsets[:]))
        nc.vector.tensor_copy(v_w[0][:], tab_w[0][:].bitcast(U32).indirect(offsets[:]))

        def gpsimd_weave(dst, src):
            nc.gpsimd.tensor_scalar(
                dst.rearrange("p t m j -> p m t j"), src.rearrange("p j (m t) -> p m t j", t=PACK),
                1.0, 1.0, ALU.mult, ALU.mult,
            )

        def paired_weave(copy):
            return lambda dst, src: copy(
                dst.rearrange("p (u i) m j -> p m u j i", i=2),
                src.rearrange("p j (m u i) -> p m u j i", u=2, i=2),
            )

        scalar_weave, vector_weave = paired_weave(nc.scalar.copy), paired_weave(nc.vector.tensor_copy)

        def quantise_w1_shared(a, b, cut, copies):
            values = place([P, PACK, P, PACK], BF16, "w1_woven%d%d" % (a, b), 64 + 4 * a)
            for first, end, copy in ((0, cut, copies[0]), (cut, P, copies[1])):
                copy(values[:, :, first:end, :], w1_raw[a, b][:, :, PACK * first : PACK * end])
            return quantise(values[:].rearrange("p t m j -> p (t m j)"), PASS, "w1_%d%d" % (a, b))

        def quantise_w1_in_halves(a, b):
            values = place([P, PACK, P, PACK], BF16, "w1_woven%d%d" % (a, b), 64 + 4 * a)
            src = w1_raw[a, b][:].rearrange("p j (m u i) -> p u m j i", u=2, i=2)
            for u in range(2):
                nc.vector.tensor_copy(values[:, 2 * u : 2 * u + 2, :, :].rearrange("p i m j -> p m j i"), src[:, u, :, :, :])
            return quantise(values[:].rearrange("p t m j -> p (t m j)"), PASS, "w1_%d%d" % (a, b), None, 2)

        def quantise_w5(b, kibs):
            codes = keep.tile([P, N], U32, name="w5_%d_codes" % b, align_bytes=64)
            scales = keep.tile([P, N], U8, name="w5_%d_scales" % b, align_bytes=64)
            halves = []
            for half, kib in enumerate(kibs):
                cols = slice(N // 2 * half, N // 2 * (half + 1))
                values = place([P, N // 2, PACK], BF16, "w5_woven%d%d" % (b, half), kib)
                nc.vector.tensor_copy(
                    values[:].rearrange("p (c i) j -> p c j i", i=2),
                    w5_raw[b][:, :, cols].rearrange("p j (c i) -> p c j i", i=2),
                )
                halves.append((cols, values))
            for cols, values in halves:
                nc.vector.quantize_mx(
                    out=codes[:, cols].bitcast(FP8X4), scales=scales[:, cols], in_=values[:].rearrange("p c j -> p (c j)")
                )
            return codes, scales

        w1_q = {
            (0, 0): quantise_w1_shared(0, 0, 72, [scalar_weave, gpsimd_weave]),
            (1, 0): quantise_w1_shared(1, 0, 48, [scalar_weave, vector_weave]),
        }
        nc.vector.tensor_copy(v_w[1][:, entries(0)], tab_w[1][:].bitcast(U32).indirect(places(0)))
        nc.vector.tensor_copy(v_w[1][:, entries(1, last)], tab_w[1][:].bitcast(U32).indirect(places(1, last)))
        for a in range(PASSES):
            w1_q[a, 1] = quantise_w1_in_halves(a, 1)

        def angle_products(s, b, banks, order=(0, 1)):
            group = PACK // len(banks)
            tiles = []
            for k, index in enumerate(banks):
                bank = psum_bank("h_bank%d%d%d" % (s, b, k), index)
                for i in range(group):
                    t = group * k + i
                    for a in order:
                        codes, scales = w1_q[a, b]
                        nc.tensor.matmul_mx(
                            out=bank[:, i, :],
                            lhsT=codes[:, P * t : P * (t + 1)].bitcast(FP8X4),
                            lhsT_scale=scales[:, P * t : P * (t + 1)],
                            rhs=v_w[a][:, entries(s)].bitcast(FP8X4),
                            rhs_scale=v_sc[4 * a : P, entries(s)],
                            start=(a == order[0]),
                            stop=(a == order[-1]),
                        )
                    tiles.append(bank[:, i, :])
            return tiles

        def read_function(b, tiles, t, func, into):
            nc.scalar.activation(into[:, t, :], tiles[t], func, bias=bias_sb[:, b, t : t + 1])

        def read_angles(s, b, tiles, kibs, sines_first=False):
            sines = place([P, PACK, WIDTH], F32, "sines%d%d" % (s, b), kibs[0])
            folded = place([P, PACK, WIDTH], F32, "folded%d%d" % (s, b), kibs[1])
            for t in range(PACK):
                steps = [(folded, ACT.Abs), (sines, ACT.Sin)]
                for tile, func in reversed(steps) if sines_first else steps:
                    read_function(b, tiles, t, func, tile)
            return sines, folded

        def vector_scale(dst, src, amp):
            nc.vector.tensor_tensor(
                dst.rearrange("p (c i) t -> p c t i", i=2),
                src.rearrange("p t (c i) -> p c t i", i=2),
                amp.unsqueeze(1).unsqueeze(3).to_broadcast([P, WIDTH // 2, PACK, 2]),
                ALU.mult,
            )

        def scale_sines(s, b, sines, kib):
            rounded = place([P, PACK, WIDTH], BF16, "rounded%d%d" % (s, b), kib)
            for t in range(PACK):
                nc.scalar.activation(rounded[:, t, :], sines[:, t, :], ACT.Copy, scale=amp_sin[:, b, t : t + 1])
            return rounded

        def woven_cosines(s, b, folded, kib):
            cosines = place([P, WIDTH, PACK], F32, "cosines%d%d" % (s, b), kib)
            nc.scalar.activation(
                cosines[:].rearrange("p (c i) t -> p c t i", i=2),
                folded[:].rearrange("p t (c i) -> p c t i", i=2),
                ACT.Sin, bias=math.pi / 2, scale=-1.0,
            )
            return cosines

        def weave(b, rounded, cosines, target, cut=WIDTH):
            if cut > 0:
                nc.gpsimd.tensor_scalar(
                    target[0][:, :cut, :], rounded[:, :, :cut].rearrange("p t c -> p c t"), 1.0, 1.0, ALU.mult, ALU.mult
                )
            if cut < WIDTH:
                nc.scalar.copy(
                    target[0][:, cut:, :].rearrange("p (c i) t -> p c t i", i=4),
                    rounded[:, :, cut:].rearrange("p t (c i) -> p c t i", i=4),
                )
            nc.gpsimd.tensor_tensor(
                target[1], cosines[:], amp_cos[:, b, :].unsqueeze(1).to_broadcast([P, WIDTH, PACK]), ALU.mult
            )

        h_q = {}

        def quantise_parts(parts, name, kib):
            step = parts[0].shape[1] // PACK
            codes = place([P, step * len(parts)], U32, name + "_codes", kib)
            scales = keep.tile([P, step * len(parts)], U8, name=name + "_scales", align_bytes=64)
            for k, values in enumerate(parts):
                cols = slice(step * k, step * (k + 1))
                nc.vector.quantize_mx(out=codes[:, cols].bitcast(FP8X4), scales=scales[:, cols], in_=values)
            return codes, scales

        def woven_slice(s):
            tiles = [place([P, 2, WIDTH, PACK], BF16, "h_woven%d%d" % (s, b), 68 + 4 * b) for b in range(PASSES)]
            return [(tile[:, 0, :, :], tile[:, 1, :, :], tile[:].rearrange("p h c t -> p (h c t)")) for tile in tiles]

        def quantise_slice(s, woven):
            codes, scales = quantise_parts([unit[2] for unit in woven], "h%d" % s, 36 + 4 * s)
            for b in range(PASSES):
                h_q[s, b] = (codes, scales, 2 * WIDTH * b)

        def product_pass(s, n, sums, step, order):
            b, half = order[step // 2], step % 2
            codes, scales, first = h_q[s, b]
            cols = slice(first + WIDTH * half, first + WIDTH * (half + 1))
            if half == 0:
                words, planes = w4_w[:, b, 2 * P * n : 2 * P * (n + 1)].bitcast(FP4X4), w4_sc[:, b, P * n : P * (n + 1)]
            else:
                words, planes = w5_q[b][0][:, P * n : P * (n + 1)].bitcast(FP8X4), w5_q[b][1][:, P * n : P * (n + 1)]
            nc.tensor.matmul_mx(
                out=sums, lhsT=words, lhsT_scale=planes, rhs=codes[:, cols].bitcast(FP8X4), rhs_scale=scales[:, cols],
                start=(step == 0), stop=(step == 2 * PASSES - 1),
            )

        def products(s, n, sums, order=(0, 1)):
            for step in range(2 * PASSES):
                product_pass(s, n, sums, step, order)
            return sums

        def pair_of_products(s, half, index):
            bank = psum_bank("y_bank%d%d" % (s, half), index)
            return [products(s, 2 * half + i, bank[:, i, :]) for i in range(2)]

        def retune_pair(s, half, sums, kibs):
            new = [place([P, WIDTH], F32, "new%d%d" % (s, 2 * half + i), kibs[i]) for i in range(2)]
            for i in range(2):
                nc.vector.tensor_tensor(new[i][:], sums[i], old[2 * half + i][:, entries(s)], ALU.add)
            for i in range(2):
                nc.vector.tensor_copy(phases[2 * half + i][:].indirect(places(s)), new[i][:])

        def scatter_sum(s, n, y_sb, count=1):
            nc.vector.tensor_tensor(phases[n][:].indirect(places(s, count)), old[n][:, entries(s, count)], y_sb, ALU.add)

        def gather_phases(tile, n):
            nc.vector.tensor_copy(tile[:], phases[n][:].indirect(offsets[:]))
            return tile

        EVEN, ODD = (84, 88), (130, 134)
        woven = place([P, 2, WIDTH, PACK], BF16, "h_woven00", 40)
        sines, folded = read_angles(0, 0, angle_products(0, 0, (4, 5, 6, 7)), (76, 80))
        turned = psum.tile([P, PACK, P], F32, name="turned", offset=4 * 2 * KIB)
        for t in range(PACK):
            nc.tensor.transpose(turned[:, t, :], rows[:, t:PASS:PACK], identity[:])
        nc.scalar.copy(channels[:].rearrange("p k b t -> p t (k b)"), turned[:, :, used])
        nc.scalar.activation(folded[:], folded[:], ACT.Sin, bias=math.pi / 2, scale=-1.0)
        vector_scale(woven[:, 0, :, :], sines[:], amp_sin[:, 0, :])
        vector_scale(woven[:, 1, :, :], folded[:], amp_cos[:, 0, :])
        read = {(1, 0): read_angles(1, 0, angle_products(1, 0, (0, 1)), EVEN)}
        w5_q = [quantise_w5(0, (64, 66))]
        h_q[0, 0] = quantise(woven[:].rearrange("p h c t -> p (h c t)"), 2 * WIDTH, "h00", 54) + (0,)
        w5_q.append(quantise_w5(1, (124, 72)))
        old = [gather_phases(place([P, S], F32, "old0", 124), 0), gather_phases(keep.tile([P, S], F32, name="old1"), 1)]
        woven = place([P, 2, WIDTH, PACK], BF16, "h_woven01", 70)
        sines, folded = read_angles(0, 1, angle_products(0, 1, (2, 3)), (96, 103))
        weave(1, scale_sines(0, 1, sines, 114), woven_cosines(0, 1, folded, 118), (woven[:, 0, :, :], woven[:, 1, :, :]))
        h_q[0, 1] = quantise(woven[:].rearrange("p h c t -> p (h c t)"), 2 * WIDTH, "h01") + (0,)
        old.append(gather_phases(place([P, S], F32, "old2", 116), 2))
        old.append(gather_phases(place([P, S], F32, "old3", 120), 3))
        read[1, 1] = read_angles(1, 1, angle_products(1, 1, (0, 1), (1, 0)), (93, 103), True)
        tiles = {(2, 0): angle_products(2, 0, (2, 3)), (3, 0): angle_products(3, 0, (0, 1))}
        woven = woven_slice(1)
        weave(0, scale_sines(1, 0, read[1, 0][0], 97), woven_cosines(1, 0, read[1, 0][1], 99), woven[0])
        weave(1, scale_sines(1, 1, read[1, 1][0], 24), woven_cosines(1, 1, read[1, 1][1], 0), woven[1])
        sums = [psum_bank("y_first%d" % i, 4 + 2 * i)[:, 0, :] for i in range(2)]
        for step in range(2 * PASSES):
            for i in range(2):
                product_pass(0, i, sums[i], step, (0, 1))
        held = pair_of_products(0, 1, 5)
        retune_pair(0, 0, sums, (40, 52))
        quantise_slice(1, woven)
        retune_pair(0, 1, held, (0, 1))
        woven = woven_slice(2)
        sines, folded = read_angles(2, 0, tiles[2, 0], EVEN)
        weave(0, scale_sines(2, 0, sines, 26), woven_cosines(2, 0, folded, 4), woven[0])
        sines, folded = read_angles(2, 1, angle_products(2, 1, (4, 6)), ODD)
        weave(1, scale_sines(2, 1, sines, 28), woven_cosines(2, 1, folded, 8), woven[1], WIDTH // 2)
        sums = pair_of_products(1, 0, 2)
        held = pair_of_products(1, 1, 3)
        retune_pair(1, 0, sums, (44, 53))
        tiles[3, 1] = angle_products(3, 1, (5, 2))
        quantise_slice(2, woven)
        retune_pair(1, 1, held, (8, 9))
        woven = woven_slice(3)
        sines, folded = read_angles(3, 0, tiles[3, 0], (132, 128))
        weave(0, scale_sines(3, 0, sines, 30), woven_cosines(3, 0, folded, 12), woven[0])
        sines, folded = read_angles(3, 1, tiles[3, 1], ODD)
        cosines = woven_cosines(3, 1, folded, 16)
        weave(1, scale_sines(3, 1, sines, 20), cosines, woven[1], 0)
        sums = pair_of_products(2, 0, 4)
        kept = pair_of_products(2, 1, 7)
        retune_pair(2, 0, sums, (48, 54))
        quantise_slice(3, woven)
        y_sb = place([P, WIDTH], F32, "y_sb22", 19.5)
        nc.scalar.copy(y_sb[:], kept[0])
        scatter_sum(2, 2, y_sb[:])
        for n in range(ROW_TILES - 1):
            y_sb = place([P, WIDTH], F32, "y_sb3%d" % n, 60 + n)
            nc.scalar.copy(y_sb[:], products(last, n, psum_bank("y_last%d" % n, (0, 1, 6)[n])[:, 0, :], (1, 0) if n else (0, 1)))
            scatter_sum(last, n, y_sb[:])
            nc.sync.dma_start(out[P * n : P * (n + 1), :], phases[n][:])
        n = ROW_TILES - 1
        y_sb = place([P, 2 * WIDTH], F32, "y_sb_last", 21)
        nc.scalar.copy(y_sb[:, :WIDTH], kept[1])
        nc.scalar.copy(y_sb[:, WIDTH:], products(last, n, psum_bank("y_last%d" % n, n)[:, 0, :], (1, 0)))
        scatter_sum(last - 1, n, y_sb[:], 2)
        nc.sync.dma_start(out[P * n : P * (n + 1), :], phases[n][:])
